import numpy as np
import ml_dtypes


def mxq(x, axis, fmt="e4m3"):
    dtype, down = {"e4m3": (ml_dtypes.float8_e4m3fn, 7), "e5m2": (ml_dtypes.float8_e5m2, 14)}[fmt]
    v = np.moveaxis(np.asarray(x, np.float32).astype(ml_dtypes.bfloat16).astype(np.float64), axis, -1)
    blocks = v.reshape(v.shape[:-1] + (-1, 32))
    amax = np.abs(blocks).max(-1, keepdims=True)
    byte = np.maximum(np.where(amax > 0, np.frexp(amax)[1] - 1 + 127, 0) - down, 1)
    scale = np.exp2(byte - 127.0)
    codes = (blocks / scale).astype(np.float32).astype(dtype).astype(np.float64)
    return np.moveaxis((codes * scale).reshape(v.shape), -1, axis)


WIDE = False


def mx_kscale(k):
    if not WIDE:
        return np.ones(k)
    levels = np.array([10, -10, 5, -5, 0])
    if k % 512:
        return np.exp2(np.random.permutation(np.resize(levels, k // 32))).repeat(32)
    a = np.empty((k // 512, 16))
    for p in range(k // 512):
        a[p, :8] = np.random.permutation(np.resize(levels, 8))
        for g in range(8):
            far = levels[np.abs(levels - a[p, g]) >= 10]
            a[p, g + 8] = far[np.random.randint(len(far))]
    return np.exp2(a.ravel()).repeat(32)


def f64(x):
    return np.asarray(x).astype(np.float64)


def striped(idx):
    return np.tile(idx.reshape(-1, 16).T, (8, 1)).astype(np.uint16)


def unstriped(offs):
    return offs[:16].T.reshape(-1).astype(np.int64)


E2M1 = np.array([0.0, 0.5, 1.0, 1.5, 2.0, 3.0, 4.0, 6.0, -0.0, -0.5, -1.0, -1.5, -2.0, -3.0, -4.0, -6.0])


def pack_weight(w, fmt):
    k, n = w.shape
    w = f64(np.asarray(w, np.float32).astype(ml_dtypes.bfloat16)).reshape(k // 32, 32, n)
    amax = np.abs(w).max(1)
    if fmt == "e4m3":
        byte = np.frexp(amax)[1] - 1 + 127 - 7
    else:
        mant, ex = np.frexp(amax / 6.0)
        byte = np.where(mant > 0.5, ex, ex - 1) + 127
    byte = np.clip(np.where(amax > 0, byte, 1), 1, 254)
    scaled = (w * np.exp2(127.0 - byte)[:, None, :]).reshape(k, n).astype(np.float32)
    by_word = np.ascontiguousarray(scaled.reshape(k // 512, 128, 4, n).transpose(0, 1, 3, 2))
    if fmt == "e4m3":
        words = by_word.astype(ml_dtypes.float8_e4m3fn).view(np.uint8)
    else:
        c = by_word.astype(ml_dtypes.float4_e2m1fn).view(np.uint8) & 0xF
        words = (c[..., 0::2] | (c[..., 1::2] << 4)).reshape(k // 512, 128, 2 * n)
    return np.ascontiguousarray(words), np.ascontiguousarray(byte.astype(np.uint8).reshape(k // 512, 16, n))


def unpack_weight(words, scales, fmt):
    g, _, n = scales.shape
    words = np.ascontiguousarray(words).reshape(g, 128, n, -1)
    if fmt == "e4m3":
        vals = words.view(ml_dtypes.float8_e4m3fn).astype(np.float64)
    else:
        nib = np.empty((g, 128, n, 4), np.uint8)
        nib[..., 0::2] = words & 0xF
        nib[..., 1::2] = words >> 4
        vals = E2M1[nib]
    vals = vals * np.repeat(np.exp2(scales.astype(np.float64) - 127.0), 8, axis=1)[..., None]
    return vals.transpose(0, 1, 3, 2).reshape(g * 512, n)


def silu(v):
    return v / (1.0 + np.exp(-np.maximum(v, -700.0)))


K, T, E, C, H, N = 1536, 512, 4, 256, 512, 128


def by_expert(wq, xq):
    return np.concatenate([wq[e].T @ xq[:, e * C:(e + 1) * C] for e in range(E)], axis=1)


def setup_inputs():
    n = np.random.standard_normal
    s = mx_kscale(K)
    u = mx_kscale(H)
    first = np.random.permutation(np.repeat(np.arange(E), T // E))
    second = (first + 1 + np.random.permutation(np.repeat(np.arange(E - 1), -(-T // (E - 1)))[:T])) % E
    while np.bincount(second, minlength=E).max() != T // E:
        load = np.bincount(second, minlength=E); hi, lo = int(load.argmax()), int(load.argmin())
        t = np.flatnonzero((second == hi) & (first != lo))[0]; second[t] = lo
    slot_token = np.empty(E * C, np.int64); pos = np.empty((2, T), np.int64); fill = np.zeros(E, np.int64)
    place = np.stack([np.random.permutation(C) for _ in range(E)])
    for r, deal in enumerate((first, second)):
        for t in np.random.permutation(T):
            e = deal[t]; j = e * C + place[e, fill[e]]; fill[e] += 1; slot_token[j] = t; pos[r, t] = j
    g = np.random.uniform(0.2, 0.8, T)
    x = pack_weight(n((K, T)) * s[:, None], "e4m3")
    w1 = [pack_weight(m, "e2m1") for m in n((E, K, H)) / np.sqrt(K) / s[None, :, None] * u]
    w2 = pack_weight(n((H, N)) / np.sqrt(H) / u[:, None], "e2m1")
    return {
        "x_words": x[0],
        "x_scales": x[1],
        "w1_words": np.stack([m[0] for m in w1]),
        "w1_scales": np.stack([m[1] for m in w1]),
        "w2_words": w2[0],
        "w2_scales": w2[1],
        "gate": np.stack([np.tile(g, (128, 1)), np.tile(1.0 - g, (128, 1))]).astype(np.float32),
        "offs": striped(slot_token),
        "pos1": striped(pos[0]),
        "pos2": striped(pos[1]),
    }


def reference(x_words, x_scales, w1_words, w1_scales, w2_words, w2_scales, gate, offs, pos1, pos2):
    w1 = np.stack([unpack_weight(w1_words[e], w1_scales[e], "e2m1") for e in range(E)])
    w2 = unpack_weight(w2_words, w2_scales, "e2m1")
    idx = unstriped(offs)
    xq = unpack_weight(x_words, x_scales, "e4m3")[:, idx]
    h = silu(by_expert(w1, xq))
    c = sum(f64(gate[r, :1]) * h[:, unstriped(p)] for r, p in enumerate((pos1, pos2)))
    return w2.T @ mxq(c, 0, "e4m3")

@@ -1,0 +1,230 @@
+from contextlib import ExitStack
+
+import concourse.mybir as mybir
+from concourse.masks import make_identity
+
+K, T, E, C, H, N = 1536, 512, 4, 256, 512, 128
+FLOPS = 2 * K * H * E * C + 2 * H * N * T
+
+F32 = mybir.dt.float32
+BF16 = mybir.dt.bfloat16
+I32 = mybir.dt.int32
+U32 = mybir.dt.uint32
+U16 = mybir.dt.uint16
+U8 = mybir.dt.uint8
+FP8X4 = mybir.dt.float8_e4m3fn_x4
+FP4X4 = mybir.dt.float4_e2m1fn_x4
+MULT = mybir.AluOpType.mult
+SILU = mybir.ActivationFunctionType.Silu
+
+P = 128
+PASSES = K // 512
+SLOTS = E * C
+H_TILES = H // P
+CHUNKS = ((0, 384), (384, 128))
+
+
+def tile_moe_sdn_lin_silu_kernel(
+    tc, x_words, x_scales, w1_words, w1_scales, w2_words, w2_scales, gate, offs, pos1, pos2, out
+):
+    nc = tc.nc
+    with ExitStack() as ctx:
+        lists = ctx.enter_context(tc.tile_pool(name="lists", bufs=1))
+        keep = ctx.enter_context(tc.tile_pool(name="keep", bufs=1))
+        ring = ctx.enter_context(tc.tile_pool(name="ring", bufs=6))
+        psum = ctx.enter_context(tc.psum_pool(name="psum", bufs=4))
+
+        offs_sb = lists.tile([P, SLOTS // 16], U16, name="offs_sb")
+        pos_sb = [lists.tile([P, T // 16], U16, name=f"pos_sb{r}") for r in range(2)]
+
+        xs_win = keep.tile([P, T], U8, name="xs_win", tag="xs_then_gate", align_bytes=64)
+        w1s = keep.tile([P, E * PASSES, H], U8, name="w1s", align_bytes=64)
+        planes = keep.tile([P, 2, SLOTS], U8, name="planes", align_bytes=64)
+        zero = keep.tile([P, 8], F32, name="zero")
+        nc.gpsimd.memset(xs_win[:].bitcast(I32), 0)
+        nc.gpsimd.memset(zero[:], 0.0)
+        nc.vector.memset(w1s[:].rearrange("p a n -> p (a n)").bitcast(I32), 0)
+        nc.gpsimd.memset(planes[:].rearrange("p a n -> p (a n)").bitcast(I32), 0)
+        ident = keep.tile([P, P], F32, name="ident")
+        make_identity(nc, ident[:])
+
+        xw = [keep.tile([P, T], I32, name=f"xw{s}", align_bytes=64) for s in range(PASSES)]
+        h = [keep.tile([P, SLOTS], F32, name=f"h{t}") for t in range(H_TILES)]
+
+        def load_x_words(queue, s):
+            queue.dma_start(xw[s][:], x_words[s].rearrange("p t d -> p (t d)").bitcast(I32))
+
+        xs_pairs = x_scales[0:2].rearrange("s (q r) t -> r q s t", r=4)
+
+        def load_x_scale_pair(queue, r):
+            queue.dma_start(xs_win[r:P:16, :].bitcast(I32), xs_pairs[r].bitcast(I32))
+
+        w2w = keep.tile([P, 2 * N], U8, name="w2w", align_bytes=64)
+        nc.sync.dma_start(offs_sb[:], offs)
+        nc.scalar.dma_start(w2w[:].bitcast(I32), w2_words[0].bitcast(I32))
+        load_x_scale_pair(nc.scalar, 0)
+        load_x_scale_pair(nc.sync, 1)
+        load_x_scale_pair(nc.scalar, 2)
+        load_x_scale_pair(nc.sync, 3)
+        nc.scalar.dma_start(xs_win[4:P:8, :].bitcast(I32), x_scales[2].bitcast(I32))
+        load_x_words(nc.sync, 0)
+        nc.scalar.activation(h[0][:, 0:1], zero[:, 0:1], SILU)
+        load_x_words(nc.sync, 1)
+        load_x_words(nc.sync, 2)
+        w1w = [keep.tile([P, PASSES, 2 * H], U8, name=f"w1w{e}", align_bytes=64) for e in range(E)]
+
+        def load_w1_words(queue, e):
+            queue.dma_start(w1w[e][:].bitcast(I32), w1_words[e].rearrange("s p b -> p s b").bitcast(I32))
+
+        load_w1_words(nc.sync, 0)
+        nc.sync.dma_start(pos_sb[0][:], pos1)
+        nc.sync.dma_start(pos_sb[1][:], pos2)
+
+        w1s_rows = w1_scales.rearrange("e s b n -> b (e s) n")
+        for q in range(4):
+            nc.scalar.dma_start(
+                w1s[32 * q : 32 * q + 4, :, :].bitcast(I32), w1s_rows[4 * q : 4 * q + 4].bitcast(I32)
+            )
+
+        gs = keep.tile([P, SLOTS], U8, name="gs", align_bytes=64)
+        gw = [
+            [
+                keep.tile([P, C], U32, name=f"gw{e}_{s}", tag=f"gw{e}_{s}", align_bytes=64)
+                for s in range(PASSES)
+            ]
+            for e in range(E)
+        ]
+
+        def expert_offsets(e):
+            return offs_sb[:, e * C // 16 : (e + 1) * C // 16]
+
+        for e in range(E):
+            nc.vector.tensor_copy(gs[:, e * C : (e + 1) * C], xs_win[:].indirect(expert_offsets(e)))
+        nc.scalar.dma_start(planes[0:112, 0, :].bitcast(I32), gs[16:P, :].bitcast(I32))
+        for r in range(4):
+            nc.scalar.dma_start(
+                planes[r:P:32, 1, :].bitcast(I32), gs[8 * r + 4 : P : 32, :].bitcast(I32)
+            )
+        for e in range(1, E):
+            load_w1_words(nc.scalar, e)
+        gate_sb = keep.tile([P, 2, T], F32, name="gate_sb", tag="xs_then_gate", align_bytes=64)
+        nc.scalar.dma_start(gate_sb[:], gate.rearrange("r p t -> p r t"))
+        for e in range(E):
+            for s in range(PASSES):
+                nc.vector.tensor_copy(gw[e][s][:], xw[s][:].bitcast(U32).indirect(expert_offsets(e)))
+
+        def first_pass(acc, e, t, half, s):
+            cols = slice(e * C + half * P, e * C + (half + 1) * P)
+            nc.tensor.matmul_mx(
+                out=acc,
+                lhsT=w1w[e][:, s, 2 * P * t : 2 * P * (t + 1)].bitcast(FP4X4),
+                lhsT_scale=w1s[:, e * PASSES + s, P * t : P * (t + 1)],
+                rhs=gw[e][s][:, half * P : (half + 1) * P].bitcast(FP8X4),
+                rhs_scale=gs[:, cols] if s == 0 else planes[:, s - 1, cols],
+                start=(s == 0),
+                stop=(s == PASSES - 1),
+            )
+
+        def hidden_in_own_banks(e, groups, tags):
+            accs = [psum.tile([P, P], F32, name="acc", tag=tag) for tag in tags]
+            for s in range(PASSES):
+                for acc, (t, half) in zip(accs, groups):
+                    first_pass(acc[:], e, t, half, s)
+            for acc, (t, half) in zip(accs, groups):
+                col = e * C + half * P
+                nc.scalar.activation(h[t][:, col : col + P], acc[:], SILU)
+
+        def hidden_in_one_bank(e, t):
+            acc = psum.tile([P, C], F32, name="acc", tag="work")
+            for half in range(2):
+                for s in range(PASSES):
+                    first_pass(acc[:, half * P : (half + 1) * P], e, t, half, s)
+            nc.scalar.activation(h[t][:, e * C : (e + 1) * C], acc[:], SILU)
+
+        hidden_in_own_banks(
+            0, [(t, half) for t in range(H_TILES) for half in range(2)], ["work"] * 4 + ["sums"] * 4
+        )
+        for e in (1, 2):
+            for t in range(3):
+                hidden_in_one_bank(e, t)
+        hidden_in_own_banks(3, [(0, 0), (0, 1)], ["sums"] * 2)
+        for t in (1, 2):
+            hidden_in_one_bank(3, t)
+        for e in (1, 2, 3):
+            hidden_in_one_bank(e, 3)
+
+        w2s = keep.tile([P, N], U8, name="w2s", tag="gw0_0", align_bytes=64)
+        nc.gpsimd.memset(w2s[:].bitcast(I32), 0)
+        for q in range(4):
+            nc.sync.dma_start(
+                w2s[32 * q : 32 * q + 4, :].bitcast(I32), w2_scales[0, 4 * q : 4 * q + 4, :].bitcast(I32)
+            )
+
+        grouped = []
+        for tok0, ntok in CHUNKS:
+            tiles = ntok // P
+            sums = [psum.tile([P, H], F32, name="sums", tag="sums") for j in range(tiles)]
+            c_tok = [keep.tile([P, 2, P, 2], BF16, name=f"c_tok{tok0 + j * P}") for j in range(tiles)]
+            for t in range(H_TILES):
+                prods = []
+                for r in range(2):
+                    prod = ring.tile([P, ntok], F32, name="prod", tag="prod")
+                    nc.vector.tensor_tensor(
+                        prod[:],
+                        h[t][:].indirect(pos_sb[r][:, tok0 // 16 : (tok0 + ntok) // 16]),
+                        gate_sb[:, r, tok0 : tok0 + ntok],
+                        MULT,
+                    )
+                    prods.append(prod)
+                for j in range(tiles):
+                    for r in range(2):
+                        nc.tensor.matmul(
+                            sums[j][:, t * P : (t + 1) * P],
+                            prods[r][:, j * P : (j + 1) * P],
+                            ident[:],
+                            start=(r == 0),
+                            stop=(r == 1),
+                            is_transpose=True,
+                        )
+                if t >= H_TILES - 2:
+                    p0 = 0 if t == H_TILES - 2 else 32 * t
+                    p1 = 32 * (t + 1)
+                    for j in range(tiles):
+                        nc.scalar.copy(
+                            c_tok[j][:, :, p0:p1, :],
+                            sums[j][:].rearrange("k (p u e) -> k u p e", u=2, e=2)[:, :, p0:p1, :],
+                        )
+            group = keep.tile([P, ntok, 2], F32, name=f"group{tok0}", align_bytes=64)
+            for j in range(tiles):
+                words = c_tok[j][:].rearrange("k u p e -> k (u p e)").bitcast(F32)
+                turned = psum.tile([P, 2, P], F32, name="turned", tag="work")
+                for u in range(2):
+                    nc.tensor.transpose(turned[:, u, :], words[:, u * P : (u + 1) * P], ident[:])
+                nc.scalar.copy(group[:, j * P : (j + 1) * P, :], turned[:].rearrange("p u k -> p k u"))
+            grouped.append(group)
+
+        for (tok0, ntok), group in zip(CHUNKS, grouped):
+            values = group[:].rearrange("p k u -> p (k u)").bitcast(BF16)
+            codes = keep.tile([P, ntok], U32, name=f"codes{tok0}", align_bytes=64)
+            scales = keep.tile([P, ntok], U8, name=f"scales{tok0}", align_bytes=64)
+            result = keep.tile([P, ntok], F32, name=f"result{tok0}")
+            res = psum.tile([P, ntok], F32, name="res", tag="work")
+            pieces = [(a, min(256, ntok - a)) for a in range(0, ntok, 256)]
+            for a, n in pieces:
+                nc.vector.quantize_mx(
+                    out=codes[:, a : a + n].bitcast(FP8X4),
+                    scales=scales[:, a : a + n],
+                    in_=values[:, 4 * a : 4 * (a + n)],
+                )
+            for a, n in pieces:
+                nc.tensor.matmul_mx(
+                    out=res[:, a : a + n],
+                    lhsT=w2w[:].bitcast(FP4X4),
+                    lhsT_scale=w2s[:],
+                    rhs=codes[:, a : a + n].bitcast(FP8X4),
+                    rhs_scale=scales[:, a : a + n],
+                    start=True,
+                    stop=True,
+                )
+            nc.vector.tensor_copy(result[:], res[:])
+            nc.sync.dma_start(out[:, tok0 : tok0 + ntok], result[:])

@@ -31,13 +31,14 @@ def tile_moe_sdn_lin_silu_kernel(
     with ExitStack() as ctx:
         lists = ctx.enter_context(tc.tile_pool(name="lists", bufs=1))
         keep = ctx.enter_context(tc.tile_pool(name="keep", bufs=1))
-        ring = ctx.enter_context(tc.tile_pool(name="ring", bufs=6))
-        psum = ctx.enter_context(tc.psum_pool(name="psum", bufs=4))
+        ring = ctx.enter_context(tc.tile_pool(name="ring", bufs=8))
+        late = ctx.enter_context(tc.tile_pool(name="late", bufs=1))
+        psum = ctx.enter_context(tc.psum_pool(name="psum", bufs=1))
 
         offs_sb = lists.tile([P, SLOTS // 16], U16, name="offs_sb")
         pos_sb = [lists.tile([P, T // 16], U16, name=f"pos_sb{r}") for r in range(2)]
 
-        xs_win = keep.tile([P, T], U8, name="xs_win", tag="xs_then_gate", align_bytes=64)
+        xs_win = late.tile([P, T], U8, name="xs_win", align_bytes=64, offset=4096)
         w1s = keep.tile([P, E * PASSES, H], U8, name="w1s", align_bytes=64)
         planes = keep.tile([P, 2, SLOTS], U8, name="planes", align_bytes=64)
         zero = keep.tile([P, 8], F32, name="zero")
@@ -48,36 +49,29 @@ def tile_moe_sdn_lin_silu_kernel(
         ident = keep.tile([P, P], F32, name="ident")
         make_identity(nc, ident[:])
 
-        xw = [keep.tile([P, T], I32, name=f"xw{s}", align_bytes=64) for s in range(PASSES)]
+        xw = keep.tile([P, PASSES, T], I32, name="xw", align_bytes=64)
         h = [keep.tile([P, SLOTS], F32, name=f"h{t}") for t in range(H_TILES)]
 
-        def load_x_words(queue, s):
-            queue.dma_start(xw[s][:], x_words[s].rearrange("p t d -> p (t d)").bitcast(I32))
+        def load_x_scale_pair(queue, q):
+            queue.dma_start(
+                xs_win[32 * q : 32 * q + 8, :].bitcast(I32),
+                x_scales[0:2, 4 * q : 4 * q + 4, :].bitcast(I32),
+            )
 
-        xs_pairs = x_scales[0:2].rearrange("s (q r) t -> r q s t", r=4)
-
-        def load_x_scale_pair(queue, r):
-            queue.dma_start(xs_win[r:P:16, :].bitcast(I32), xs_pairs[r].bitcast(I32))
-
-        w2w = keep.tile([P, 2 * N], U8, name="w2w", align_bytes=64)
         nc.sync.dma_start(offs_sb[:], offs)
-        nc.scalar.dma_start(w2w[:].bitcast(I32), w2_words[0].bitcast(I32))
         load_x_scale_pair(nc.scalar, 0)
         load_x_scale_pair(nc.sync, 1)
         load_x_scale_pair(nc.scalar, 2)
         load_x_scale_pair(nc.sync, 3)
-        nc.scalar.dma_start(xs_win[4:P:8, :].bitcast(I32), x_scales[2].bitcast(I32))
-        load_x_words(nc.sync, 0)
+        nc.scalar.dma_start(xs_win[8:24, :].bitcast(I32), x_scales[2].bitcast(I32))
         nc.scalar.activation(h[0][:, 0:1], zero[:, 0:1], SILU)
-        load_x_words(nc.sync, 1)
-        load_x_words(nc.sync, 2)
-        w1w = [keep.tile([P, PASSES, 2 * H], U8, name=f"w1w{e}", align_bytes=64) for e in range(E)]
-
-        def load_w1_words(queue, e):
-            queue.dma_start(w1w[e][:].bitcast(I32), w1_words[e].rearrange("s p b -> p s b").bitcast(I32))
-
-        load_w1_words(nc.sync, 0)
         nc.sync.dma_start(pos_sb[0][:], pos1)
+        x_rows = x_words.rearrange("s p t d -> p s (t d)").bitcast(I32)
+        nc.sync.dma_start(xw[:, 0:1, :], x_rows[:, 0:1, :])
+        nc.sync.dma_start(xw[:, 1:PASSES, :], x_rows[:, 1:PASSES, :])
+        w1_rows = w1_words.rearrange("e s p (g b) -> g p (e s) b", g=2).bitcast(I32)
+        w1w_early = keep.tile([P, 2 * PASSES, H], U8, name="w1w_early", align_bytes=64)
+        nc.sync.dma_start(w1w_early[:].bitcast(I32), w1_rows[0][:, 0 : 2 * PASSES, :])
         nc.sync.dma_start(pos_sb[1][:], pos2)
 
         w1s_rows = w1_scales.rearrange("e s b n -> b (e s) n")
@@ -100,24 +94,36 @@ def tile_moe_sdn_lin_silu_kernel(
 
         for e in range(E):
             nc.vector.tensor_copy(gs[:, e * C : (e + 1) * C], xs_win[:].indirect(expert_offsets(e)))
-        nc.scalar.dma_start(planes[0:112, 0, :].bitcast(I32), gs[16:P, :].bitcast(I32))
-        for r in range(4):
+        nc.sync.dma_start(planes[0:112, 0, :].bitcast(I32), gs[4:116, :].bitcast(I32))
+        for q in range(4):
             nc.scalar.dma_start(
-                planes[r:P:32, 1, :].bitcast(I32), gs[8 * r + 4 : P : 32, :].bitcast(I32)
+                planes[32 * q : 32 * q + 4, 1, :].bitcast(I32),
+                gs[8 + 4 * q : 12 + 4 * q, :].bitcast(I32),
             )
-        for e in range(1, E):
-            load_w1_words(nc.scalar, e)
-        gate_sb = keep.tile([P, 2, T], F32, name="gate_sb", tag="xs_then_gate", align_bytes=64)
+        w1w_late = late.tile([P, 6 * PASSES, H], U8, name="w1w_late", align_bytes=64, offset=4352)
+        nc.scalar.dma_start(
+            w1w_late[:, 0 : 2 * PASSES, :].bitcast(I32), w1_rows[0][:, 2 * PASSES :, :]
+        )
+        gate_sb = late.tile([P, 2, T], F32, name="gate_sb", align_bytes=64, offset=256)
         nc.scalar.dma_start(gate_sb[:], gate.rearrange("r p t -> p r t"))
+        nc.scalar.dma_start(w1w_late[:, 2 * PASSES :, :].bitcast(I32), w1_rows[1])
         for e in range(E):
             for s in range(PASSES):
-                nc.vector.tensor_copy(gw[e][s][:], xw[s][:].bitcast(U32).indirect(expert_offsets(e)))
+                nc.vector.tensor_copy(gw[e][s][:], xw[:, s, :].bitcast(U32).indirect(expert_offsets(e)))
+
+        def w1_codes(e, t, s):
+            cols = slice(2 * P * (t % 2), 2 * P * (t % 2 + 1))
+            if t >= 2:
+                return w1w_late[:, (2 + e) * PASSES + s, cols]
+            if e >= 2:
+                return w1w_late[:, (e - 2) * PASSES + s, cols]
+            return w1w_early[:, e * PASSES + s, cols]
 
         def first_pass(acc, e, t, half, s):
             cols = slice(e * C + half * P, e * C + (half + 1) * P)
             nc.tensor.matmul_mx(
                 out=acc,
-                lhsT=w1w[e][:, s, 2 * P * t : 2 * P * (t + 1)].bitcast(FP4X4),
+                lhsT=w1_codes(e, t, s).bitcast(FP4X4),
                 lhsT_scale=w1s[:, e * PASSES + s, P * t : P * (t + 1)],
                 rhs=gw[e][s][:, half * P : (half + 1) * P].bitcast(FP8X4),
                 rhs_scale=gs[:, cols] if s == 0 else planes[:, s - 1, cols],
@@ -125,8 +131,8 @@ def tile_moe_sdn_lin_silu_kernel(
                 stop=(s == PASSES - 1),
             )
 
-        def hidden_in_own_banks(e, groups, tags):
-            accs = [psum.tile([P, P], F32, name="acc", tag=tag) for tag in tags]
+        def hidden_in_own_banks(e, groups):
+            accs = [psum.tile([P, P], F32, name="acc", tag=f"bank{b}") for b in range(len(groups))]
             for s in range(PASSES):
                 for acc, (t, half) in zip(accs, groups):
                     first_pass(acc[:], e, t, half, s)
@@ -134,25 +140,25 @@ def tile_moe_sdn_lin_silu_kernel(
                 col = e * C + half * P
                 nc.scalar.activation(h[t][:, col : col + P], acc[:], SILU)
 
-        def hidden_in_one_bank(e, t):
-            acc = psum.tile([P, C], F32, name="acc", tag="work")
+        def hidden_in_one_bank(e, t, bank):
+            acc = psum.tile([P, C], F32, name="acc", tag=f"bank{bank}")
             for half in range(2):
                 for s in range(PASSES):
                     first_pass(acc[:, half * P : (half + 1) * P], e, t, half, s)
             nc.scalar.activation(h[t][:, e * C : (e + 1) * C], acc[:], SILU)
 
-        hidden_in_own_banks(
-            0, [(t, half) for t in range(H_TILES) for half in range(2)], ["work"] * 4 + ["sums"] * 4
-        )
+        hidden_in_own_banks(0, [(t, half) for t in range(2) for half in range(2)])
         for e in (1, 2):
-            for t in range(3):
-                hidden_in_one_bank(e, t)
-        hidden_in_own_banks(3, [(0, 0), (0, 1)], ["sums"] * 2)
-        for t in (1, 2):
-            hidden_in_one_bank(3, t)
-        for e in (1, 2, 3):
-            hidden_in_one_bank(e, 3)
+            for t in range(2):
+                hidden_in_one_bank(e, t, 2 + 2 * e + t)
+        hidden_in_own_banks(3, [(0, 0), (0, 1)])
+        hidden_in_one_bank(3, 1, 2)
+        for t in (2, 3):
+            for e in range(E):
+                hidden_in_one_bank(e, t, (3 + (t - 2) * E + e) % 8)
 
+        w2w = keep.tile([P, 2 * N], U8, name="w2w", tag="gw0_1", align_bytes=64)
+        nc.sync.dma_start(w2w[:].bitcast(I32), w2_words[0].bitcast(I32))
         w2s = keep.tile([P, N], U8, name="w2s", tag="gw0_0", align_bytes=64)
         nc.gpsimd.memset(w2s[:].bitcast(I32), 0)
         for q in range(4):
@@ -163,12 +169,12 @@ def tile_moe_sdn_lin_silu_kernel(
         grouped = []
         for tok0, ntok in CHUNKS:
             tiles = ntok // P
-            sums = [psum.tile([P, H], F32, name="sums", tag="sums") for j in range(tiles)]
+            sums = [psum.tile([P, H], F32, name="sums", tag=f"bank{3 - tiles + j}") for j in range(tiles)]
             c_tok = [keep.tile([P, 2, P, 2], BF16, name=f"c_tok{tok0 + j * P}") for j in range(tiles)]
             for t in range(H_TILES):
                 prods = []
                 for r in range(2):
-                    prod = ring.tile([P, ntok], F32, name="prod", tag="prod")
+                    prod = ring.tile([P, ntok], F32, name="prod", tag=f"prod{tok0}")
                     nc.vector.tensor_tensor(
                         prod[:],
                         h[t][:].indirect(pos_sb[r][:, tok0 // 16 : (tok0 + ntok) // 16]),
@@ -197,7 +203,7 @@ def tile_moe_sdn_lin_silu_kernel(
             group = keep.tile([P, ntok, 2], F32, name=f"group{tok0}", align_bytes=64)
             for j in range(tiles):
                 words = c_tok[j][:].rearrange("k u p e -> k (u p e)").bitcast(F32)
-                turned = psum.tile([P, 2, P], F32, name="turned", tag="work")
+                turned = psum.tile([P, 2, P], F32, name="turned", tag=f"bank{3 + tok0 // P + j}")
                 for u in range(2):
                     nc.tensor.transpose(turned[:, u, :], words[:, u * P : (u + 1) * P], ident[:])
                 nc.scalar.copy(group[:, j * P : (j + 1) * P, :], turned[:].rearrange("p u k -> p k u"))
@@ -208,7 +214,7 @@ def tile_moe_sdn_lin_silu_kernel(
             codes = keep.tile([P, ntok], U32, name=f"codes{tok0}", align_bytes=64)
             scales = keep.tile([P, ntok], U8, name=f"scales{tok0}", align_bytes=64)
             result = keep.tile([P, ntok], F32, name=f"result{tok0}")
-            res = psum.tile([P, ntok], F32, name="res", tag="work")
+            res = psum.tile([P, ntok], F32, name="res", tag="bank7" if tok0 == 0 else "bank0")
             pieces = [(a, min(256, ntok - a)) for a in range(0, ntok, 256)]
             for a, n in pieces:
                 nc.vector.quantize_mx(

@@ -15,6 +15,7 @@ U8 = mybir.dt.uint8
 FP8X4 = mybir.dt.float8_e4m3fn_x4
 FP4X4 = mybir.dt.float4_e2m1fn_x4
 MULT = mybir.AluOpType.mult
+ADD = mybir.AluOpType.add
 SILU = mybir.ActivationFunctionType.Silu
 
 P = 128
@@ -31,7 +32,7 @@ def tile_moe_sdn_lin_silu_kernel(
     with ExitStack() as ctx:
         lists = ctx.enter_context(tc.tile_pool(name="lists", bufs=1))
         keep = ctx.enter_context(tc.tile_pool(name="keep", bufs=1))
-        ring = ctx.enter_context(tc.tile_pool(name="ring", bufs=8))
+        ring = ctx.enter_context(tc.tile_pool(name="ring", bufs=1))
         late = ctx.enter_context(tc.tile_pool(name="late", bufs=1))
         psum = ctx.enter_context(tc.psum_pool(name="psum", bufs=1))
 
@@ -48,6 +49,8 @@ def tile_moe_sdn_lin_silu_kernel(
         nc.gpsimd.memset(planes[:].rearrange("p a n -> p (a n)").bitcast(I32), 0)
         ident = keep.tile([P, P], F32, name="ident")
         make_identity(nc, ident[:])
+        ident_bf = keep.tile([P, P], BF16, name="ident_bf")
+        make_identity(nc, ident_bf[:])
 
         xw = keep.tile([P, PASSES, T], I32, name="xw", align_bytes=64)
         h = [keep.tile([P, SLOTS], F32, name=f"h{t}") for t in range(H_TILES)]
@@ -109,7 +112,13 @@ def tile_moe_sdn_lin_silu_kernel(
         nc.scalar.dma_start(w1w_late[:, 2 * PASSES :, :].bitcast(I32), w1_rows[1])
         for e in range(E):
             for s in range(PASSES):
-                nc.vector.tensor_copy(gw[e][s][:], xw[:, s, :].bitcast(U32).indirect(expert_offsets(e)))
+                width = P if (e, s) == (E - 1, PASSES - 1) else C
+                for a in range(0, C, width):
+                    first = (e * C + a) // 16
+                    nc.vector.tensor_copy(
+                        gw[e][s][:, a : a + width],
+                        xw[:, s, :].bitcast(U32).indirect(offs_sb[:, first : first + width // 16]),
+                    )
 
         def w1_codes(e, t, s):
             cols = slice(2 * P * (t % 2), 2 * P * (t % 2 + 1))
@@ -166,55 +175,68 @@ def tile_moe_sdn_lin_silu_kernel(
                 w2s[32 * q : 32 * q + 4, :].bitcast(I32), w2_scales[0, 4 * q : 4 * q + 4, :].bitcast(I32)
             )
 
-        grouped = []
-        for tok0, ntok in CHUNKS:
-            tiles = ntok // P
-            sums = [psum.tile([P, H], F32, name="sums", tag=f"bank{3 - tiles + j}") for j in range(tiles)]
-            c_tok = [keep.tile([P, 2, P, 2], BF16, name=f"c_tok{tok0 + j * P}") for j in range(tiles)]
-            for t in range(H_TILES):
-                prods = []
-                for r in range(2):
-                    prod = ring.tile([P, ntok], F32, name="prod", tag=f"prod{tok0}")
-                    nc.vector.tensor_tensor(
-                        prod[:],
-                        h[t][:].indirect(pos_sb[r][:, tok0 // 16 : (tok0 + ntok) // 16]),
-                        gate_sb[:, r, tok0 : tok0 + ntok],
-                        MULT,
+        grouped = [
+            keep.tile([P, ntok, 2], F32, name=f"group{tok0}", align_bytes=64) for tok0, ntok in CHUNKS
+        ]
+        prods, rows_by_token, c_tok = {}, {}, {}
+
+        def gather_product(tok0, ntok, t, r):
+            prods[tok0, t, r] = ring.tile([P, ntok], F32, name=f"prod{tok0}_{t}_{r}")
+            nc.vector.tensor_tensor(
+                prods[tok0, t, r][:],
+                h[t][:].indirect(pos_sb[r][:, tok0 // 16 : (tok0 + ntok) // 16]),
+                gate_sb[:, r, tok0 : tok0 + ntok],
+                MULT,
+            )
+
+        def combine(tok0, ntok, t):
+            tiles = range(tok0 // P, (tok0 + ntok) // P)
+            c_rows = keep.tile([P, ntok], BF16, name=f"c_rows{tok0}_{t}")
+            nc.vector.tensor_tensor(c_rows[:], prods[tok0, t, 0][:], prods[tok0, t, 1][:], ADD)
+            for g in tiles:
+                if t == 0:
+                    rows_by_token[g] = psum.tile([P, H], BF16, name="by_token", tag=f"bank{g}")
+                    c_tok[g] = keep.tile([P, 2, P], F32, name=f"c_tok{g}")
+                nc.tensor.transpose(
+                    rows_by_token[g][:, t * P : (t + 1) * P],
+                    c_rows[:, g * P - tok0 : (g + 1) * P - tok0],
+                    ident_bf[:],
+                )
+            if t % 2 == 1:
+                rows = slice(32 * (t - 1), 32 * (t + 1))
+                for g in tiles:
+                    nc.scalar.copy(
+                        c_tok[g][:, :, rows],
+                        rows_by_token[g][:].bitcast(F32).rearrange("k (p u) -> k u p", u=2)[:, :, rows],
                     )
-                    prods.append(prod)
-                for j in range(tiles):
-                    for r in range(2):
-                        nc.tensor.matmul(
-                            sums[j][:, t * P : (t + 1) * P],
-                            prods[r][:, j * P : (j + 1) * P],
-                            ident[:],
-                            start=(r == 0),
-                            stop=(r == 1),
-                            is_transpose=True,
-                        )
-                if t >= H_TILES - 2:
-                    p0 = 0 if t == H_TILES - 2 else 32 * t
-                    p1 = 32 * (t + 1)
-                    for j in range(tiles):
-                        nc.scalar.copy(
-                            c_tok[j][:, :, p0:p1, :],
-                            sums[j][:].rearrange("k (p u e) -> k u p e", u=2, e=2)[:, :, p0:p1, :],
-                        )
-            group = keep.tile([P, ntok, 2], F32, name=f"group{tok0}", align_bytes=64)
-            for j in range(tiles):
-                words = c_tok[j][:].rearrange("k u p e -> k (u p e)").bitcast(F32)
-                turned = psum.tile([P, 2, P], F32, name="turned", tag=f"bank{3 + tok0 // P + j}")
-                for u in range(2):
-                    nc.tensor.transpose(turned[:, u, :], words[:, u * P : (u + 1) * P], ident[:])
-                nc.scalar.copy(group[:, j * P : (j + 1) * P, :], turned[:].rearrange("p u k -> p k u"))
-            grouped.append(group)
+            if t == H_TILES - 1:
+                for g in tiles:
+                    turned = psum.tile([P, 2, P], F32, name="turned", tag=f"bank{4 + g}")
+                    for u in range(2):
+                        nc.tensor.transpose(turned[:, u, :], c_tok[g][:, u, :], ident[:])
+                    j = g % 3
+                    nc.scalar.copy(
+                        grouped[g // 3][:, j * P : (j + 1) * P, :], turned[:].rearrange("p u k -> p k u")
+                    )
+
+        steps = [
+            (tok0, ntok, t)
+            for tok0, ntok, ts in ((0, 256, (0, 1, 2)), (256, 128, (0, 1)), (0, 256, (3,)), (256, 128, (2, 3)), (384, 128, (0, 1, 2, 3)))
+            for t in ts
+        ]
+        for n, step in enumerate(steps):
+            gather_product(*step, 0)
+            if n > 0:
+                combine(*steps[n - 1])
+            gather_product(*step, 1)
+        combine(*steps[-1])
 
         for (tok0, ntok), group in zip(CHUNKS, grouped):
             values = group[:].rearrange("p k u -> p (k u)").bitcast(BF16)
             codes = keep.tile([P, ntok], U32, name=f"codes{tok0}", align_bytes=64)
             scales = keep.tile([P, ntok], U8, name=f"scales{tok0}", align_bytes=64)
             result = keep.tile([P, ntok], F32, name=f"result{tok0}")
-            res = psum.tile([P, ntok], F32, name="res", tag="bank7" if tok0 == 0 else "bank0")
+            res = psum.tile([P, ntok], F32, name="res", tag="bank0" if tok0 == 0 else "bank1")
             pieces = [(a, min(256, ntok - a)) for a in range(0, ntok, 256)]
             for a, n in pieces:
                 nc.vector.quantize_mx(

@@ -178,42 +178,71 @@ def tile_moe_sdn_lin_silu_kernel(
         grouped = [
             keep.tile([P, ntok, 2], F32, name=f"group{tok0}", align_bytes=64) for tok0, ntok in CHUNKS
         ]
-        prods, rows_by_token, c_tok = {}, {}, {}
+        prods, by_token, c_tok = {}, {}, {}
+
+        def adds_on_vector(tok0, t):
+            return tok0 == 256 or (tok0 == 384 and t < 2)
+
+        def token_rows(g, t, dtype):
+            key = (g, t // 2 if g == 3 else 0)
+            if key not in by_token:
+                by_token[key] = psum.tile([P, H], dtype, name="by_token", tag=f"bank{g + key[1]}")
+            return by_token[key]
 
         def gather_product(tok0, ntok, t, r):
-            prods[tok0, t, r] = ring.tile([P, ntok], F32, name=f"prod{tok0}_{t}_{r}")
+            prod = ring.tile([P, ntok], F32, name=f"prod{tok0}_{t}_{r}")
+            prods[tok0, t, r] = prod
             nc.vector.tensor_tensor(
-                prods[tok0, t, r][:],
+                prod[:],
                 h[t][:].indirect(pos_sb[r][:, tok0 // 16 : (tok0 + ntok) // 16]),
                 gate_sb[:, r, tok0 : tok0 + ntok],
                 MULT,
             )
+            if not adds_on_vector(tok0, t):
+                for g in range(tok0 // P, (tok0 + ntok) // P):
+                    nc.tensor.matmul(
+                        token_rows(g, t, F32)[:, t * P : (t + 1) * P],
+                        prod[:, g * P - tok0 : (g + 1) * P - tok0],
+                        ident[:],
+                        start=(r == 0),
+                        stop=(r == 1),
+                        is_transpose=True,
+                    )
 
-        def combine(tok0, ntok, t):
+        def finish_step(tok0, ntok, t):
             tiles = range(tok0 // P, (tok0 + ntok) // P)
-            c_rows = keep.tile([P, ntok], BF16, name=f"c_rows{tok0}_{t}")
-            nc.vector.tensor_tensor(c_rows[:], prods[tok0, t, 0][:], prods[tok0, t, 1][:], ADD)
-            for g in tiles:
-                if t == 0:
-                    rows_by_token[g] = psum.tile([P, H], BF16, name="by_token", tag=f"bank{g}")
-                    c_tok[g] = keep.tile([P, 2, P], F32, name=f"c_tok{g}")
+            on_vector = adds_on_vector(tok0, t)
+            if on_vector:
+                c_rows = keep.tile([P, ntok], BF16, name=f"c_rows{tok0}_{t}")
+                nc.vector.tensor_tensor(c_rows[:], prods[tok0, t, 0][:], prods[tok0, t, 1][:], ADD)
                 nc.tensor.transpose(
-                    rows_by_token[g][:, t * P : (t + 1) * P],
-                    c_rows[:, g * P - tok0 : (g + 1) * P - tok0],
-                    ident_bf[:],
+                    token_rows(tok0 // P, t, BF16)[:, t * P : (t + 1) * P], c_rows[:], ident_bf[:]
                 )
             if t % 2 == 1:
                 rows = slice(32 * (t - 1), 32 * (t + 1))
                 for g in tiles:
-                    nc.scalar.copy(
-                        c_tok[g][:, :, rows],
-                        rows_by_token[g][:].bitcast(F32).rearrange("k (p u) -> k u p", u=2)[:, :, rows],
-                    )
+                    if t == 1:
+                        c_tok[g] = keep.tile([P, 2, P, 2], BF16, name=f"c_tok{g}")
+                    if on_vector:
+                        nc.scalar.copy(
+                            c_tok[g][:].rearrange("k u p e -> k u (p e)").bitcast(F32)[:, :, rows],
+                            token_rows(g, t, BF16)[:]
+                            .bitcast(F32)
+                            .rearrange("k (p u) -> k u p", u=2)[:, :, rows],
+                        )
+                    else:
+                        nc.scalar.copy(
+                            c_tok[g][:, :, rows, :],
+                            token_rows(g, t, F32)[:].rearrange("k (p u e) -> k u p e", u=2, e=2)[
+                                :, :, rows, :
+                            ],
+                        )
             if t == H_TILES - 1:
                 for g in tiles:
-                    turned = psum.tile([P, 2, P], F32, name="turned", tag=f"bank{4 + g}")
+                    words = c_tok[g][:].rearrange("k u p e -> k (u p e)").bitcast(F32)
+                    turned = psum.tile([P, 2, P], F32, name="turned", tag=f"bank{5 + g % 3}")
                     for u in range(2):
-                        nc.tensor.transpose(turned[:, u, :], c_tok[g][:, u, :], ident[:])
+                        nc.tensor.transpose(turned[:, u, :], words[:, u * P : (u + 1) * P], ident[:])
                     j = g % 3
                     nc.scalar.copy(
                         grouped[g // 3][:, j * P : (j + 1) * P, :], turned[:].rearrange("p u k -> p k u")
@@ -221,15 +250,15 @@ def tile_moe_sdn_lin_silu_kernel(
 
         steps = [
             (tok0, ntok, t)
-            for tok0, ntok, ts in ((0, 256, (0, 1, 2)), (256, 128, (0, 1)), (0, 256, (3,)), (256, 128, (2, 3)), (384, 128, (0, 1, 2, 3)))
+            for tok0, ntok, ts in ((0, 256, (0, 1)), (256, 128, (0, 1)), (0, 256, (2, 3)), (256, 128, (2, 3)), (384, 128, (0, 1, 2, 3)))
             for t in ts
         ]
         for n, step in enumerate(steps):
             gather_product(*step, 0)
             if n > 0:
-                combine(*steps[n - 1])
+                finish_step(*steps[n - 1])
             gather_product(*step, 1)
-        combine(*steps[-1])
+        finish_step(*steps[-1])
 
         for (tok0, ntok), group in zip(CHUNKS, grouped):
             values = group[:].rearrange("p k u -> p (k u)").bitcast(BF16)

@@ -15,14 +15,15 @@ U8 = mybir.dt.uint8
 FP8X4 = mybir.dt.float8_e4m3fn_x4
 FP4X4 = mybir.dt.float4_e2m1fn_x4
 MULT = mybir.AluOpType.mult
-ADD = mybir.AluOpType.add
 SILU = mybir.ActivationFunctionType.Silu
 
 P = 128
 PASSES = K // 512
 SLOTS = E * C
 H_TILES = H // P
-CHUNKS = ((0, 384), (384, 128))
+BANKS = 8
+CHUNKS = ((0, 256), (256, 128), (384, 128))
+XS_COLS = 768
 
 
 def tile_moe_sdn_lin_silu_kernel(
@@ -32,256 +33,231 @@ def tile_moe_sdn_lin_silu_kernel(
     with ExitStack() as ctx:
         lists = ctx.enter_context(tc.tile_pool(name="lists", bufs=1))
         keep = ctx.enter_context(tc.tile_pool(name="keep", bufs=1))
-        ring = ctx.enter_context(tc.tile_pool(name="ring", bufs=1))
         late = ctx.enter_context(tc.tile_pool(name="late", bufs=1))
         psum = ctx.enter_context(tc.psum_pool(name="psum", bufs=1))
+
+        used_banks = []
+
+        def next_bank(shape):
+            tag = f"bank{len(used_banks) % BANKS}"
+            used_banks.append(tag)
+            return psum.tile(shape, F32, name="bank", tag=tag)
 
         offs_sb = lists.tile([P, SLOTS // 16], U16, name="offs_sb")
         pos_sb = [lists.tile([P, T // 16], U16, name=f"pos_sb{r}") for r in range(2)]
 
-        xs_win = late.tile([P, T], U8, name="xs_win", align_bytes=64, offset=4096)
+        xs_win = late.tile([P, XS_COLS], U8, name="xs_win", align_bytes=64, offset=0)
+        w2s = keep.tile([P, N], U8, name="w2s", align_bytes=64)
         w1s = keep.tile([P, E * PASSES, H], U8, name="w1s", align_bytes=64)
-        planes = keep.tile([P, 2, SLOTS], U8, name="planes", align_bytes=64)
+        planes = [keep.tile([P, SLOTS], U8, name=f"plane{s}", align_bytes=64) for s in (1, 2)]
         zero = keep.tile([P, 8], F32, name="zero")
         nc.gpsimd.memset(xs_win[:].bitcast(I32), 0)
         nc.gpsimd.memset(zero[:], 0.0)
         nc.vector.memset(w1s[:].rearrange("p a n -> p (a n)").bitcast(I32), 0)
-        nc.gpsimd.memset(planes[:].rearrange("p a n -> p (a n)").bitcast(I32), 0)
+        for plane in planes:
+            nc.gpsimd.memset(plane[96:P, :].bitcast(I32), 0)
+        nc.gpsimd.memset(w2s[:].bitcast(I32), 0)
         ident = keep.tile([P, P], F32, name="ident")
         make_identity(nc, ident[:])
-        ident_bf = keep.tile([P, P], BF16, name="ident_bf")
-        make_identity(nc, ident_bf[:])
 
-        xw = keep.tile([P, PASSES, T], I32, name="xw", align_bytes=64)
+        x_first = keep.tile([P, T], I32, name="x_first", align_bytes=64)
+        x_rest = keep.tile([P, PASSES - 1, T], I32, name="x_rest", align_bytes=64)
         h = [keep.tile([P, SLOTS], F32, name=f"h{t}") for t in range(H_TILES)]
 
-        def load_x_scale_pair(queue, q):
-            queue.dma_start(
-                xs_win[32 * q : 32 * q + 8, :].bitcast(I32),
-                x_scales[0:2, 4 * q : 4 * q + 4, :].bitcast(I32),
-            )
-
-        nc.sync.dma_start(offs_sb[:], offs)
-        load_x_scale_pair(nc.scalar, 0)
-        load_x_scale_pair(nc.sync, 1)
-        load_x_scale_pair(nc.scalar, 2)
-        load_x_scale_pair(nc.sync, 3)
-        nc.scalar.dma_start(xs_win[8:24, :].bitcast(I32), x_scales[2].bitcast(I32))
-        nc.scalar.activation(h[0][:, 0:1], zero[:, 0:1], SILU)
-        nc.sync.dma_start(pos_sb[0][:], pos1)
         x_rows = x_words.rearrange("s p t d -> p s (t d)").bitcast(I32)
-        nc.sync.dma_start(xw[:, 0:1, :], x_rows[:, 0:1, :])
-        nc.sync.dma_start(xw[:, 1:PASSES, :], x_rows[:, 1:PASSES, :])
-        w1_rows = w1_words.rearrange("e s p (g b) -> g p (e s) b", g=2).bitcast(I32)
-        w1w_early = keep.tile([P, 2 * PASSES, H], U8, name="w1w_early", align_bytes=64)
-        nc.sync.dma_start(w1w_early[:].bitcast(I32), w1_rows[0][:, 0 : 2 * PASSES, :])
-        nc.sync.dma_start(pos_sb[1][:], pos2)
-
-        w1s_rows = w1_scales.rearrange("e s b n -> b (e s) n")
+        nc.sync.dma_start(offs_sb[:], offs)
+        nc.sync.dma_start(x_first[:], x_rows[:, 0, :])
         for q in range(4):
-            nc.scalar.dma_start(
-                w1s[32 * q : 32 * q + 4, :, :].bitcast(I32), w1s_rows[4 * q : 4 * q + 4].bitcast(I32)
+            queue = nc.scalar if q % 2 == 0 else nc.sync
+            queue.dma_start(
+                xs_win[32 * q : 32 * q + 4 * PASSES, 0:T].bitcast(I32),
+                x_scales[:, 4 * q : 4 * q + 4, :].bitcast(I32),
             )
+        nc.scalar.activation(h[0][:, 0:1], zero[:, 0:1], SILU)
+        nc.sync.dma_start(x_rest[:], x_rows[:, 1:PASSES, :])
+        w1s_rows = w1_scales.rearrange("e s (q r) n -> r q (e s) n", r=4)
+        for r in range(4):
+            nc.sync.dma_start(w1s[r:P:32, :, :].bitcast(I32), w1s_rows[r].bitcast(I32))
+        w1_rows = w1_words.rearrange("e s p b -> p (e s) b").bitcast(I32)
+        w1w_early = keep.tile([P, 2 * PASSES, 2 * H], U8, name="w1w_early", align_bytes=64)
+        nc.sync.dma_start(w1w_early[:].bitcast(I32), w1_rows[:, 0 : 2 * PASSES, :])
+        w1w_late = keep.tile([P, 2 * PASSES, 2 * H], U8, name="w1w_late", align_bytes=64)
+        nc.sync.dma_start(w1w_late[:].bitcast(I32), w1_rows[:, 2 * PASSES :, :])
+        gate_sb = keep.tile([P, 2, T], F32, name="gate_sb", align_bytes=64)
+        nc.sync.dma_start(gate_sb[:], gate.rearrange("r p t -> p r t"))
+        nc.sync.dma_start(pos_sb[0][:], pos1)
+        nc.sync.dma_start(pos_sb[1][:], pos2)
+        w2w = keep.tile([P, 2 * N], U8, name="w2w", align_bytes=64)
+        nc.sync.dma_start(w2w[:].bitcast(I32), w2_words[0].bitcast(I32))
+        w2s_rows = w2_scales[0].rearrange("(q r) n -> r q n", r=4)
+        for r in range(4):
+            nc.sync.dma_start(w2s[r:P:32, :].bitcast(I32), w2s_rows[r].bitcast(I32))
 
         gs = keep.tile([P, SLOTS], U8, name="gs", align_bytes=64)
         gw = [
-            [
-                keep.tile([P, C], U32, name=f"gw{e}_{s}", tag=f"gw{e}_{s}", align_bytes=64)
-                for s in range(PASSES)
-            ]
-            for e in range(E)
+            [keep.tile([P, C], U32, name=f"gw{e}_{s}", align_bytes=64)[:] for s in range(PASSES)]
+            for e in range(2)
         ]
-
-        def expert_offsets(e):
-            return offs_sb[:, e * C // 16 : (e + 1) * C // 16]
-
-        for e in range(E):
-            nc.vector.tensor_copy(gs[:, e * C : (e + 1) * C], xs_win[:].indirect(expert_offsets(e)))
-        nc.sync.dma_start(planes[0:112, 0, :].bitcast(I32), gs[4:116, :].bitcast(I32))
-        for q in range(4):
-            nc.scalar.dma_start(
-                planes[32 * q : 32 * q + 4, 1, :].bitcast(I32),
-                gs[8 + 4 * q : 12 + 4 * q, :].bitcast(I32),
+        gw_held = late.tile([P, 2 * C], U32, name="gw_held", align_bytes=64, offset=0)
+        for e in range(2, E):
+            gw.append(
+                [gw_held[:, (e - 2) * C : (e - 1) * C]]
+                + [keep.tile([P, C], U32, name=f"gw{e}_{s}", align_bytes=64)[:] for s in range(1, PASSES)]
             )
-        w1w_late = late.tile([P, 6 * PASSES, H], U8, name="w1w_late", align_bytes=64, offset=4352)
-        nc.scalar.dma_start(
-            w1w_late[:, 0 : 2 * PASSES, :].bitcast(I32), w1_rows[0][:, 2 * PASSES :, :]
-        )
-        gate_sb = late.tile([P, 2, T], F32, name="gate_sb", align_bytes=64, offset=256)
-        nc.scalar.dma_start(gate_sb[:], gate.rearrange("r p t -> p r t"))
-        nc.scalar.dma_start(w1w_late[:, 2 * PASSES :, :].bitcast(I32), w1_rows[1])
-        for e in range(E):
-            for s in range(PASSES):
-                width = P if (e, s) == (E - 1, PASSES - 1) else C
-                for a in range(0, C, width):
-                    first = (e * C + a) // 16
-                    nc.vector.tensor_copy(
-                        gw[e][s][:, a : a + width],
-                        xw[:, s, :].bitcast(U32).indirect(offs_sb[:, first : first + width // 16]),
-                    )
 
-        def w1_codes(e, t, s):
-            cols = slice(2 * P * (t % 2), 2 * P * (t % 2 + 1))
-            if t >= 2:
-                return w1w_late[:, (2 + e) * PASSES + s, cols]
-            if e >= 2:
-                return w1w_late[:, (e - 2) * PASSES + s, cols]
-            return w1w_early[:, e * PASSES + s, cols]
+        def gather_words(e, s, a=0, width=C):
+            window = x_first[:] if s == 0 else x_rest[:, s - 1, :]
+            first = (e * C + a) // 16
+            nc.vector.tensor_copy(
+                gw[e][s][:, a : a + width],
+                window.bitcast(U32).indirect(offs_sb[:, first : first + width // 16]),
+            )
+
+        gather_words(0, 0)
+        gather_words(1, 0)
+        for a in range(0, SLOTS, 2 * C):
+            nc.vector.tensor_copy(
+                gs[:, a : a + 2 * C], xs_win[:].indirect(offs_sb[:, a // 16 : (a + 2 * C) // 16])
+            )
+        for s in range(1, PASSES):
+            nc.scalar.dma_start(planes[s - 1][0:112, :].bitcast(I32), gs[4 * s : 4 * s + 112, :].bitcast(I32))
+
+        for e in range(2):
+            for s in range(1, PASSES):
+                gather_words(e, s)
+        for e in range(2, E):
+            for s in range(PASSES):
+                if (e, s) == (E - 1, PASSES - 1):
+                    gather_words(e, s, 0, P)
+                    gather_words(e, s, P, P)
+                else:
+                    gather_words(e, s)
 
         def first_pass(acc, e, t, half, s):
             cols = slice(e * C + half * P, e * C + (half + 1) * P)
+            w1w = w1w_early if e < 2 else w1w_late
             nc.tensor.matmul_mx(
                 out=acc,
-                lhsT=w1_codes(e, t, s).bitcast(FP4X4),
+                lhsT=w1w[:, (e % 2) * PASSES + s, 2 * P * t : 2 * P * (t + 1)].bitcast(FP4X4),
                 lhsT_scale=w1s[:, e * PASSES + s, P * t : P * (t + 1)],
                 rhs=gw[e][s][:, half * P : (half + 1) * P].bitcast(FP8X4),
-                rhs_scale=gs[:, cols] if s == 0 else planes[:, s - 1, cols],
+                rhs_scale=gs[:, cols] if s == 0 else planes[s - 1][:, cols],
                 start=(s == 0),
                 stop=(s == PASSES - 1),
             )
 
-        def hidden_in_own_banks(e, groups):
-            accs = [psum.tile([P, P], F32, name="acc", tag=f"bank{b}") for b in range(len(groups))]
+        def hidden_in_own_banks(units):
+            groups = [(e, t, half) for e, t in units for half in range(2)]
+            accs = [next_bank([P, P]) for group in groups]
             for s in range(PASSES):
-                for acc, (t, half) in zip(accs, groups):
-                    first_pass(acc[:], e, t, half, s)
-            for acc, (t, half) in zip(accs, groups):
+                for acc, group in zip(accs, groups):
+                    first_pass(acc[:], *group, s)
+            for acc, (e, t, half) in zip(accs, groups):
                 col = e * C + half * P
                 nc.scalar.activation(h[t][:, col : col + P], acc[:], SILU)
 
-        def hidden_in_one_bank(e, t, bank):
-            acc = psum.tile([P, C], F32, name="acc", tag=f"bank{bank}")
+        def hidden_in_one_bank(e, t):
+            acc = next_bank([P, C])
             for half in range(2):
                 for s in range(PASSES):
                     first_pass(acc[:, half * P : (half + 1) * P], e, t, half, s)
             nc.scalar.activation(h[t][:, e * C : (e + 1) * C], acc[:], SILU)
 
-        hidden_in_own_banks(0, [(t, half) for t in range(2) for half in range(2)])
-        for e in (1, 2):
-            for t in range(2):
-                hidden_in_one_bank(e, t, 2 + 2 * e + t)
-        hidden_in_own_banks(3, [(0, 0), (0, 1)])
-        hidden_in_one_bank(3, 1, 2)
-        for t in (2, 3):
+        hidden_in_own_banks([(e, t) for t in range(2) for e in range(2)])
+        for t in range(2):
+            hidden_in_one_bank(2, t)
+        hidden_in_own_banks([(E - 1, 0)])
+        hidden_in_one_bank(E - 1, 1)
+        for t in range(2, H_TILES):
             for e in range(E):
-                hidden_in_one_bank(e, t, (3 + (t - 2) * E + e) % 8)
+                hidden_in_one_bank(e, t)
 
-        w2w = keep.tile([P, 2 * N], U8, name="w2w", tag="gw0_1", align_bytes=64)
-        nc.sync.dma_start(w2w[:].bitcast(I32), w2_words[0].bitcast(I32))
-        w2s = keep.tile([P, N], U8, name="w2s", tag="gw0_0", align_bytes=64)
-        nc.gpsimd.memset(w2s[:].bitcast(I32), 0)
-        for q in range(4):
-            nc.sync.dma_start(
-                w2s[32 * q : 32 * q + 4, :].bitcast(I32), w2_scales[0, 4 * q : 4 * q + 4, :].bitcast(I32)
-            )
-
-        grouped = [
-            keep.tile([P, ntok, 2], F32, name=f"group{tok0}", align_bytes=64) for tok0, ntok in CHUNKS
+        c_tok = [
+            keep.tile([P, ntok // P, 2, P, 2], BF16, name=f"c_tok{tok0}") for tok0, ntok in CHUNKS
         ]
-        prods, by_token, c_tok = {}, {}, {}
 
-        def adds_on_vector(tok0, t):
-            return tok0 == 256 or (tok0 == 384 and t < 2)
-
-        def token_rows(g, t, dtype):
-            key = (g, t // 2 if g == 3 else 0)
-            if key not in by_token:
-                by_token[key] = psum.tile([P, H], dtype, name="by_token", tag=f"bank{g + key[1]}")
-            return by_token[key]
-
-        def gather_product(tok0, ntok, t, r):
-            prod = ring.tile([P, ntok], F32, name=f"prod{tok0}_{t}_{r}")
-            prods[tok0, t, r] = prod
-            nc.vector.tensor_tensor(
-                prod[:],
-                h[t][:].indirect(pos_sb[r][:, tok0 // 16 : (tok0 + ntok) // 16]),
-                gate_sb[:, r, tok0 : tok0 + ntok],
-                MULT,
-            )
-            if not adds_on_vector(tok0, t):
-                for g in range(tok0 // P, (tok0 + ntok) // P):
+        def combine(chunks, t):
+            tok0 = CHUNKS[chunks[0]][0]
+            ntok = sum(CHUNKS[j][1] for j in chunks)
+            prods = []
+            for r in range(2):
+                prod = keep.tile([P, ntok], F32, name=f"prod{tok0}_{t}_{r}")
+                nc.vector.tensor_tensor(
+                    prod[:],
+                    h[t][:].indirect(pos_sb[r][:, tok0 // 16 : (tok0 + ntok) // 16]),
+                    gate_sb[:, r, tok0 : tok0 + ntok],
+                    MULT,
+                )
+                prods.append(prod)
+            sums = next_bank([P, ntok])
+            for a in range(0, ntok, P):
+                for r in range(2):
                     nc.tensor.matmul(
-                        token_rows(g, t, F32)[:, t * P : (t + 1) * P],
-                        prod[:, g * P - tok0 : (g + 1) * P - tok0],
+                        sums[:, a : a + P],
+                        prods[r][:, a : a + P],
                         ident[:],
                         start=(r == 0),
                         stop=(r == 1),
                         is_transpose=True,
                     )
-
-        def finish_step(tok0, ntok, t):
-            tiles = range(tok0 // P, (tok0 + ntok) // P)
-            on_vector = adds_on_vector(tok0, t)
-            if on_vector:
-                c_rows = keep.tile([P, ntok], BF16, name=f"c_rows{tok0}_{t}")
-                nc.vector.tensor_tensor(c_rows[:], prods[tok0, t, 0][:], prods[tok0, t, 1][:], ADD)
-                nc.tensor.transpose(
-                    token_rows(tok0 // P, t, BF16)[:, t * P : (t + 1) * P], c_rows[:], ident_bf[:]
+            for j in chunks:
+                a, n = CHUNKS[j][0] - tok0, CHUNKS[j][1]
+                nc.scalar.copy(
+                    c_tok[j][:, :, :, 32 * t : 32 * (t + 1), :],
+                    sums[:, a : a + n].rearrange("k (g p u e) -> k g u p e", p=32, u=2, e=2),
                 )
-            if t % 2 == 1:
-                rows = slice(32 * (t - 1), 32 * (t + 1))
-                for g in tiles:
-                    if t == 1:
-                        c_tok[g] = keep.tile([P, 2, P, 2], BF16, name=f"c_tok{g}")
-                    if on_vector:
-                        nc.scalar.copy(
-                            c_tok[g][:].rearrange("k u p e -> k u (p e)").bitcast(F32)[:, :, rows],
-                            token_rows(g, t, BF16)[:]
-                            .bitcast(F32)
-                            .rearrange("k (p u) -> k u p", u=2)[:, :, rows],
-                        )
-                    else:
-                        nc.scalar.copy(
-                            c_tok[g][:, :, rows, :],
-                            token_rows(g, t, F32)[:].rearrange("k (p u e) -> k u p e", u=2, e=2)[
-                                :, :, rows, :
-                            ],
-                        )
-            if t == H_TILES - 1:
-                for g in tiles:
-                    words = c_tok[g][:].rearrange("k u p e -> k (u p e)").bitcast(F32)
-                    turned = psum.tile([P, 2, P], F32, name="turned", tag=f"bank{5 + g % 3}")
-                    for u in range(2):
-                        nc.tensor.transpose(turned[:, u, :], words[:, u * P : (u + 1) * P], ident[:])
-                    j = g % 3
-                    nc.scalar.copy(
-                        grouped[g // 3][:, j * P : (j + 1) * P, :], turned[:].rearrange("p u k -> p k u")
-                    )
 
-        steps = [
-            (tok0, ntok, t)
-            for tok0, ntok, ts in ((0, 256, (0, 1)), (256, 128, (0, 1)), (0, 256, (2, 3)), (256, 128, (2, 3)), (384, 128, (0, 1, 2, 3)))
-            for t in ts
-        ]
-        for n, step in enumerate(steps):
-            gather_product(*step, 0)
-            if n > 0:
-                finish_step(*steps[n - 1])
-            gather_product(*step, 1)
-        finish_step(*steps[-1])
+        def turn_back(j, copy):
+            tiles = CHUNKS[j][1] // P
+            words = c_tok[j][:].rearrange("k g u p e -> k (g u p e)").bitcast(F32)
+            turned = next_bank([P, tiles, 2, P])
+            for g in range(tiles):
+                for u in range(2):
+                    a = (2 * g + u) * P
+                    nc.tensor.transpose(turned[:, g, u, :], words[:, a : a + P], ident[:])
+            group = keep.tile([P, tiles, P, 2], F32, name=f"group{j}", align_bytes=64)
+            copy(group[:], turned[:].rearrange("p g u k -> p g k u"))
+            return group
 
-        for (tok0, ntok), group in zip(CHUNKS, grouped):
-            values = group[:].rearrange("p k u -> p (k u)").bitcast(BF16)
-            codes = keep.tile([P, ntok], U32, name=f"codes{tok0}", align_bytes=64)
-            scales = keep.tile([P, ntok], U8, name=f"scales{tok0}", align_bytes=64)
+        def second_product(j, group, res):
+            ntok = CHUNKS[j][1]
+            codes = keep.tile([P, ntok], U32, name=f"codes{j}", align_bytes=64)
+            scales = keep.tile([P, ntok], U8, name=f"scales{j}", align_bytes=64)
+            nc.vector.quantize_mx(
+                out=codes[:].bitcast(FP8X4),
+                scales=scales[:],
+                in_=group[:].rearrange("p g k u -> p (g k u)").bitcast(BF16),
+            )
+            nc.tensor.matmul_mx(
+                out=res,
+                lhsT=w2w[:].bitcast(FP4X4),
+                lhsT_scale=w2s[:],
+                rhs=codes[:].bitcast(FP8X4),
+                rhs_scale=scales[:],
+                start=True,
+                stop=True,
+            )
+
+        def store(tok0, ntok, res, copy):
             result = keep.tile([P, ntok], F32, name=f"result{tok0}")
-            res = psum.tile([P, ntok], F32, name="res", tag="bank0" if tok0 == 0 else "bank1")
-            pieces = [(a, min(256, ntok - a)) for a in range(0, ntok, 256)]
-            for a, n in pieces:
-                nc.vector.quantize_mx(
-                    out=codes[:, a : a + n].bitcast(FP8X4),
-                    scales=scales[:, a : a + n],
-                    in_=values[:, 4 * a : 4 * (a + n)],
-                )
-            for a, n in pieces:
-                nc.tensor.matmul_mx(
-                    out=res[:, a : a + n],
-                    lhsT=w2w[:].bitcast(FP4X4),
-                    lhsT_scale=w2s[:],
-                    rhs=codes[:, a : a + n].bitcast(FP8X4),
-                    rhs_scale=scales[:, a : a + n],
-                    start=True,
-                    stop=True,
-                )
-            nc.vector.tensor_copy(result[:], res[:])
+            copy(result[:], res)
             nc.sync.dma_start(out[:, tok0 : tok0 + ntok], result[:])
+
+        combine((0, 1, 2), 0)
+        combine((0, 1, 2), 1)
+        combine((0,), 2)
+        combine((0,), 3)
+        combine((1,), 2)
+        group0 = turn_back(0, nc.scalar.copy)
+        combine((1,), 3)
+        combine((2,), 2)
+        combine((2,), 3)
+        group1 = turn_back(1, nc.vector.tensor_copy)
+        res_a = next_bank([P, 384])
+        second_product(0, group0, res_a[:, 0:256])
+        group2 = turn_back(2, nc.vector.tensor_copy)
+        second_product(1, group1, res_a[:, 256:384])
+        store(0, 384, res_a[:], nc.scalar.copy)
+        res_b = next_bank([P, P])
+        second_product(2, group2, res_b[:])
+        store(384, P, res_b[:], nc.vector.tensor_copy)

@@ -24,6 +24,7 @@ H_TILES = H // P
 BANKS = 8
 CHUNKS = ((0, 256), (256, 128), (384, 128))
 XS_COLS = 768
+LATE_W1 = 2 * PASSES * 2 * H
 
 
 def tile_moe_sdn_lin_silu_kernel(
@@ -46,45 +47,48 @@ def tile_moe_sdn_lin_silu_kernel(
         offs_sb = lists.tile([P, SLOTS // 16], U16, name="offs_sb")
         pos_sb = [lists.tile([P, T // 16], U16, name=f"pos_sb{r}") for r in range(2)]
 
-        xs_win = late.tile([P, XS_COLS], U8, name="xs_win", align_bytes=64, offset=0)
-        w2s = keep.tile([P, N], U8, name="w2s", align_bytes=64)
+        xs_win = late.tile([P, XS_COLS], U8, name="xs_win", align_bytes=64, offset=LATE_W1 - 64)
         w1s = keep.tile([P, E * PASSES, H], U8, name="w1s", align_bytes=64)
+        w2s = keep.tile([P, N], U8, name="w2s", align_bytes=64)
         planes = [keep.tile([P, SLOTS], U8, name=f"plane{s}", align_bytes=64) for s in (1, 2)]
         zero = keep.tile([P, 8], F32, name="zero")
+        ident = keep.tile([P, P], F32, name="ident")
         nc.gpsimd.memset(xs_win[:].bitcast(I32), 0)
         nc.gpsimd.memset(zero[:], 0.0)
         nc.vector.memset(w1s[:].rearrange("p a n -> p (a n)").bitcast(I32), 0)
-        for plane in planes:
-            nc.gpsimd.memset(plane[96:P, :].bitcast(I32), 0)
+        nc.vector.memset(ident[:], 0.0)
+        nc.gpsimd.memset(planes[0][96:P, :].bitcast(I32), 0)
+        nc.gpsimd.memset(planes[1][:].bitcast(I32), 0)
         nc.gpsimd.memset(w2s[:].bitcast(I32), 0)
-        ident = keep.tile([P, P], F32, name="ident")
-        make_identity(nc, ident[:])
+        make_identity(nc, ident[:], nomemset=True)
 
-        x_first = keep.tile([P, T], I32, name="x_first", align_bytes=64)
-        x_rest = keep.tile([P, PASSES - 1, T], I32, name="x_rest", align_bytes=64)
+        xw = keep.tile([P, PASSES, T], I32, name="xw", align_bytes=64)
         h = [keep.tile([P, SLOTS], F32, name=f"h{t}") for t in range(H_TILES)]
 
-        x_rows = x_words.rearrange("s p t d -> p s (t d)").bitcast(I32)
         nc.sync.dma_start(offs_sb[:], offs)
-        nc.sync.dma_start(x_first[:], x_rows[:, 0, :])
         for q in range(4):
             queue = nc.scalar if q % 2 == 0 else nc.sync
             queue.dma_start(
-                xs_win[32 * q : 32 * q + 4 * PASSES, 0:T].bitcast(I32),
-                x_scales[:, 4 * q : 4 * q + 4, :].bitcast(I32),
+                xs_win[32 * q : 32 * q + 8, 0:T].bitcast(I32),
+                x_scales[0:2, 4 * q : 4 * q + 4, :].bitcast(I32),
             )
-        nc.scalar.activation(h[0][:, 0:1], zero[:, 0:1], SILU)
-        nc.sync.dma_start(x_rest[:], x_rows[:, 1:PASSES, :])
+        nc.sync.dma_start(xs_win[8:24, 0:T].bitcast(I32), x_scales[2].bitcast(I32))
+        nc.sync.dma_start(xw[:], x_words.rearrange("s p t d -> p s (t d)").bitcast(I32))
+        w1_rows = w1_words.rearrange("e s p b -> p (e s) b").bitcast(I32)
+        w1w = []
+
+        def load_experts(queue, words, first):
+            count = words.shape[1] // PASSES
+            queue.dma_start(words[:].bitcast(I32), w1_rows[:, first * PASSES : (first + count) * PASSES, :])
+            w1w.extend(words[:, j * PASSES : (j + 1) * PASSES, :] for j in range(count))
+
+        load_experts(nc.sync, keep.tile([P, PASSES, 2 * H], U8, name="w1w0", align_bytes=64), 0)
         w1s_rows = w1_scales.rearrange("e s (q r) n -> r q (e s) n", r=4)
         for r in range(4):
-            nc.sync.dma_start(w1s[r:P:32, :, :].bitcast(I32), w1s_rows[r].bitcast(I32))
-        w1_rows = w1_words.rearrange("e s p b -> p (e s) b").bitcast(I32)
-        w1w_early = keep.tile([P, 2 * PASSES, 2 * H], U8, name="w1w_early", align_bytes=64)
-        nc.sync.dma_start(w1w_early[:].bitcast(I32), w1_rows[:, 0 : 2 * PASSES, :])
-        w1w_late = keep.tile([P, 2 * PASSES, 2 * H], U8, name="w1w_late", align_bytes=64)
-        nc.sync.dma_start(w1w_late[:].bitcast(I32), w1_rows[:, 2 * PASSES :, :])
-        gate_sb = keep.tile([P, 2, T], F32, name="gate_sb", align_bytes=64)
-        nc.sync.dma_start(gate_sb[:], gate.rearrange("r p t -> p r t"))
+            queue = nc.scalar if r < 2 else nc.sync
+            queue.dma_start(w1s[r:P:32, :, :].bitcast(I32), w1s_rows[r].bitcast(I32))
+        nc.scalar.activation(h[0][:, 0:1], zero[:, 0:1], SILU)
+        load_experts(nc.sync, keep.tile([P, PASSES, 2 * H], U8, name="w1w1", align_bytes=64), 1)
         nc.sync.dma_start(pos_sb[0][:], pos1)
         nc.sync.dma_start(pos_sb[1][:], pos2)
         w2w = keep.tile([P, 2 * N], U8, name="w2w", align_bytes=64)
@@ -95,37 +99,29 @@ def tile_moe_sdn_lin_silu_kernel(
 
         gs = keep.tile([P, SLOTS], U8, name="gs", align_bytes=64)
         gw = [
-            [keep.tile([P, C], U32, name=f"gw{e}_{s}", align_bytes=64)[:] for s in range(PASSES)]
-            for e in range(2)
+            [keep.tile([P, C], U32, name=f"gw{e}_{s}", align_bytes=64) for s in range(PASSES)]
+            for e in range(E)
         ]
-        gw_held = late.tile([P, 2 * C], U32, name="gw_held", align_bytes=64, offset=0)
-        for e in range(2, E):
-            gw.append(
-                [gw_held[:, (e - 2) * C : (e - 1) * C]]
-                + [keep.tile([P, C], U32, name=f"gw{e}_{s}", align_bytes=64)[:] for s in range(1, PASSES)]
-            )
 
         def gather_words(e, s, a=0, width=C):
-            window = x_first[:] if s == 0 else x_rest[:, s - 1, :]
             first = (e * C + a) // 16
             nc.vector.tensor_copy(
                 gw[e][s][:, a : a + width],
-                window.bitcast(U32).indirect(offs_sb[:, first : first + width // 16]),
+                xw[:, s, :].bitcast(U32).indirect(offs_sb[:, first : first + width // 16]),
             )
 
-        gather_words(0, 0)
-        gather_words(1, 0)
         for a in range(0, SLOTS, 2 * C):
             nc.vector.tensor_copy(
                 gs[:, a : a + 2 * C], xs_win[:].indirect(offs_sb[:, a // 16 : (a + 2 * C) // 16])
             )
-        for s in range(1, PASSES):
-            nc.scalar.dma_start(planes[s - 1][0:112, :].bitcast(I32), gs[4 * s : 4 * s + 112, :].bitcast(I32))
+        nc.scalar.dma_start(planes[0][0:112, :].bitcast(I32), gs[4:116, :].bitcast(I32))
+        for r in range(4):
+            nc.scalar.dma_start(planes[1][r:P:32, :].bitcast(I32), gs[8 + r : 24 : 4, :].bitcast(I32))
+        load_experts(nc.scalar, late.tile([P, 2 * PASSES, 2 * H], U8, name="w1w2", align_bytes=64, offset=0), 2)
+        gate_sb = late.tile([P, 2, T], F32, name="gate_sb", align_bytes=64, offset=LATE_W1)
+        nc.scalar.dma_start(gate_sb[:], gate.rearrange("r p t -> p r t"))
 
-        for e in range(2):
-            for s in range(1, PASSES):
-                gather_words(e, s)
-        for e in range(2, E):
+        for e in range(E):
             for s in range(PASSES):
                 if (e, s) == (E - 1, PASSES - 1):
                     gather_words(e, s, 0, P)
@@ -135,10 +131,9 @@ def tile_moe_sdn_lin_silu_kernel(
 
         def first_pass(acc, e, t, half, s):
             cols = slice(e * C + half * P, e * C + (half + 1) * P)
-            w1w = w1w_early if e < 2 else w1w_late
             nc.tensor.matmul_mx(
                 out=acc,
-                lhsT=w1w[:, (e % 2) * PASSES + s, 2 * P * t : 2 * P * (t + 1)].bitcast(FP4X4),
+                lhsT=w1w[e][:, s, 2 * P * t : 2 * P * (t + 1)].bitcast(FP4X4),
                 lhsT_scale=w1s[:, e * PASSES + s, P * t : P * (t + 1)],
                 rhs=gw[e][s][:, half * P : (half + 1) * P].bitcast(FP8X4),
                 rhs_scale=gs[:, cols] if s == 0 else planes[s - 1][:, cols],
@@ -163,14 +158,6 @@ def tile_moe_sdn_lin_silu_kernel(
                     first_pass(acc[:, half * P : (half + 1) * P], e, t, half, s)
             nc.scalar.activation(h[t][:, e * C : (e + 1) * C], acc[:], SILU)
 
-        hidden_in_own_banks([(e, t) for t in range(2) for e in range(2)])
-        for t in range(2):
-            hidden_in_one_bank(2, t)
-        hidden_in_own_banks([(E - 1, 0)])
-        hidden_in_one_bank(E - 1, 1)
-        for t in range(2, H_TILES):
-            for e in range(E):
-                hidden_in_one_bank(e, t)
 
         c_tok = [
             keep.tile([P, ntok // P, 2, P, 2], BF16, name=f"c_tok{tok0}") for tok0, ntok in CHUNKS
@@ -243,7 +230,18 @@ def tile_moe_sdn_lin_silu_kernel(
             copy(result[:], res)
             nc.sync.dma_start(out[:, tok0 : tok0 + ntok], result[:])
 
+        hidden_in_own_banks([(0, 0), (0, 1)])
+        for e in range(1, E - 1):
+            for t in range(2):
+                hidden_in_one_bank(e, t)
+        hidden_in_one_bank(0, 2)
+        hidden_in_own_banks([(E - 1, 0)])
+        hidden_in_one_bank(E - 1, 1)
+        for e in range(1, E):
+            hidden_in_one_bank(e, 2)
         combine((0, 1, 2), 0)
+        for e in range(E):
+            hidden_in_one_bank(e, 3)
         combine((0, 1, 2), 1)
         combine((0,), 2)
         combine((0,), 3)

@@ -22,7 +22,7 @@ PASSES = K // 512
 SLOTS = E * C
 H_TILES = H // P
 BANKS = 8
-CHUNKS = ((0, 256), (256, 128), (384, 128))
+CHUNKS = ((0, 128), (128, 128), (256, 128), (384, 128))
 XS_COLS = 768
 LATE_W1 = 2 * PASSES * 2 * H
 
@@ -88,14 +88,6 @@ def tile_moe_sdn_lin_silu_kernel(
             queue = nc.scalar if r < 2 else nc.sync
             queue.dma_start(w1s[r:P:32, :, :].bitcast(I32), w1s_rows[r].bitcast(I32))
         nc.scalar.activation(h[0][:, 0:1], zero[:, 0:1], SILU)
-        load_experts(nc.sync, keep.tile([P, PASSES, 2 * H], U8, name="w1w1", align_bytes=64), 1)
-        nc.sync.dma_start(pos_sb[0][:], pos1)
-        nc.sync.dma_start(pos_sb[1][:], pos2)
-        w2w = keep.tile([P, 2 * N], U8, name="w2w", align_bytes=64)
-        nc.sync.dma_start(w2w[:].bitcast(I32), w2_words[0].bitcast(I32))
-        w2s_rows = w2_scales[0].rearrange("(q r) n -> r q n", r=4)
-        for r in range(4):
-            nc.sync.dma_start(w2s[r:P:32, :].bitcast(I32), w2s_rows[r].bitcast(I32))
 
         gs = keep.tile([P, SLOTS], U8, name="gs", align_bytes=64)
         gw = [
@@ -114,12 +106,20 @@ def tile_moe_sdn_lin_silu_kernel(
             nc.vector.tensor_copy(
                 gs[:, a : a + 2 * C], xs_win[:].indirect(offs_sb[:, a // 16 : (a + 2 * C) // 16])
             )
-        nc.scalar.dma_start(planes[0][0:112, :].bitcast(I32), gs[4:116, :].bitcast(I32))
+        nc.sync.dma_start(planes[0][0:112, :].bitcast(I32), gs[4:116, :].bitcast(I32))
         for r in range(4):
             nc.scalar.dma_start(planes[1][r:P:32, :].bitcast(I32), gs[8 + r : 24 : 4, :].bitcast(I32))
-        load_experts(nc.scalar, late.tile([P, 2 * PASSES, 2 * H], U8, name="w1w2", align_bytes=64, offset=0), 2)
+        load_experts(nc.sync, keep.tile([P, PASSES, 2 * H], U8, name="w1w1", align_bytes=64), 1)
+        load_experts(nc.sync, late.tile([P, 2 * PASSES, 2 * H], U8, name="w1w2", align_bytes=64, offset=0), 2)
         gate_sb = late.tile([P, 2, T], F32, name="gate_sb", align_bytes=64, offset=LATE_W1)
-        nc.scalar.dma_start(gate_sb[:], gate.rearrange("r p t -> p r t"))
+        nc.sync.dma_start(gate_sb[:], gate.rearrange("r p t -> p r t"))
+        nc.sync.dma_start(pos_sb[0][:], pos1)
+        nc.sync.dma_start(pos_sb[1][:], pos2)
+        w2w = keep.tile([P, 2 * N], U8, name="w2w", align_bytes=64)
+        nc.sync.dma_start(w2w[:].bitcast(I32), w2_words[0].bitcast(I32))
+        w2s_rows = w2_scales[0].rearrange("(q r) n -> r q n", r=4)
+        for r in range(4):
+            nc.sync.dma_start(w2s[r:P:32, :].bitcast(I32), w2s_rows[r].bitcast(I32))
 
         for e in range(E):
             for s in range(PASSES):
@@ -225,37 +225,37 @@ def tile_moe_sdn_lin_silu_kernel(
                 stop=True,
             )
 
-        def store(tok0, ntok, res, copy):
+        def store(tok0, ntok, res, copy, queue):
             result = keep.tile([P, ntok], F32, name=f"result{tok0}")
             copy(result[:], res)
-            nc.sync.dma_start(out[:, tok0 : tok0 + ntok], result[:])
+            queue.dma_start(out[:, tok0 : tok0 + ntok], result[:])
 
         hidden_in_own_banks([(0, 0), (0, 1)])
-        for e in range(1, E - 1):
-            for t in range(2):
+        for t in range(2):
+            hidden_in_one_bank(1, t)
+        hidden_in_one_bank(2, 0)
+        hidden_in_own_banks([(3, 0)])
+        for e in range(2, E):
+            hidden_in_one_bank(e, 1)
+        for t in range(2, H_TILES):
+            for e in range(E):
                 hidden_in_one_bank(e, t)
-        hidden_in_one_bank(0, 2)
-        hidden_in_own_banks([(E - 1, 0)])
-        hidden_in_one_bank(E - 1, 1)
-        for e in range(1, E):
-            hidden_in_one_bank(e, 2)
-        combine((0, 1, 2), 0)
-        for e in range(E):
-            hidden_in_one_bank(e, 3)
-        combine((0, 1, 2), 1)
-        combine((0,), 2)
-        combine((0,), 3)
-        combine((1,), 2)
-        group0 = turn_back(0, nc.scalar.copy)
-        combine((1,), 3)
-        combine((2,), 2)
-        combine((2,), 3)
-        group1 = turn_back(1, nc.vector.tensor_copy)
-        res_a = next_bank([P, 384])
-        second_product(0, group0, res_a[:, 0:256])
-        group2 = turn_back(2, nc.vector.tensor_copy)
-        second_product(1, group1, res_a[:, 256:384])
-        store(0, 384, res_a[:], nc.scalar.copy)
+        combine((0, 1, 2, 3), 0)
+        combine((0, 1, 2, 3), 1)
+        combine((0, 1, 2), 2)
+        for j in range(3):
+            combine((j,), 3)
+        groups = [turn_back(0, nc.scalar.copy)]
+        combine((3,), 2)
+        groups.append(turn_back(1, nc.scalar.copy))
+        combine((3,), 3)
+        groups.append(turn_back(2, nc.vector.tensor_copy))
+        res_a = next_bank([P, 3 * P])
+        for j in range(2):
+            second_product(j, groups[j], res_a[:, j * P : (j + 1) * P])
+        groups.append(turn_back(3, nc.vector.tensor_copy))
+        second_product(2, groups[2], res_a[:, 2 * P : 3 * P])
+        store(0, 3 * P, res_a[:], nc.scalar.copy, nc.sync)
         res_b = next_bank([P, P])
-        second_product(2, group2, res_b[:])
-        store(384, P, res_b[:], nc.vector.tensor_copy)
+        second_product(3, groups[3], res_b[:])
+        store(3 * P, P, res_b[:], nc.vector.tensor_copy, nc.scalar)

@@ -24,7 +24,6 @@ H_TILES = H // P
 BANKS = 8
 CHUNKS = ((0, 128), (128, 128), (256, 128), (384, 128))
 XS_COLS = 768
-LATE_W1 = 2 * PASSES * 2 * H
 
 
 def tile_moe_sdn_lin_silu_kernel(
@@ -34,7 +33,6 @@ def tile_moe_sdn_lin_silu_kernel(
     with ExitStack() as ctx:
         lists = ctx.enter_context(tc.tile_pool(name="lists", bufs=1))
         keep = ctx.enter_context(tc.tile_pool(name="keep", bufs=1))
-        late = ctx.enter_context(tc.tile_pool(name="late", bufs=1))
         psum = ctx.enter_context(tc.psum_pool(name="psum", bufs=1))
 
         used_banks = []
@@ -47,14 +45,12 @@ def tile_moe_sdn_lin_silu_kernel(
         offs_sb = lists.tile([P, SLOTS // 16], U16, name="offs_sb")
         pos_sb = [lists.tile([P, T // 16], U16, name=f"pos_sb{r}") for r in range(2)]
 
-        xs_win = late.tile([P, XS_COLS], U8, name="xs_win", align_bytes=64, offset=LATE_W1 - 64)
+        xs_win = keep.tile([P, XS_COLS], U8, name="xs_win", align_bytes=64)
         w1s = keep.tile([P, E * PASSES, H], U8, name="w1s", align_bytes=64)
         w2s = keep.tile([P, N], U8, name="w2s", align_bytes=64)
         planes = [keep.tile([P, SLOTS], U8, name=f"plane{s}", align_bytes=64) for s in (1, 2)]
-        zero = keep.tile([P, 8], F32, name="zero")
         ident = keep.tile([P, P], F32, name="ident")
         nc.gpsimd.memset(xs_win[:].bitcast(I32), 0)
-        nc.gpsimd.memset(zero[:], 0.0)
         nc.vector.memset(w1s[:].rearrange("p a n -> p (a n)").bitcast(I32), 0)
         nc.vector.memset(ident[:], 0.0)
         nc.gpsimd.memset(planes[0][96:P, :].bitcast(I32), 0)
@@ -74,20 +70,22 @@ def tile_moe_sdn_lin_silu_kernel(
             )
         nc.sync.dma_start(xs_win[8:24, 0:T].bitcast(I32), x_scales[2].bitcast(I32))
         nc.sync.dma_start(xw[:], x_words.rearrange("s p t d -> p s (t d)").bitcast(I32))
-        w1_rows = w1_words.rearrange("e s p b -> p (e s) b").bitcast(I32)
-        w1w = []
+        w1_rows = w1_words.rearrange("e s p (g b) -> g p (e s) b", g=2).bitcast(I32)
+        w1w = {}
 
-        def load_experts(queue, words, first):
-            count = words.shape[1] // PASSES
-            queue.dma_start(words[:].bitcast(I32), w1_rows[:, first * PASSES : (first + count) * PASSES, :])
-            w1w.extend(words[:, j * PASSES : (j + 1) * PASSES, :] for j in range(count))
+        def load_weights(half, first, count):
+            words = keep.tile([P, count * PASSES, H], U8, name=f"w1w{half}_{first}", align_bytes=64)
+            nc.sync.dma_start(
+                words[:].bitcast(I32), w1_rows[half][:, first * PASSES : (first + count) * PASSES, :]
+            )
+            for j in range(count):
+                w1w[first + j, half] = words[:, j * PASSES : (j + 1) * PASSES, :]
 
-        load_experts(nc.sync, keep.tile([P, PASSES, 2 * H], U8, name="w1w0", align_bytes=64), 0)
+        load_weights(0, 0, 1)
         w1s_rows = w1_scales.rearrange("e s (q r) n -> r q (e s) n", r=4)
         for r in range(4):
             queue = nc.scalar if r < 2 else nc.sync
             queue.dma_start(w1s[r:P:32, :, :].bitcast(I32), w1s_rows[r].bitcast(I32))
-        nc.scalar.activation(h[0][:, 0:1], zero[:, 0:1], SILU)
 
         gs = keep.tile([P, SLOTS], U8, name="gs", align_bytes=64)
         gw = [
@@ -109,12 +107,12 @@ def tile_moe_sdn_lin_silu_kernel(
         nc.sync.dma_start(planes[0][0:112, :].bitcast(I32), gs[4:116, :].bitcast(I32))
         for r in range(4):
             nc.scalar.dma_start(planes[1][r:P:32, :].bitcast(I32), gs[8 + r : 24 : 4, :].bitcast(I32))
-        load_experts(nc.sync, keep.tile([P, PASSES, 2 * H], U8, name="w1w1", align_bytes=64), 1)
-        load_experts(nc.sync, late.tile([P, 2 * PASSES, 2 * H], U8, name="w1w2", align_bytes=64, offset=0), 2)
-        gate_sb = late.tile([P, 2, T], F32, name="gate_sb", align_bytes=64, offset=LATE_W1)
-        nc.sync.dma_start(gate_sb[:], gate.rearrange("r p t -> p r t"))
+        load_weights(0, 1, E - 1)
         nc.sync.dma_start(pos_sb[0][:], pos1)
         nc.sync.dma_start(pos_sb[1][:], pos2)
+        gate_sb = keep.tile([P, 2, T], F32, name="gate_sb", align_bytes=64)
+        nc.sync.dma_start(gate_sb[:], gate.rearrange("r p t -> p r t"))
+        load_weights(1, 0, E)
         w2w = keep.tile([P, 2 * N], U8, name="w2w", align_bytes=64)
         nc.sync.dma_start(w2w[:].bitcast(I32), w2_words[0].bitcast(I32))
         w2s_rows = w2_scales[0].rearrange("(q r) n -> r q n", r=4)
@@ -133,7 +131,7 @@ def tile_moe_sdn_lin_silu_kernel(
             cols = slice(e * C + half * P, e * C + (half + 1) * P)
             nc.tensor.matmul_mx(
                 out=acc,
-                lhsT=w1w[e][:, s, 2 * P * t : 2 * P * (t + 1)].bitcast(FP4X4),
+                lhsT=w1w[e, t // 2][:, s, 2 * P * (t % 2) : 2 * P * (t % 2 + 1)].bitcast(FP4X4),
                 lhsT_scale=w1s[:, e * PASSES + s, P * t : P * (t + 1)],
                 rhs=gw[e][s][:, half * P : (half + 1) * P].bitcast(FP8X4),
                 rhs_scale=gs[:, cols] if s == 0 else planes[s - 1][:, cols],

@@ -53,9 +53,9 @@ def tile_moe_sdn_lin_silu_kernel(
         nc.gpsimd.memset(xs_win[:].bitcast(I32), 0)
         nc.vector.memset(w1s[:].rearrange("p a n -> p (a n)").bitcast(I32), 0)
         nc.vector.memset(ident[:], 0.0)
-        nc.gpsimd.memset(planes[0][96:P, :].bitcast(I32), 0)
-        nc.gpsimd.memset(planes[1][:].bitcast(I32), 0)
-        nc.gpsimd.memset(w2s[:].bitcast(I32), 0)
+        nc.vector.memset(planes[0][96:P, :].bitcast(I32), 0)
+        nc.vector.memset(planes[1][:].bitcast(I32), 0)
+        nc.vector.memset(w2s[:].bitcast(I32), 0)
         make_identity(nc, ident[:], nomemset=True)
 
         xw = keep.tile([P, PASSES, T], I32, name="xw", align_bytes=64)
@@ -88,8 +88,14 @@ def tile_moe_sdn_lin_silu_kernel(
             queue.dma_start(w1s[r:P:32, :, :].bitcast(I32), w1s_rows[r].bitcast(I32))
 
         gs = keep.tile([P, SLOTS], U8, name="gs", align_bytes=64)
+        gw_pair = keep.tile([P, 2 * C], U32, name="gw_pair", align_bytes=64)
         gw = [
-            [keep.tile([P, C], U32, name=f"gw{e}_{s}", align_bytes=64) for s in range(PASSES)]
+            [
+                gw_pair[:, e * C : (e + 1) * C]
+                if e < 2 and s == 0
+                else keep.tile([P, C], U32, name=f"gw{e}_{s}", align_bytes=64)[:]
+                for s in range(PASSES)
+            ]
             for e in range(E)
         ]
 
@@ -157,9 +163,7 @@ def tile_moe_sdn_lin_silu_kernel(
             nc.scalar.activation(h[t][:, e * C : (e + 1) * C], acc[:], SILU)
 
 
-        c_tok = [
-            keep.tile([P, ntok // P, 2, P, 2], BF16, name=f"c_tok{tok0}") for tok0, ntok in CHUNKS
-        ]
+        c_tok = keep.tile([P, T // P * H], BF16, name="c_tok")
 
         def combine(chunks, t):
             tok0 = CHUNKS[chunks[0]][0]
@@ -185,16 +189,28 @@ def tile_moe_sdn_lin_silu_kernel(
                         stop=(r == 1),
                         is_transpose=True,
                     )
-            for j in chunks:
-                a, n = CHUNKS[j][0] - tok0, CHUNKS[j][1]
-                nc.scalar.copy(
-                    c_tok[j][:, :, :, 32 * t : 32 * (t + 1), :],
-                    sums[:, a : a + n].rearrange("k (g p u e) -> k g u p e", p=32, u=2, e=2),
-                )
+            nc.scalar.copy(
+                c_tok[:, chunks[0] * H : (chunks[-1] + 1) * H].rearrange(
+                    "k (g u p e) -> k g u p e", u=2, p=P, e=2
+                )[:, :, :, 32 * t : 32 * (t + 1), :],
+                sums[:].rearrange("k (g p u e) -> k g u p e", p=32, u=2, e=2),
+            )
+
+        def keep_clock_up(back):
+            unread = psum.tile([P, 2 * C], F32, name="unread", tag=used_banks[-back])
+            nc.tensor.matmul_mx(
+                out=unread[:],
+                lhsT=w1w[0, 0][:, 0, 0 : 2 * P].bitcast(FP4X4),
+                lhsT_scale=w1s[:, 0, 0:P],
+                rhs=gw_pair[:].bitcast(FP8X4),
+                rhs_scale=gs[:, 0 : 2 * C],
+                start=True,
+                stop=True,
+            )
 
         def turn_back(j, copy):
             tiles = CHUNKS[j][1] // P
-            words = c_tok[j][:].rearrange("k g u p e -> k (g u p e)").bitcast(F32)
+            words = c_tok[:, j * H : (j + 1) * H].bitcast(F32)
             turned = next_bank([P, tiles, 2, P])
             for g in range(tiles):
                 for u in range(2):
@@ -239,19 +255,25 @@ def tile_moe_sdn_lin_silu_kernel(
             for e in range(E):
                 hidden_in_one_bank(e, t)
         combine((0, 1, 2, 3), 0)
+        keep_clock_up(2)
         combine((0, 1, 2, 3), 1)
+        keep_clock_up(2)
         combine((0, 1, 2), 2)
+        keep_clock_up(2)
         for j in range(3):
             combine((j,), 3)
         groups = [turn_back(0, nc.scalar.copy)]
+        keep_clock_up(4)
         combine((3,), 2)
-        groups.append(turn_back(1, nc.scalar.copy))
+        groups.append(turn_back(1, nc.vector.tensor_copy))
         combine((3,), 3)
         groups.append(turn_back(2, nc.vector.tensor_copy))
+        keep_clock_up(4)
         res_a = next_bank([P, 3 * P])
         for j in range(2):
             second_product(j, groups[j], res_a[:, j * P : (j + 1) * P])
-        groups.append(turn_back(3, nc.vector.tensor_copy))
+        groups.append(turn_back(3, nc.scalar.copy))
+        keep_clock_up(4)
         second_product(2, groups[2], res_a[:, 2 * P : 3 * P])
         store(0, 3 * P, res_a[:], nc.scalar.copy, nc.sync)
         res_b = next_bank([P, P])

@@ -35,10 +35,11 @@ def tile_moe_sdn_lin_silu_kernel(
         keep = ctx.enter_context(tc.tile_pool(name="keep", bufs=1))
         psum = ctx.enter_context(tc.psum_pool(name="psum", bufs=1))
 
-        used_banks = []
+        used_banks = [f"bank{b}" for b in range(BANKS)]
 
-        def next_bank(shape):
-            tag = f"bank{len(used_banks) % BANKS}"
+        def next_bank(shape, back=BANKS):
+            tag = used_banks[-back]
+            used_banks.remove(tag)
             used_banks.append(tag)
             return psum.tile(shape, F32, name="bank", tag=tag)
 
@@ -165,7 +166,7 @@ def tile_moe_sdn_lin_silu_kernel(
 
         c_tok = keep.tile([P, T // P * H], BF16, name="c_tok")
 
-        def combine(chunks, t):
+        def combine(chunks, t, back=BANKS):
             tok0 = CHUNKS[chunks[0]][0]
             ntok = sum(CHUNKS[j][1] for j in chunks)
             prods = []
@@ -178,7 +179,7 @@ def tile_moe_sdn_lin_silu_kernel(
                     MULT,
                 )
                 prods.append(prod)
-            sums = next_bank([P, ntok])
+            sums = next_bank([P, ntok], back)
             for a in range(0, ntok, P):
                 for r in range(2):
                     nc.tensor.matmul(
@@ -198,15 +199,16 @@ def tile_moe_sdn_lin_silu_kernel(
 
         def keep_clock_up(back):
             unread = psum.tile([P, 2 * C], F32, name="unread", tag=used_banks[-back])
-            nc.tensor.matmul_mx(
-                out=unread[:],
-                lhsT=w1w[0, 0][:, 0, 0 : 2 * P].bitcast(FP4X4),
-                lhsT_scale=w1s[:, 0, 0:P],
-                rhs=gw_pair[:].bitcast(FP8X4),
-                rhs_scale=gs[:, 0 : 2 * C],
-                start=True,
-                stop=True,
-            )
+            for repeat in range(2):
+                nc.tensor.matmul_mx(
+                    out=unread[:],
+                    lhsT=w1w[0, 0][:, 0, 0 : 2 * P].bitcast(FP4X4),
+                    lhsT_scale=w1s[:, 0, 0:P],
+                    rhs=gw_pair[:].bitcast(FP8X4),
+                    rhs_scale=gs[:, 0 : 2 * C],
+                    start=True,
+                    stop=True,
+                )
 
         def turn_back(j, copy):
             tiles = CHUNKS[j][1] // P
@@ -251,31 +253,29 @@ def tile_moe_sdn_lin_silu_kernel(
         hidden_in_own_banks([(3, 0)])
         for e in range(2, E):
             hidden_in_one_bank(e, 1)
-        for t in range(2, H_TILES):
-            for e in range(E):
-                hidden_in_one_bank(e, t)
-        combine((0, 1, 2, 3), 0)
-        keep_clock_up(2)
+        for e in range(E):
+            hidden_in_one_bank(e, 2)
+        combine((0, 1, 2, 3), 0, back=2)
+        for e in range(E):
+            hidden_in_one_bank(e, 3)
         combine((0, 1, 2, 3), 1)
         keep_clock_up(2)
         combine((0, 1, 2), 2)
-        keep_clock_up(2)
-        for j in range(3):
+        for j in range(2):
             combine((j,), 3)
-        groups = [turn_back(0, nc.scalar.copy)]
         keep_clock_up(4)
+        combine((2,), 3)
+        groups = [turn_back(0, nc.scalar.copy)]
         combine((3,), 2)
         groups.append(turn_back(1, nc.vector.tensor_copy))
         combine((3,), 3)
         groups.append(turn_back(2, nc.vector.tensor_copy))
-        keep_clock_up(4)
-        res_a = next_bank([P, 3 * P])
+        res_a = next_bank([P, 2 * P])
         for j in range(2):
             second_product(j, groups[j], res_a[:, j * P : (j + 1) * P])
         groups.append(turn_back(3, nc.scalar.copy))
-        keep_clock_up(4)
-        second_product(2, groups[2], res_a[:, 2 * P : 3 * P])
-        store(0, 3 * P, res_a[:], nc.scalar.copy, nc.sync)
-        res_b = next_bank([P, P])
-        second_product(3, groups[3], res_b[:])
-        store(3 * P, P, res_b[:], nc.vector.tensor_copy, nc.scalar)
+        store(0, 2 * P, res_a[:], nc.scalar.copy, nc.sync)
+        for j, copy, queue in ((2, nc.scalar.copy, nc.sync), (3, nc.vector.tensor_copy, nc.scalar)):
+            res_b = next_bank([P, P])
+            second_product(j, groups[j], res_b[:])
+            store(j * P, P, res_b[:], copy, queue)

@@ -119,7 +119,8 @@ def tile_moe_sdn_lin_silu_kernel(
         nc.sync.dma_start(pos_sb[1][:], pos2)
         gate_sb = keep.tile([P, 2, T], F32, name="gate_sb", align_bytes=64)
         nc.sync.dma_start(gate_sb[:], gate.rearrange("r p t -> p r t"))
-        load_weights(1, 0, E)
+        load_weights(1, 0, 2)
+        load_weights(1, 2, 2)
         w2w = keep.tile([P, 2 * N], U8, name="w2w", align_bytes=64)
         nc.sync.dma_start(w2w[:].bitcast(I32), w2_words[0].bitcast(I32))
         w2s_rows = w2_scales[0].rearrange("(q r) n -> r q n", r=4)

@@ -135,7 +135,7 @@ def tile_moe_sdn_lin_silu_kernel(
                 else:
                     gather_words(e, s)
 
-        def first_pass(acc, e, t, half, s):
+        def first_pass(acc, e, t, half, s, order=(0, 1, 2)):
             cols = slice(e * C + half * P, e * C + (half + 1) * P)
             nc.tensor.matmul_mx(
                 out=acc,
@@ -143,16 +143,16 @@ def tile_moe_sdn_lin_silu_kernel(
                 lhsT_scale=w1s[:, e * PASSES + s, P * t : P * (t + 1)],
                 rhs=gw[e][s][:, half * P : (half + 1) * P].bitcast(FP8X4),
                 rhs_scale=gs[:, cols] if s == 0 else planes[s - 1][:, cols],
-                start=(s == 0),
-                stop=(s == PASSES - 1),
+                start=(s == order[0]),
+                stop=(s == order[-1]),
             )
 
-        def hidden_in_own_banks(units):
+        def hidden_in_own_banks(units, order):
             groups = [(e, t, half) for e, t in units for half in range(2)]
             accs = [next_bank([P, P]) for group in groups]
-            for s in range(PASSES):
+            for s in order:
                 for acc, group in zip(accs, groups):
-                    first_pass(acc[:], *group, s)
+                    first_pass(acc[:], *group, s, order)
             for acc, (e, t, half) in zip(accs, groups):
                 col = e * C + half * P
                 nc.scalar.activation(h[t][:, col : col + P], acc[:], SILU)
@@ -247,11 +247,11 @@ def tile_moe_sdn_lin_silu_kernel(
             copy(result[:], res)
             queue.dma_start(out[:, tok0 : tok0 + ntok], result[:])
 
-        hidden_in_own_banks([(0, 0), (0, 1)])
+        hidden_in_own_banks([(0, 0), (0, 1)], (0, 2, 1))
         for t in range(2):
             hidden_in_one_bank(1, t)
         hidden_in_one_bank(2, 0)
-        hidden_in_own_banks([(3, 0)])
+        hidden_in_own_banks([(3, 0)], (0, 1, 2))
         for e in range(2, E):
             hidden_in_one_bank(e, 1)
         for e in range(E):
@@ -260,21 +260,19 @@ def tile_moe_sdn_lin_silu_kernel(
         for e in range(E):
             hidden_in_one_bank(e, 3)
         combine((0, 1, 2, 3), 1)
-        keep_clock_up(2)
-        combine((0, 1, 2), 2)
+        keep_clock_up(3)
+        combine((0, 1, 2, 3), 2)
         for j in range(2):
             combine((j,), 3)
-        keep_clock_up(4)
-        combine((2,), 3)
         groups = [turn_back(0, nc.scalar.copy)]
-        combine((3,), 2)
+        combine((2,), 3, back=3)
         groups.append(turn_back(1, nc.vector.tensor_copy))
-        combine((3,), 3)
+        combine((3,), 3, back=4)
         groups.append(turn_back(2, nc.vector.tensor_copy))
-        res_a = next_bank([P, 2 * P])
+        groups.append(turn_back(3, nc.scalar.copy))
+        res_a = next_bank([P, 2 * P], 3)
         for j in range(2):
             second_product(j, groups[j], res_a[:, j * P : (j + 1) * P])
-        groups.append(turn_back(3, nc.scalar.copy))
         store(0, 2 * P, res_a[:], nc.scalar.copy, nc.sync)
         for j, copy, queue in ((2, nc.scalar.copy, nc.sync), (3, nc.vector.tensor_copy, nc.scalar)):
             res_b = next_bank([P, P])

@@ -15,6 +15,8 @@ U8 = mybir.dt.uint8
 FP8X4 = mybir.dt.float8_e4m3fn_x4
 FP4X4 = mybir.dt.float4_e2m1fn_x4
 MULT = mybir.AluOpType.mult
+ADD = mybir.AluOpType.add
+COPY = mybir.ActivationFunctionType.Copy
 SILU = mybir.ActivationFunctionType.Silu
 
 P = 128
@@ -22,8 +24,8 @@ PASSES = K // 512
 SLOTS = E * C
 H_TILES = H // P
 BANKS = 8
-CHUNKS = ((0, 128), (128, 128), (256, 128), (384, 128))
 XS_COLS = 768
+GATED_TOKENS = 3 * P
 
 
 def tile_moe_sdn_lin_silu_kernel(
@@ -47,16 +49,19 @@ def tile_moe_sdn_lin_silu_kernel(
         pos_sb = [lists.tile([P, T // 16], U16, name=f"pos_sb{r}") for r in range(2)]
 
         xs_win = keep.tile([P, XS_COLS], U8, name="xs_win", align_bytes=64)
-        w1s = keep.tile([P, E * PASSES, H], U8, name="w1s", align_bytes=64)
+        w1s = [keep.tile([P, 2 * PASSES, H], U8, name=f"w1s{a}", align_bytes=64) for a in range(2)]
         w2s = keep.tile([P, N], U8, name="w2s", align_bytes=64)
         planes = [keep.tile([P, SLOTS], U8, name=f"plane{s}", align_bytes=64) for s in (1, 2)]
         ident = keep.tile([P, P], F32, name="ident")
+        gate_rows = keep.tile([P, P], F32, name="gate_rows")
         nc.gpsimd.memset(xs_win[:].bitcast(I32), 0)
-        nc.vector.memset(w1s[:].rearrange("p a n -> p (a n)").bitcast(I32), 0)
+        for a in range(2):
+            nc.vector.memset(w1s[a][:].rearrange("p a n -> p (a n)").bitcast(I32), 0)
         nc.vector.memset(ident[:], 0.0)
         nc.vector.memset(planes[0][96:P, :].bitcast(I32), 0)
         nc.vector.memset(planes[1][:].bitcast(I32), 0)
         nc.vector.memset(w2s[:].bitcast(I32), 0)
+        nc.vector.memset(gate_rows[:], 0.0)
         make_identity(nc, ident[:], nomemset=True)
 
         xw = keep.tile([P, PASSES, T], I32, name="xw", align_bytes=64)
@@ -71,32 +76,24 @@ def tile_moe_sdn_lin_silu_kernel(
             )
         nc.sync.dma_start(xs_win[8:24, 0:T].bitcast(I32), x_scales[2].bitcast(I32))
         nc.sync.dma_start(xw[:], x_words.rearrange("s p t d -> p s (t d)").bitcast(I32))
-        w1_rows = w1_words.rearrange("e s p (g b) -> g p (e s) b", g=2).bitcast(I32)
         w1w = {}
 
-        def load_weights(half, first, count):
-            words = keep.tile([P, count * PASSES, H], U8, name=f"w1w{half}_{first}", align_bytes=64)
-            nc.sync.dma_start(
-                words[:].bitcast(I32), w1_rows[half][:, first * PASSES : (first + count) * PASSES, :]
-            )
-            for j in range(count):
-                w1w[first + j, half] = words[:, j * PASSES : (j + 1) * PASSES, :]
+        def load_weights(e):
+            w1w[e] = keep.tile([P, PASSES, 2 * H], U8, name=f"w1w{e}", align_bytes=64)
+            nc.sync.dma_start(w1w[e][:].bitcast(I32), w1_words[e].rearrange("s p b -> p s b").bitcast(I32))
 
-        load_weights(0, 0, 1)
-        w1s_rows = w1_scales.rearrange("e s (q r) n -> r q (e s) n", r=4)
-        for r in range(4):
-            queue = nc.scalar if r < 2 else nc.sync
-            queue.dma_start(w1s[r:P:32, :, :].bitcast(I32), w1s_rows[r].bitcast(I32))
+        w1s_rows = w1_scales.rearrange("(a e) s (q r) n -> a r q (e s) n", a=2, r=4)
+
+        def load_weight_scales(a, queues):
+            for r in range(4):
+                queues[r].dma_start(w1s[a][r:P:32, :, :].bitcast(I32), w1s_rows[a][r].bitcast(I32))
+
+        load_weights(0)
+        load_weight_scales(0, (nc.scalar, nc.scalar, nc.sync, nc.sync))
 
         gs = keep.tile([P, SLOTS], U8, name="gs", align_bytes=64)
-        gw_pair = keep.tile([P, 2 * C], U32, name="gw_pair", align_bytes=64)
         gw = [
-            [
-                gw_pair[:, e * C : (e + 1) * C]
-                if e < 2 and s == 0
-                else keep.tile([P, C], U32, name=f"gw{e}_{s}", align_bytes=64)[:]
-                for s in range(PASSES)
-            ]
+            [keep.tile([P, C], U32, name=f"gw{e}_{s}", align_bytes=64) for s in range(PASSES)]
             for e in range(E)
         ]
 
@@ -114,13 +111,15 @@ def tile_moe_sdn_lin_silu_kernel(
         nc.sync.dma_start(planes[0][0:112, :].bitcast(I32), gs[4:116, :].bitcast(I32))
         for r in range(4):
             nc.scalar.dma_start(planes[1][r:P:32, :].bitcast(I32), gs[8 + r : 24 : 4, :].bitcast(I32))
-        load_weights(0, 1, E - 1)
+        load_weights(1)
+        load_weight_scales(1, (nc.sync,) * 4)
+        load_weights(2)
+        load_weights(3)
         nc.sync.dma_start(pos_sb[0][:], pos1)
         nc.sync.dma_start(pos_sb[1][:], pos2)
-        gate_sb = keep.tile([P, 2, T], F32, name="gate_sb", align_bytes=64)
-        nc.sync.dma_start(gate_sb[:], gate.rearrange("r p t -> p r t"))
-        load_weights(1, 0, 2)
-        load_weights(1, 2, 2)
+        gate_sb = keep.tile([P, 2, GATED_TOKENS], F32, name="gate_sb", align_bytes=64)
+        nc.sync.dma_start(gate_sb[:], gate[:, :, 0:GATED_TOKENS].rearrange("r p t -> p r t"))
+        nc.sync.dma_start(gate_rows[0:8, :], gate[:, 0, :].rearrange("r (j t) -> r j t", t=P))
         w2w = keep.tile([P, 2 * N], U8, name="w2w", align_bytes=64)
         nc.sync.dma_start(w2w[:].bitcast(I32), w2_words[0].bitcast(I32))
         w2s_rows = w2_scales[0].rearrange("(q r) n -> r q n", r=4)
@@ -135,105 +134,110 @@ def tile_moe_sdn_lin_silu_kernel(
                 else:
                     gather_words(e, s)
 
-        def first_pass(acc, e, t, half, s, order=(0, 1, 2)):
-            cols = slice(e * C + half * P, e * C + (half + 1) * P)
-            nc.tensor.matmul_mx(
-                out=acc,
-                lhsT=w1w[e, t // 2][:, s, 2 * P * (t % 2) : 2 * P * (t % 2 + 1)].bitcast(FP4X4),
-                lhsT_scale=w1s[:, e * PASSES + s, P * t : P * (t + 1)],
-                rhs=gw[e][s][:, half * P : (half + 1) * P].bitcast(FP8X4),
-                rhs_scale=gs[:, cols] if s == 0 else planes[s - 1][:, cols],
-                start=(s == order[0]),
-                stop=(s == order[-1]),
-            )
-
-        def hidden_in_own_banks(units, order):
-            groups = [(e, t, half) for e, t in units for half in range(2)]
-            accs = [next_bank([P, P]) for group in groups]
+        def hidden(e, groups, order=(0, 1, 2)):
+            accs = [next_bank([P, width]) for t, a, width in groups]
             for s in order:
-                for acc, group in zip(accs, groups):
-                    first_pass(acc[:], *group, s, order)
-            for acc, (e, t, half) in zip(accs, groups):
-                col = e * C + half * P
-                nc.scalar.activation(h[t][:, col : col + P], acc[:], SILU)
-
-        def hidden_in_one_bank(e, t):
-            acc = next_bank([P, C])
-            for half in range(2):
-                for s in range(PASSES):
-                    first_pass(acc[:, half * P : (half + 1) * P], e, t, half, s)
-            nc.scalar.activation(h[t][:, e * C : (e + 1) * C], acc[:], SILU)
-
+                for acc, (t, a, width) in zip(accs, groups):
+                    cols = slice(e * C + a, e * C + a + width)
+                    nc.tensor.matmul_mx(
+                        out=acc[:],
+                        lhsT=w1w[e][:, s, 2 * P * t : 2 * P * (t + 1)].bitcast(FP4X4),
+                        lhsT_scale=w1s[e // 2][:, (e % 2) * PASSES + s, P * t : P * (t + 1)],
+                        rhs=gw[e][s][:, a : a + width].bitcast(FP8X4),
+                        rhs_scale=gs[:, cols] if s == 0 else planes[s - 1][:, cols],
+                        start=(s == order[0]),
+                        stop=(s == order[-1]),
+                    )
+            for acc, (t, a, width) in zip(accs, groups):
+                nc.scalar.activation(h[t][:, e * C + a : e * C + a + width], acc[:], SILU)
 
         c_tok = keep.tile([P, T // P * H], BF16, name="c_tok")
+        fetched = {}
 
-        def combine(chunks, t, back=BANKS):
-            tok0 = CHUNKS[chunks[0]][0]
-            ntok = sum(CHUNKS[j][1] for j in chunks)
-            prods = []
+        def fetch(t, tok0, ntok, gated):
             for r in range(2):
-                prod = keep.tile([P, ntok], F32, name=f"prod{tok0}_{t}_{r}")
-                nc.vector.tensor_tensor(
-                    prod[:],
-                    h[t][:].indirect(pos_sb[r][:, tok0 // 16 : (tok0 + ntok) // 16]),
-                    gate_sb[:, r, tok0 : tok0 + ntok],
-                    MULT,
-                )
-                prods.append(prod)
-            sums = next_bank([P, ntok], back)
-            for a in range(0, ntok, P):
+                cols = keep.tile([P, ntok], F32, name=f"cols{tok0}_{t}_{r}")
+                window = h[t][:].indirect(pos_sb[r][:, tok0 // 16 : (tok0 + ntok) // 16])
+                if gated:
+                    nc.vector.tensor_tensor(cols[:], window, gate_sb[:, r, tok0 : tok0 + ntok], MULT)
+                else:
+                    nc.scalar.activation(cols[:], window, COPY)
+                for a in range(0, ntok, P):
+                    fetched[(tok0 + a) // P, t, r] = cols[:, a : a + P]
+
+        def turn_gated(bank, js, ts, t):
+            for g, j in enumerate(js):
+                a = (g * len(ts) + ts.index(t)) * P
                 for r in range(2):
                     nc.tensor.matmul(
-                        sums[:, a : a + P],
-                        prods[r][:, a : a + P],
+                        bank[:, a : a + P],
+                        fetched[j, t, r],
                         ident[:],
                         start=(r == 0),
                         stop=(r == 1),
                         is_transpose=True,
                     )
-            nc.scalar.copy(
-                c_tok[:, chunks[0] * H : (chunks[-1] + 1) * H].rearrange(
-                    "k (g u p e) -> k g u p e", u=2, p=P, e=2
-                )[:, :, :, 32 * t : 32 * (t + 1), :],
-                sums[:].rearrange("k (g p u e) -> k g u p e", p=32, u=2, e=2),
-            )
 
-        def keep_clock_up(back):
-            unread = psum.tile([P, 2 * C], F32, name="unread", tag=used_banks[-back])
-            for repeat in range(2):
-                nc.tensor.matmul_mx(
-                    out=unread[:],
-                    lhsT=w1w[0, 0][:, 0, 0 : 2 * P].bitcast(FP4X4),
-                    lhsT_scale=w1s[:, 0, 0:P],
-                    rhs=gw_pair[:].bitcast(FP8X4),
-                    rhs_scale=gs[:, 0 : 2 * C],
-                    start=True,
-                    stop=True,
+        def round_gated(bank, js, ts, parted):
+            rows = c_tok[:, js[0] * H : (js[-1] + 1) * H]
+            if parted:
+                nc.scalar.copy(
+                    rows.rearrange("k (g u p e) -> k g u p e", u=2, p=P, e=2)[
+                        :, :, :, 32 * ts[0] : 32 * (ts[-1] + 1), :
+                    ],
+                    bank[:].rearrange("k (g p u e) -> k g u p e", g=len(js), u=2, e=2),
+                )
+            else:
+                nc.scalar.copy(
+                    rows.rearrange("k (g i) -> k g i", i=H)[:, :, P * ts[0] : P * (ts[-1] + 1)],
+                    bank[:].rearrange("k (g i) -> k g i", g=len(js)),
                 )
 
-        def turn_back(j, copy):
-            tiles = CHUNKS[j][1] // P
-            words = c_tok[:, j * H : (j + 1) * H].bitcast(F32)
+        def turn_plain(bank, j, ts, t):
+            for r in range(2):
+                a = (r * len(ts) + ts.index(t)) * P
+                nc.tensor.transpose(bank[:, a : a + P], fetched[j, t, r], ident[:])
+
+        def gate_plain(bank, j, ts):
+            width = len(ts) * P
+            first = keep.tile([P, width], F32, name=f"first{j}_{ts[0]}")
+            nc.scalar.activation(first[:], bank[:, 0:width], COPY, scale=gate_cols[:, j : j + 1])
+            nc.vector.scalar_tensor_tensor(
+                c_tok[:, j * H + ts[0] * P : j * H + ts[0] * P + width],
+                bank[:, width : 2 * width],
+                gate_cols[:, 4 + j : 5 + j],
+                first[:],
+                MULT,
+                ADD,
+            )
+
+        def turn_back(js, parted, copy):
+            tiles = len(js)
+            words = c_tok[:, js[0] * H : (js[-1] + 1) * H].bitcast(F32)
             turned = next_bank([P, tiles, 2, P])
             for g in range(tiles):
                 for u in range(2):
-                    a = (2 * g + u) * P
-                    nc.tensor.transpose(turned[:, g, u, :], words[:, a : a + P], ident[:])
-            group = keep.tile([P, tiles, P, 2], F32, name=f"group{j}", align_bytes=64)
+                    if parted:
+                        half = words[:, (2 * g + u) * P : (2 * g + u + 1) * P]
+                    else:
+                        half = words[:, 2 * g * P + u : 2 * (g + 1) * P : 2]
+                    nc.tensor.transpose(turned[:, g, u, :], half, ident[:])
+            group = keep.tile([P, tiles, P, 2], F32, name=f"group{js[0]}", align_bytes=64)
             copy(group[:], turned[:].rearrange("p g u k -> p g k u"))
             return group
 
-        def second_product(j, group, res):
-            ntok = CHUNKS[j][1]
-            codes = keep.tile([P, ntok], U32, name=f"codes{j}", align_bytes=64)
-            scales = keep.tile([P, ntok], U8, name=f"scales{j}", align_bytes=64)
+        def second_product(js, group, copy, queue):
+            ntok = len(js) * P
+            codes = keep.tile([P, ntok], U32, name=f"codes{js[0]}", align_bytes=64)
+            scales = keep.tile([P, ntok], U8, name=f"scales{js[0]}", align_bytes=64)
             nc.vector.quantize_mx(
                 out=codes[:].bitcast(FP8X4),
                 scales=scales[:],
                 in_=group[:].rearrange("p g k u -> p (g k u)").bitcast(BF16),
             )
+            res = next_bank([P, ntok])
             nc.tensor.matmul_mx(
-                out=res,
+                out=res[:],
                 lhsT=w2w[:].bitcast(FP4X4),
                 lhsT_scale=w2s[:],
                 rhs=codes[:].bitcast(FP8X4),
@@ -241,40 +245,52 @@ def tile_moe_sdn_lin_silu_kernel(
                 start=True,
                 stop=True,
             )
+            result = keep.tile([P, ntok], F32, name=f"result{js[0]}")
+            copy(result[:], res[:])
+            queue.dma_start(out[:, js[0] * P : js[0] * P + ntok], result[:])
 
-        def store(tok0, ntok, res, copy, queue):
-            result = keep.tile([P, ntok], F32, name=f"result{tok0}")
-            copy(result[:], res)
-            queue.dma_start(out[:, tok0 : tok0 + ntok], result[:])
+        whole = [(t, 0, C) for t in range(H_TILES)]
+        hidden(0, whole, (0, 2, 1))
+        hidden(1, whole)
+        hidden(2, whole)
+        hidden(3, [(0, 0, P), (0, P, P)] + whole[1:])
 
-        hidden_in_own_banks([(0, 0), (0, 1)], (0, 2, 1))
-        for t in range(2):
-            hidden_in_one_bank(1, t)
-        hidden_in_one_bank(2, 0)
-        hidden_in_own_banks([(3, 0)], (0, 1, 2))
-        for e in range(2, E):
-            hidden_in_one_bank(e, 1)
-        for e in range(E):
-            hidden_in_one_bank(e, 2)
-        combine((0, 1, 2, 3), 0, back=2)
-        for e in range(E):
-            hidden_in_one_bank(e, 3)
-        combine((0, 1, 2, 3), 1)
-        keep_clock_up(3)
-        combine((0, 1, 2, 3), 2)
-        for j in range(2):
-            combine((j,), 3)
-        groups = [turn_back(0, nc.scalar.copy)]
-        combine((2,), 3, back=3)
-        groups.append(turn_back(1, nc.vector.tensor_copy))
-        combine((3,), 3, back=4)
-        groups.append(turn_back(2, nc.vector.tensor_copy))
-        groups.append(turn_back(3, nc.scalar.copy))
-        res_a = next_bank([P, 2 * P], 3)
-        for j in range(2):
-            second_product(j, groups[j], res_a[:, j * P : (j + 1) * P])
-        store(0, 2 * P, res_a[:], nc.scalar.copy, nc.sync)
-        for j, copy, queue in ((2, nc.scalar.copy, nc.sync), (3, nc.vector.tensor_copy, nc.scalar)):
-            res_b = next_bank([P, P])
-            second_product(j, groups[j], res_b[:])
-            store(j * P, P, res_b[:], copy, queue)
+        gate_bank = next_bank([P, P])
+        nc.tensor.transpose(gate_bank[:], gate_rows[:], ident[:])
+        gate_cols = keep.tile([P, 8], F32, name="gate_cols")
+        nc.scalar.copy(gate_cols[:], gate_bank[:, 0:8])
+
+        low, high = (0, 1), (2, 3)
+        gated_low = next_bank([P, 4 * P])
+        plain_low = [next_bank([P, 4 * P]) for j in high]
+        for t in low:
+            fetch(t, 0, 2 * P, True)
+            fetch(t, 2 * P, 2 * P, False)
+            turn_gated(gated_low, low, low, t)
+            for j in high:
+                turn_plain(plain_low[j - 2], j, low, t)
+        round_gated(gated_low, low, low, True)
+        gated_high = next_bank([P, 4 * P])
+        plain_high = next_bank([P, 4 * P])
+        for t in high:
+            fetch(t, 0, 2 * P, True)
+            turn_gated(gated_high, low, high, t)
+        for j in high:
+            gate_plain(plain_low[j - 2], j, low)
+        for t in high:
+            fetch(t, 3 * P, P, False)
+            turn_plain(plain_high, 3, high, t)
+        round_gated(gated_high, low, high, True)
+        gated_last = next_bank([P, 2 * P])
+        for t in high:
+            fetch(t, 2 * P, P, True)
+        gate_plain(plain_high, 3, high)
+        group_low = turn_back(low, True, nc.scalar.copy)
+        for t in high:
+            turn_gated(gated_last, (2,), high, t)
+        group_3 = turn_back((3,), False, nc.vector.tensor_copy)
+        round_gated(gated_last, (2,), high, False)
+        second_product(low, group_low, nc.scalar.copy, nc.sync)
+        group_2 = turn_back((2,), False, nc.vector.tensor_copy)
+        second_product((3,), group_3, nc.scalar.copy, nc.sync)
+        second_product((2,), group_2, nc.vector.tensor_copy, nc.scalar)

@@ -78,9 +78,26 @@ def tile_moe_sdn_lin_silu_kernel(
         nc.sync.dma_start(xw[:], x_words.rearrange("s p t d -> p s (t d)").bitcast(I32))
         w1w = {}
 
-        def load_weights(e):
-            w1w[e] = keep.tile([P, PASSES, 2 * H], U8, name=f"w1w{e}", align_bytes=64)
-            nc.sync.dma_start(w1w[e][:].bitcast(I32), w1_words[e].rearrange("s p b -> p s b").bitcast(I32))
+        w1_rows = w1_words.rearrange("e s p b -> p (e s) b").bitcast(I32)
+
+        def load_weights(experts, tiles):
+            words = keep.tile(
+                [P, len(experts) * PASSES, len(tiles) * 2 * P],
+                U8,
+                name=f"w1w{experts[0]}_{tiles[0]}",
+                align_bytes=64,
+            )
+            nc.sync.dma_start(
+                words[:].bitcast(I32),
+                w1_rows[
+                    :,
+                    experts[0] * PASSES : (experts[-1] + 1) * PASSES,
+                    tiles[0] * P // 2 : (tiles[-1] + 1) * P // 2,
+                ],
+            )
+            for a, e in enumerate(experts):
+                for b, t in enumerate(tiles):
+                    w1w[e, t] = words[:, a * PASSES : (a + 1) * PASSES, b * 2 * P : (b + 1) * 2 * P]
 
         w1s_rows = w1_scales.rearrange("(a e) s (q r) n -> a r q (e s) n", a=2, r=4)
 
@@ -88,7 +105,7 @@ def tile_moe_sdn_lin_silu_kernel(
             for r in range(4):
                 queues[r].dma_start(w1s[a][r:P:32, :, :].bitcast(I32), w1s_rows[a][r].bitcast(I32))
 
-        load_weights(0)
+        load_weights((0,), (0, 1, 2, 3))
         load_weight_scales(0, (nc.scalar, nc.scalar, nc.sync, nc.sync))
 
         gs = keep.tile([P, SLOTS], U8, name="gs", align_bytes=64)
@@ -111,12 +128,12 @@ def tile_moe_sdn_lin_silu_kernel(
         nc.sync.dma_start(planes[0][0:112, :].bitcast(I32), gs[4:116, :].bitcast(I32))
         for r in range(4):
             nc.scalar.dma_start(planes[1][r:P:32, :].bitcast(I32), gs[8 + r : 24 : 4, :].bitcast(I32))
-        load_weights(1)
+        load_weights((1,), (0, 1))
         load_weight_scales(1, (nc.sync,) * 4)
-        load_weights(2)
-        load_weights(3)
+        load_weights((2, 3), (0, 1))
         nc.sync.dma_start(pos_sb[0][:], pos1)
         nc.sync.dma_start(pos_sb[1][:], pos2)
+        load_weights((1, 2, 3), (2, 3))
         gate_sb = keep.tile([P, 2, GATED_TOKENS], F32, name="gate_sb", align_bytes=64)
         nc.sync.dma_start(gate_sb[:], gate[:, :, 0:GATED_TOKENS].rearrange("r p t -> p r t"))
         nc.sync.dma_start(gate_rows[0:8, :], gate[:, 0, :].rearrange("r (j t) -> r j t", t=P))
@@ -141,7 +158,7 @@ def tile_moe_sdn_lin_silu_kernel(
                     cols = slice(e * C + a, e * C + a + width)
                     nc.tensor.matmul_mx(
                         out=acc[:],
-                        lhsT=w1w[e][:, s, 2 * P * t : 2 * P * (t + 1)].bitcast(FP4X4),
+                        lhsT=w1w[e, t][:, s, :].bitcast(FP4X4),
                         lhsT_scale=w1s[e // 2][:, (e % 2) * PASSES + s, P * t : P * (t + 1)],
                         rhs=gw[e][s][:, a : a + width].bitcast(FP8X4),
                         rhs_scale=gs[:, cols] if s == 0 else planes[s - 1][:, cols],
@@ -249,48 +266,50 @@ def tile_moe_sdn_lin_silu_kernel(
             copy(result[:], res[:])
             queue.dma_start(out[:, js[0] * P : js[0] * P + ntok], result[:])
 
-        whole = [(t, 0, C) for t in range(H_TILES)]
-        hidden(0, whole, (0, 2, 1))
-        hidden(1, whole)
-        hidden(2, whole)
-        hidden(3, [(0, 0, P), (0, P, P)] + whole[1:])
-
+        low, high, gated = (0, 1), (2, 3), (0, 1, 2)
+        hidden(0, [(t, 0, C) for t in range(H_TILES)], (0, 2, 1))
+        for e in (1, 2):
+            hidden(e, [(t, 0, C) for t in low])
+        hidden(3, [(0, 0, P), (0, P, P), (1, 0, C)])
+        for e in range(1, E):
+            hidden(e, [(2, 0, C)])
+        fetch(0, 0, 3 * P, True)
+        fetch(0, 3 * P, P, False)
+        for e in range(1, E):
+            hidden(e, [(3, 0, C)])
         gate_bank = next_bank([P, P])
         nc.tensor.transpose(gate_bank[:], gate_rows[:], ident[:])
         gate_cols = keep.tile([P, 8], F32, name="gate_cols")
         nc.scalar.copy(gate_cols[:], gate_bank[:, 0:8])
 
-        low, high = (0, 1), (2, 3)
-        gated_low = next_bank([P, 4 * P])
-        plain_low = [next_bank([P, 4 * P]) for j in high]
+        def combine_gated(js, t):
+            bank = next_bank([P, len(js) * P])
+            turn_gated(bank, js, (t,), t)
+            round_gated(bank, js, (t,), True)
+
+        fetch(1, 0, 3 * P, True)
+        fetch(1, 3 * P, P, False)
+        combine_gated(gated, 0)
+        plain_low = next_bank([P, 4 * P])
         for t in low:
-            fetch(t, 0, 2 * P, True)
-            fetch(t, 2 * P, 2 * P, False)
-            turn_gated(gated_low, low, low, t)
-            for j in high:
-                turn_plain(plain_low[j - 2], j, low, t)
-        round_gated(gated_low, low, low, True)
-        gated_high = next_bank([P, 4 * P])
+            turn_plain(plain_low, 3, low, t)
+        fetch(2, 0, 3 * P, True)
+        gate_plain(plain_low, 3, low)
+        fetch(2, 3 * P, P, False)
+        combine_gated(gated, 1)
+        fetch(3, 3 * P, P, False)
+        fetch(3, 0, 2 * P, True)
+        combine_gated(gated, 2)
         plain_high = next_bank([P, 4 * P])
         for t in high:
-            fetch(t, 0, 2 * P, True)
-            turn_gated(gated_high, low, high, t)
-        for j in high:
-            gate_plain(plain_low[j - 2], j, low)
-        for t in high:
-            fetch(t, 3 * P, P, False)
             turn_plain(plain_high, 3, high, t)
-        round_gated(gated_high, low, high, True)
-        gated_last = next_bank([P, 2 * P])
-        for t in high:
-            fetch(t, 2 * P, P, True)
+        fetch(3, 2 * P, P, True)
         gate_plain(plain_high, 3, high)
-        group_low = turn_back(low, True, nc.scalar.copy)
-        for t in high:
-            turn_gated(gated_last, (2,), high, t)
-        group_3 = turn_back((3,), False, nc.vector.tensor_copy)
-        round_gated(gated_last, (2,), high, False)
+        combine_gated(low, 3)
+        combine_gated((2,), 3)
+        group_low = turn_back(low, True, nc.vector.tensor_copy)
+        group_3 = turn_back((3,), False, nc.scalar.copy)
+        group_2 = turn_back((2,), True, nc.scalar.copy)
         second_product(low, group_low, nc.scalar.copy, nc.sync)
-        group_2 = turn_back((2,), False, nc.vector.tensor_copy)
-        second_product((3,), group_3, nc.scalar.copy, nc.sync)
-        second_product((2,), group_2, nc.vector.tensor_copy, nc.scalar)
+        second_product((3,), group_3, nc.vector.tensor_copy, nc.sync)
+        second_product((2,), group_2, nc.scalar.copy, nc.scalar)

@@ -49,14 +49,13 @@ def tile_moe_sdn_lin_silu_kernel(
         pos_sb = [lists.tile([P, T // 16], U16, name=f"pos_sb{r}") for r in range(2)]
 
         xs_win = keep.tile([P, XS_COLS], U8, name="xs_win", align_bytes=64)
-        w1s = [keep.tile([P, 2 * PASSES, H], U8, name=f"w1s{a}", align_bytes=64) for a in range(2)]
+        w1s = keep.tile([P, E * PASSES, H], U8, name="w1s", align_bytes=64)
         w2s = keep.tile([P, N], U8, name="w2s", align_bytes=64)
         planes = [keep.tile([P, SLOTS], U8, name=f"plane{s}", align_bytes=64) for s in (1, 2)]
         ident = keep.tile([P, P], F32, name="ident")
         gate_rows = keep.tile([P, P], F32, name="gate_rows")
         nc.gpsimd.memset(xs_win[:].bitcast(I32), 0)
-        for a in range(2):
-            nc.vector.memset(w1s[a][:].rearrange("p a n -> p (a n)").bitcast(I32), 0)
+        nc.vector.memset(w1s[:].rearrange("p a n -> p (a n)").bitcast(I32), 0)
         nc.vector.memset(ident[:], 0.0)
         nc.vector.memset(planes[0][96:P, :].bitcast(I32), 0)
         nc.vector.memset(planes[1][:].bitcast(I32), 0)
@@ -99,14 +98,11 @@ def tile_moe_sdn_lin_silu_kernel(
                 for b, t in enumerate(tiles):
                     w1w[e, t] = words[:, a * PASSES : (a + 1) * PASSES, b * 2 * P : (b + 1) * 2 * P]
 
-        w1s_rows = w1_scales.rearrange("(a e) s (q r) n -> a r q (e s) n", a=2, r=4)
-
-        def load_weight_scales(a, queues):
-            for r in range(4):
-                queues[r].dma_start(w1s[a][r:P:32, :, :].bitcast(I32), w1s_rows[a][r].bitcast(I32))
-
-        load_weights((0,), (0, 1, 2, 3))
-        load_weight_scales(0, (nc.scalar, nc.scalar, nc.sync, nc.sync))
+        load_weights((0,), (0, 1))
+        w1s_rows = w1_scales.rearrange("e s (q r) n -> r q (e s) n", r=4)
+        for r in range(4):
+            queue = nc.scalar if r < 2 else nc.sync
+            queue.dma_start(w1s[r:P:32, :, :].bitcast(I32), w1s_rows[r].bitcast(I32))
 
         gs = keep.tile([P, SLOTS], U8, name="gs", align_bytes=64)
         gw = [
@@ -128,12 +124,11 @@ def tile_moe_sdn_lin_silu_kernel(
         nc.sync.dma_start(planes[0][0:112, :].bitcast(I32), gs[4:116, :].bitcast(I32))
         for r in range(4):
             nc.scalar.dma_start(planes[1][r:P:32, :].bitcast(I32), gs[8 + r : 24 : 4, :].bitcast(I32))
-        load_weights((1,), (0, 1))
-        load_weight_scales(1, (nc.sync,) * 4)
-        load_weights((2, 3), (0, 1))
+        load_weights((1, 2, 3), (0, 1))
+        load_weights((0, 1), (2, 3))
+        load_weights((2, 3), (2, 3))
         nc.sync.dma_start(pos_sb[0][:], pos1)
         nc.sync.dma_start(pos_sb[1][:], pos2)
-        load_weights((1, 2, 3), (2, 3))
         gate_sb = keep.tile([P, 2, GATED_TOKENS], F32, name="gate_sb", align_bytes=64)
         nc.sync.dma_start(gate_sb[:], gate[:, :, 0:GATED_TOKENS].rearrange("r p t -> p r t"))
         nc.sync.dma_start(gate_rows[0:8, :], gate[:, 0, :].rearrange("r (j t) -> r j t", t=P))
@@ -159,7 +154,7 @@ def tile_moe_sdn_lin_silu_kernel(
                     nc.tensor.matmul_mx(
                         out=acc[:],
                         lhsT=w1w[e, t][:, s, :].bitcast(FP4X4),
-                        lhsT_scale=w1s[e // 2][:, (e % 2) * PASSES + s, P * t : P * (t + 1)],
+                        lhsT_scale=w1s[:, e * PASSES + s, P * t : P * (t + 1)],
                         rhs=gw[e][s][:, a : a + width].bitcast(FP8X4),
                         rhs_scale=gs[:, cols] if s == 0 else planes[s - 1][:, cols],
                         start=(s == order[0]),
@@ -228,6 +223,23 @@ def tile_moe_sdn_lin_silu_kernel(
                 ADD,
             )
 
+        def gate_plain_parted(bank, j, t):
+            first = keep.tile([P, 2, 64], F32, name=f"first{j}_{t}")
+            sums = bank[:].rearrange("k (r p u e) -> k r u p e", r=2, u=2, e=2)
+            nc.scalar.activation(
+                first[:].rearrange("k u (p e) -> k u p e", e=2), sums[:, 0], COPY, scale=gate_cols[:, j : j + 1]
+            )
+            for u in range(2):
+                a = j * H + u * 2 * P + 64 * t
+                nc.vector.scalar_tensor_tensor(
+                    c_tok[:, a : a + 64].rearrange("k (p e) -> k p e", e=2),
+                    sums[:, 1, u],
+                    gate_cols[:, 4 + j : 5 + j],
+                    first[:, u, :].rearrange("k (p e) -> k p e", e=2),
+                    MULT,
+                    ADD,
+                )
+
         def turn_back(js, parted, copy):
             tiles = len(js)
             words = c_tok[:, js[0] * H : (js[-1] + 1) * H].bitcast(F32)
@@ -267,14 +279,15 @@ def tile_moe_sdn_lin_silu_kernel(
             queue.dma_start(out[:, js[0] * P : js[0] * P + ntok], result[:])
 
         low, high, gated = (0, 1), (2, 3), (0, 1, 2)
-        hidden(0, [(t, 0, C) for t in range(H_TILES)], (0, 2, 1))
-        for e in (1, 2):
-            hidden(e, [(t, 0, C) for t in low])
+        hidden(0, [(t, 0, C) for t in low], (0, 2, 1))
+        hidden(1, [(t, 0, C) for t in low])
+        hidden(0, [(t, 0, C) for t in high])
+        hidden(2, [(t, 0, C) for t in low])
         hidden(3, [(0, 0, P), (0, P, P), (1, 0, C)])
         for e in range(1, E):
             hidden(e, [(2, 0, C)])
-        fetch(0, 0, 3 * P, True)
-        fetch(0, 3 * P, P, False)
+        fetch(0, 0, 2 * P, True)
+        fetch(0, 2 * P, 2 * P, False)
         for e in range(1, E):
             hidden(e, [(3, 0, C)])
         gate_bank = next_bank([P, P])
@@ -289,11 +302,14 @@ def tile_moe_sdn_lin_silu_kernel(
 
         fetch(1, 0, 3 * P, True)
         fetch(1, 3 * P, P, False)
-        combine_gated(gated, 0)
+        combine_gated(low, 0)
+        plain_2 = next_bank([P, 2 * P])
+        turn_plain(plain_2, 2, (0,), 0)
         plain_low = next_bank([P, 4 * P])
         for t in low:
             turn_plain(plain_low, 3, low, t)
         fetch(2, 0, 3 * P, True)
+        gate_plain_parted(plain_2, 2, 0)
         gate_plain(plain_low, 3, low)
         fetch(2, 3 * P, P, False)
         combine_gated(gated, 1)

@@ -98,7 +98,7 @@ def tile_moe_sdn_lin_silu_kernel(
                 for b, t in enumerate(tiles):
                     w1w[e, t] = words[:, a * PASSES : (a + 1) * PASSES, b * 2 * P : (b + 1) * 2 * P]
 
-        load_weights((0,), (0, 1))
+        load_weights((0,), (0, 1, 2, 3))
         w1s_rows = w1_scales.rearrange("e s (q r) n -> r q (e s) n", r=4)
         for r in range(4):
             queue = nc.scalar if r < 2 else nc.sync
@@ -124,9 +124,8 @@ def tile_moe_sdn_lin_silu_kernel(
         nc.sync.dma_start(planes[0][0:112, :].bitcast(I32), gs[4:116, :].bitcast(I32))
         for r in range(4):
             nc.scalar.dma_start(planes[1][r:P:32, :].bitcast(I32), gs[8 + r : 24 : 4, :].bitcast(I32))
-        load_weights((1, 2, 3), (0, 1))
-        load_weights((0, 1), (2, 3))
-        load_weights((2, 3), (2, 3))
+        for e in range(1, E):
+            load_weights((e,), (0, 1, 2, 3))
         nc.sync.dma_start(pos_sb[0][:], pos1)
         nc.sync.dma_start(pos_sb[1][:], pos2)
         gate_sb = keep.tile([P, 2, GATED_TOKENS], F32, name="gate_sb", align_bytes=64)
@@ -139,29 +138,35 @@ def tile_moe_sdn_lin_silu_kernel(
             nc.sync.dma_start(w2s[r:P:32, :].bitcast(I32), w2s_rows[r].bitcast(I32))
 
         for e in range(E):
-            for s in range(PASSES):
+            for s in (0, 2, 1) if e < 2 else (0, 1, 2):
                 if (e, s) == (E - 1, PASSES - 1):
                     gather_words(e, s, 0, P)
                     gather_words(e, s, P, P)
                 else:
                     gather_words(e, s)
 
-        def hidden(e, groups, order=(0, 1, 2)):
-            accs = [next_bank([P, width]) for t, a, width in groups]
-            for s in order:
-                for acc, (t, a, width) in zip(accs, groups):
-                    cols = slice(e * C + a, e * C + a + width)
-                    nc.tensor.matmul_mx(
-                        out=acc[:],
-                        lhsT=w1w[e, t][:, s, :].bitcast(FP4X4),
-                        lhsT_scale=w1s[:, e * PASSES + s, P * t : P * (t + 1)],
-                        rhs=gw[e][s][:, a : a + width].bitcast(FP8X4),
-                        rhs_scale=gs[:, cols] if s == 0 else planes[s - 1][:, cols],
-                        start=(s == order[0]),
-                        stop=(s == order[-1]),
-                    )
-            for acc, (t, a, width) in zip(accs, groups):
-                nc.scalar.activation(h[t][:, e * C + a : e * C + a + width], acc[:], SILU)
+        sums = {}
+
+        def multiply(e, s, groups, first=0, last=PASSES - 1):
+            for t, a, width in groups:
+                if s == first:
+                    sums[e, t, a] = next_bank([P, width])
+                cols = slice(e * C + a, e * C + a + width)
+                nc.tensor.matmul_mx(
+                    out=sums[e, t, a][:],
+                    lhsT=w1w[e, t][:, s, :].bitcast(FP4X4),
+                    lhsT_scale=w1s[:, e * PASSES + s, P * t : P * (t + 1)],
+                    rhs=gw[e][s][:, a : a + width].bitcast(FP8X4),
+                    rhs_scale=gs[:, cols] if s == 0 else planes[s - 1][:, cols],
+                    start=(s == first),
+                    stop=(s == last),
+                )
+                if s == last:
+                    nc.scalar.activation(h[t][:, cols], sums[e, t, a][:], SILU)
+
+        def hidden(e, groups):
+            for s in range(PASSES):
+                multiply(e, s, groups)
 
         c_tok = keep.tile([P, T // P * H], BF16, name="c_tok")
         fetched = {}
@@ -225,15 +230,15 @@ def tile_moe_sdn_lin_silu_kernel(
 
         def gate_plain_parted(bank, j, t):
             first = keep.tile([P, 2, 64], F32, name=f"first{j}_{t}")
-            sums = bank[:].rearrange("k (r p u e) -> k r u p e", r=2, u=2, e=2)
+            parts = bank[:].rearrange("k (r p u e) -> k r u p e", r=2, u=2, e=2)
             nc.scalar.activation(
-                first[:].rearrange("k u (p e) -> k u p e", e=2), sums[:, 0], COPY, scale=gate_cols[:, j : j + 1]
+                first[:].rearrange("k u (p e) -> k u p e", e=2), parts[:, 0], COPY, scale=gate_cols[:, j : j + 1]
             )
             for u in range(2):
                 a = j * H + u * 2 * P + 64 * t
                 nc.vector.scalar_tensor_tensor(
                     c_tok[:, a : a + 64].rearrange("k (p e) -> k p e", e=2),
-                    sums[:, 1, u],
+                    parts[:, 1, u],
                     gate_cols[:, 4 + j : 5 + j],
                     first[:, u, :].rearrange("k (p e) -> k p e", e=2),
                     MULT,
@@ -279,16 +284,16 @@ def tile_moe_sdn_lin_silu_kernel(
             queue.dma_start(out[:, js[0] * P : js[0] * P + ntok], result[:])
 
         low, high, gated = (0, 1), (2, 3), (0, 1, 2)
-        hidden(0, [(t, 0, C) for t in low], (0, 2, 1))
-        hidden(1, [(t, 0, C) for t in low])
-        hidden(0, [(t, 0, C) for t in high])
+        whole = [(t, 0, C) for t in range(H_TILES)]
+        for e, s in ((0, 0), (0, 2), (1, 0), (0, 1), (1, 2), (1, 1)):
+            multiply(e, s, whole, last=1)
         hidden(2, [(t, 0, C) for t in low])
         hidden(3, [(0, 0, P), (0, P, P), (1, 0, C)])
-        for e in range(1, E):
+        for e in range(2, E):
             hidden(e, [(2, 0, C)])
         fetch(0, 0, 2 * P, True)
         fetch(0, 2 * P, 2 * P, False)
-        for e in range(1, E):
+        for e in range(2, E):
             hidden(e, [(3, 0, C)])
         gate_bank = next_bank([P, P])
         nc.tensor.transpose(gate_bank[:], gate_rows[:], ident[:])

@@ -25,7 +25,6 @@ SLOTS = E * C
 H_TILES = H // P
 BANKS = 8
 XS_COLS = 768
-GATED_TOKENS = 3 * P
 
 
 def tile_moe_sdn_lin_silu_kernel(
@@ -49,13 +48,14 @@ def tile_moe_sdn_lin_silu_kernel(
         pos_sb = [lists.tile([P, T // 16], U16, name=f"pos_sb{r}") for r in range(2)]
 
         xs_win = keep.tile([P, XS_COLS], U8, name="xs_win", align_bytes=64)
-        w1s = keep.tile([P, E * PASSES, H], U8, name="w1s", align_bytes=64)
+        w1s = [keep.tile([P, 2 * PASSES, H], U8, name=f"w1s{a}", align_bytes=64) for a in range(2)]
         w2s = keep.tile([P, N], U8, name="w2s", align_bytes=64)
         planes = [keep.tile([P, SLOTS], U8, name=f"plane{s}", align_bytes=64) for s in (1, 2)]
         ident = keep.tile([P, P], F32, name="ident")
         gate_rows = keep.tile([P, P], F32, name="gate_rows")
         nc.gpsimd.memset(xs_win[:].bitcast(I32), 0)
-        nc.vector.memset(w1s[:].rearrange("p a n -> p (a n)").bitcast(I32), 0)
+        for a in range(2):
+            nc.vector.memset(w1s[a][:].rearrange("p a n -> p (a n)").bitcast(I32), 0)
         nc.vector.memset(ident[:], 0.0)
         nc.vector.memset(planes[0][96:P, :].bitcast(I32), 0)
         nc.vector.memset(planes[1][:].bitcast(I32), 0)
@@ -99,10 +99,13 @@ def tile_moe_sdn_lin_silu_kernel(
                     w1w[e, t] = words[:, a * PASSES : (a + 1) * PASSES, b * 2 * P : (b + 1) * 2 * P]
 
         load_weights((0,), (0, 1, 2, 3))
-        w1s_rows = w1_scales.rearrange("e s (q r) n -> r q (e s) n", r=4)
-        for r in range(4):
-            queue = nc.scalar if r < 2 else nc.sync
-            queue.dma_start(w1s[r:P:32, :, :].bitcast(I32), w1s_rows[r].bitcast(I32))
+        w1s_rows = w1_scales.rearrange("(a e) s (q r) n -> a r q (e s) n", a=2, r=4)
+
+        def load_weight_scales(a, queues):
+            for r in range(4):
+                queues[r].dma_start(w1s[a][r:P:32, :, :].bitcast(I32), w1s_rows[a][r].bitcast(I32))
+
+        load_weight_scales(0, (nc.scalar, nc.scalar, nc.sync, nc.sync))
 
         gs = keep.tile([P, SLOTS], U8, name="gs", align_bytes=64)
         gw = [
@@ -124,12 +127,16 @@ def tile_moe_sdn_lin_silu_kernel(
         nc.sync.dma_start(planes[0][0:112, :].bitcast(I32), gs[4:116, :].bitcast(I32))
         for r in range(4):
             nc.scalar.dma_start(planes[1][r:P:32, :].bitcast(I32), gs[8 + r : 24 : 4, :].bitcast(I32))
-        for e in range(1, E):
+        load_weights((1,), (0, 1, 2, 3))
+        load_weight_scales(1, (nc.sync,) * 4)
+        for e in range(2, E):
             load_weights((e,), (0, 1, 2, 3))
         nc.sync.dma_start(pos_sb[0][:], pos1)
         nc.sync.dma_start(pos_sb[1][:], pos2)
-        gate_sb = keep.tile([P, 2, GATED_TOKENS], F32, name="gate_sb", align_bytes=64)
-        nc.sync.dma_start(gate_sb[:], gate[:, :, 0:GATED_TOKENS].rearrange("r p t -> p r t"))
+        gate_sb = {}
+        for tok0, ntok in ((0, 2 * P), (2 * P, P)):
+            gate_sb[tok0] = keep.tile([P, 2, ntok], F32, name=f"gate_sb{tok0}", align_bytes=64)
+            nc.sync.dma_start(gate_sb[tok0][:], gate[:, :, tok0 : tok0 + ntok].rearrange("r p t -> p r t"))
         nc.sync.dma_start(gate_rows[0:8, :], gate[:, 0, :].rearrange("r (j t) -> r j t", t=P))
         w2w = keep.tile([P, 2 * N], U8, name="w2w", align_bytes=64)
         nc.sync.dma_start(w2w[:].bitcast(I32), w2_words[0].bitcast(I32))
@@ -138,7 +145,7 @@ def tile_moe_sdn_lin_silu_kernel(
             nc.sync.dma_start(w2s[r:P:32, :].bitcast(I32), w2s_rows[r].bitcast(I32))
 
         for e in range(E):
-            for s in (0, 2, 1) if e < 2 else (0, 1, 2):
+            for s in (0, 2, 1) if e == 0 else (0, 1, 2):
                 if (e, s) == (E - 1, PASSES - 1):
                     gather_words(e, s, 0, P)
                     gather_words(e, s, P, P)
@@ -155,7 +162,7 @@ def tile_moe_sdn_lin_silu_kernel(
                 nc.tensor.matmul_mx(
                     out=sums[e, t, a][:],
                     lhsT=w1w[e, t][:, s, :].bitcast(FP4X4),
-                    lhsT_scale=w1s[:, e * PASSES + s, P * t : P * (t + 1)],
+                    lhsT_scale=w1s[e // 2][:, (e % 2) * PASSES + s, P * t : P * (t + 1)],
                     rhs=gw[e][s][:, a : a + width].bitcast(FP8X4),
                     rhs_scale=gs[:, cols] if s == 0 else planes[s - 1][:, cols],
                     start=(s == first),
@@ -176,7 +183,7 @@ def tile_moe_sdn_lin_silu_kernel(
                 cols = keep.tile([P, ntok], F32, name=f"cols{tok0}_{t}_{r}")
                 window = h[t][:].indirect(pos_sb[r][:, tok0 // 16 : (tok0 + ntok) // 16])
                 if gated:
-                    nc.vector.tensor_tensor(cols[:], window, gate_sb[:, r, tok0 : tok0 + ntok], MULT)
+                    nc.vector.tensor_tensor(cols[:], window, gate_sb[tok0][:, r, :], MULT)
                 else:
                     nc.scalar.activation(cols[:], window, COPY)
                 for a in range(0, ntok, P):
@@ -285,8 +292,9 @@ def tile_moe_sdn_lin_silu_kernel(
 
         low, high, gated = (0, 1), (2, 3), (0, 1, 2)
         whole = [(t, 0, C) for t in range(H_TILES)]
-        for e, s in ((0, 0), (0, 2), (1, 0), (0, 1), (1, 2), (1, 1)):
-            multiply(e, s, whole, last=1)
+        for s in (0, 2, 1):
+            multiply(0, s, whole, last=1)
+        hidden(1, whole)
         hidden(2, [(t, 0, C) for t in low])
         hidden(3, [(0, 0, P), (0, P, P), (1, 0, C)])
         for e in range(2, E):
@@ -299,38 +307,36 @@ def tile_moe_sdn_lin_silu_kernel(
         nc.tensor.transpose(gate_bank[:], gate_rows[:], ident[:])
         gate_cols = keep.tile([P, 8], F32, name="gate_cols")
         nc.scalar.copy(gate_cols[:], gate_bank[:, 0:8])
-
-        def combine_gated(js, t):
-            bank = next_bank([P, len(js) * P])
-            turn_gated(bank, js, (t,), t)
-            round_gated(bank, js, (t,), True)
-
-        fetch(1, 0, 3 * P, True)
-        fetch(1, 3 * P, P, False)
-        combine_gated(low, 0)
-        plain_2 = next_bank([P, 2 * P])
-        turn_plain(plain_2, 2, (0,), 0)
-        plain_low = next_bank([P, 4 * P])
+        fetch(1, 0, 2 * P, True)
+        fetch(1, 2 * P, 2 * P, False)
+        gated_low = next_bank([P, 4 * P])
+        plain_low = [next_bank([P, 4 * P]) for j in high]
         for t in low:
-            turn_plain(plain_low, 3, low, t)
-        fetch(2, 0, 3 * P, True)
-        gate_plain_parted(plain_2, 2, 0)
-        gate_plain(plain_low, 3, low)
-        fetch(2, 3 * P, P, False)
-        combine_gated(gated, 1)
-        fetch(3, 3 * P, P, False)
-        fetch(3, 0, 2 * P, True)
-        combine_gated(gated, 2)
+            turn_gated(gated_low, low, low, t)
+            for j in high:
+                turn_plain(plain_low[j - 2], j, low, t)
+        round_gated(gated_low, low, low, True)
+        gated_high = next_bank([P, 4 * P])
         plain_high = next_bank([P, 4 * P])
         for t in high:
+            fetch(t, 0, 2 * P, True)
+            turn_gated(gated_high, low, high, t)
+        for j in high:
+            gate_plain(plain_low[j - 2], j, low)
+        for t in high:
+            fetch(t, 3 * P, P, False)
             turn_plain(plain_high, 3, high, t)
-        fetch(3, 2 * P, P, True)
+        round_gated(gated_high, low, high, True)
+        gated_last = next_bank([P, 2 * P])
+        for t in high:
+            fetch(t, 2 * P, P, True)
         gate_plain(plain_high, 3, high)
-        combine_gated(low, 3)
-        combine_gated((2,), 3)
+        for t in high:
+            turn_gated(gated_last, (2,), high, t)
+        round_gated(gated_last, (2,), high, False)
         group_low = turn_back(low, True, nc.vector.tensor_copy)
         group_3 = turn_back((3,), False, nc.scalar.copy)
-        group_2 = turn_back((2,), True, nc.scalar.copy)
+        group_2 = turn_back((2,), False, nc.scalar.copy)
         second_product(low, group_low, nc.scalar.copy, nc.sync)
         second_product((3,), group_3, nc.vector.tensor_copy, nc.sync)
         second_product((2,), group_2, nc.scalar.copy, nc.scalar)

@@ -108,8 +108,14 @@ def tile_moe_sdn_lin_silu_kernel(
         load_weight_scales(0, (nc.scalar, nc.scalar, nc.sync, nc.sync))
 
         gs = keep.tile([P, SLOTS], U8, name="gs", align_bytes=64)
+        gw_pair = keep.tile([P, 2 * C], U32, name="gw_pair", align_bytes=64)
         gw = [
-            [keep.tile([P, C], U32, name=f"gw{e}_{s}", align_bytes=64) for s in range(PASSES)]
+            [
+                gw_pair[:, e * C : (e + 1) * C]
+                if e < 2 and s == 0
+                else keep.tile([P, C], U32, name=f"gw{e}_{s}", align_bytes=64)[:]
+                for s in range(PASSES)
+            ]
             for e in range(E)
         ]
 
@@ -252,6 +258,19 @@ def tile_moe_sdn_lin_silu_kernel(
                     ADD,
                 )
 
+        def keep_clock_up(back):
+            unread = next_bank([P, 2 * C], back)
+            for repeat in range(2):
+                nc.tensor.matmul_mx(
+                    out=unread[:],
+                    lhsT=w1w[0, 0][:, 0, :].bitcast(FP4X4),
+                    lhsT_scale=w1s[0][:, 0, 0:P],
+                    rhs=gw_pair[:].bitcast(FP8X4),
+                    rhs_scale=gs[:, 0 : 2 * C],
+                    start=True,
+                    stop=True,
+                )
+
         def turn_back(js, parted, copy):
             tiles = len(js)
             words = c_tok[:, js[0] * H : (js[-1] + 1) * H].bitcast(F32)
@@ -321,6 +340,8 @@ def tile_moe_sdn_lin_silu_kernel(
         for t in high:
             fetch(t, 0, 2 * P, True)
             turn_gated(gated_high, low, high, t)
+            if t == 2:
+                keep_clock_up(6)
         for j in high:
             gate_plain(plain_low[j - 2], j, low)
         for t in high:

@@ -24,7 +24,9 @@ PASSES = K // 512
 SLOTS = E * C
 H_TILES = H // P
 BANKS = 8
-XS_COLS = 768
+LIST_ROWS = 16
+SCALE_WINDOW = T + T // 2
+LOW, HIGH = (0, 1), (2, 3)
 
 
 def tile_moe_sdn_lin_silu_kernel(
@@ -36,171 +38,164 @@ def tile_moe_sdn_lin_silu_kernel(
         keep = ctx.enter_context(tc.tile_pool(name="keep", bufs=1))
         psum = ctx.enter_context(tc.psum_pool(name="psum", bufs=1))
 
-        used_banks = [f"bank{b}" for b in range(BANKS)]
+        bank_tags = [f"bank{b}" for b in range(BANKS)]
 
-        def next_bank(shape, back=BANKS):
-            tag = used_banks[-back]
-            used_banks.remove(tag)
-            used_banks.append(tag)
-            return psum.tile(shape, F32, name="bank", tag=tag)
+        def next_bank(shape):
+            bank_tags.append(bank_tags.pop(0))
+            return psum.tile(shape, F32, name="bank", tag=bank_tags[-1])
 
-        offs_sb = lists.tile([P, SLOTS // 16], U16, name="offs_sb")
-        pos_sb = [lists.tile([P, T // 16], U16, name=f"pos_sb{r}") for r in range(2)]
+        offs_sb = lists.tile([P, SLOTS // LIST_ROWS], U16, name="offs_sb")
+        pos_sb = [lists.tile([P, T // LIST_ROWS], U16, name=f"pos_sb{r}") for r in range(2)]
 
-        xs_win = keep.tile([P, XS_COLS], U8, name="xs_win", align_bytes=64)
-        w1s = [keep.tile([P, 2 * PASSES, H], U8, name=f"w1s{a}", align_bytes=64) for a in range(2)]
-        w2s = keep.tile([P, N], U8, name="w2s", align_bytes=64)
-        planes = [keep.tile([P, SLOTS], U8, name=f"plane{s}", align_bytes=64) for s in (1, 2)]
+        x_scale_rows = keep.tile([P, SCALE_WINDOW], U8, name="x_scale_rows", align_bytes=64)
+        w1_planes = [keep.tile([P, 2 * PASSES, H], U8, name=f"w1_planes{a}", align_bytes=64) for a in range(2)]
+        w2_plane = keep.tile([P, N], U8, name="w2_plane", align_bytes=64)
+        moved_planes = [keep.tile([P, SLOTS], U8, name=f"moved_plane{s}", align_bytes=64) for s in (1, 2)]
         ident = keep.tile([P, P], F32, name="ident")
         gate_rows = keep.tile([P, P], F32, name="gate_rows")
-        nc.gpsimd.memset(xs_win[:].bitcast(I32), 0)
-        for a in range(2):
-            nc.vector.memset(w1s[a][:].rearrange("p a n -> p (a n)").bitcast(I32), 0)
+        nc.gpsimd.memset(x_scale_rows[:].bitcast(I32), 0)
+        for planes in w1_planes:
+            nc.vector.memset(planes[:].rearrange("p a n -> p (a n)").bitcast(I32), 0)
         nc.vector.memset(ident[:], 0.0)
-        nc.vector.memset(planes[0][96:P, :].bitcast(I32), 0)
-        nc.vector.memset(planes[1][:].bitcast(I32), 0)
-        nc.vector.memset(w2s[:].bitcast(I32), 0)
+        nc.vector.memset(moved_planes[0][96:P, :].bitcast(I32), 0)
+        nc.vector.memset(moved_planes[1][:].bitcast(I32), 0)
+        nc.vector.memset(w2_plane[:].bitcast(I32), 0)
         nc.vector.memset(gate_rows[:], 0.0)
         make_identity(nc, ident[:], nomemset=True)
 
-        xw = keep.tile([P, PASSES, T], I32, name="xw", align_bytes=64)
+        x_sb = keep.tile([P, PASSES, T], I32, name="x_sb", align_bytes=64)
         h = [keep.tile([P, SLOTS], F32, name=f"h{t}") for t in range(H_TILES)]
 
         nc.sync.dma_start(offs_sb[:], offs)
         for q in range(4):
             queue = nc.scalar if q % 2 == 0 else nc.sync
             queue.dma_start(
-                xs_win[32 * q : 32 * q + 8, 0:T].bitcast(I32),
+                x_scale_rows[32 * q : 32 * q + 8, 0:T].bitcast(I32),
                 x_scales[0:2, 4 * q : 4 * q + 4, :].bitcast(I32),
             )
-        nc.sync.dma_start(xs_win[8:24, 0:T].bitcast(I32), x_scales[2].bitcast(I32))
-        nc.sync.dma_start(xw[:], x_words.rearrange("s p t d -> p s (t d)").bitcast(I32))
-        w1w = {}
+        nc.sync.dma_start(x_scale_rows[8:24, 0:T].bitcast(I32), x_scales[2].bitcast(I32))
+        nc.sync.dma_start(x_sb[:], x_words.rearrange("s p t d -> p s (t d)").bitcast(I32))
 
-        w1_rows = w1_words.rearrange("e s p b -> p (e s) b").bitcast(I32)
+        w1_sb = {}
 
-        def load_weights(experts, tiles):
-            words = keep.tile(
-                [P, len(experts) * PASSES, len(tiles) * 2 * P],
-                U8,
-                name=f"w1w{experts[0]}_{tiles[0]}",
-                align_bytes=64,
-            )
-            nc.sync.dma_start(
-                words[:].bitcast(I32),
-                w1_rows[
-                    :,
-                    experts[0] * PASSES : (experts[-1] + 1) * PASSES,
-                    tiles[0] * P // 2 : (tiles[-1] + 1) * P // 2,
-                ],
-            )
-            for a, e in enumerate(experts):
-                for b, t in enumerate(tiles):
-                    w1w[e, t] = words[:, a * PASSES : (a + 1) * PASSES, b * 2 * P : (b + 1) * 2 * P]
+        def load_weights(e):
+            w1_sb[e] = keep.tile([P, PASSES, 2 * H], U8, name=f"w1_sb{e}", align_bytes=64)
+            nc.sync.dma_start(w1_sb[e][:].bitcast(I32), w1_words[e].rearrange("s p b -> p s b").bitcast(I32))
 
-        load_weights((0,), (0, 1, 2, 3))
-        w1s_rows = w1_scales.rearrange("(a e) s (q r) n -> a r q (e s) n", a=2, r=4)
+        w1_scale_rows = w1_scales.rearrange("(a e) s (q r) n -> a r q (e s) n", a=2, r=4)
 
-        def load_weight_scales(a, queues):
+        def load_weight_planes(a, queues):
             for r in range(4):
-                queues[r].dma_start(w1s[a][r:P:32, :, :].bitcast(I32), w1s_rows[a][r].bitcast(I32))
+                queues[r].dma_start(w1_planes[a][r:P:32, :, :].bitcast(I32), w1_scale_rows[a][r].bitcast(I32))
 
-        load_weight_scales(0, (nc.scalar, nc.scalar, nc.sync, nc.sync))
+        load_weights(0)
+        load_weight_planes(0, (nc.scalar, nc.scalar, nc.sync, nc.sync))
 
-        gs = keep.tile([P, SLOTS], U8, name="gs", align_bytes=64)
-        gw_pair = keep.tile([P, 2 * C], U32, name="gw_pair", align_bytes=64)
-        gw = [
-            [
-                gw_pair[:, e * C : (e + 1) * C]
-                if e < 2 and s == 0
-                else keep.tile([P, C], U32, name=f"gw{e}_{s}", align_bytes=64)[:]
-                for s in range(PASSES)
-            ]
+        slot_scales = keep.tile([P, SLOTS], U8, name="slot_scales", align_bytes=64)
+        slot_words = [
+            [keep.tile([P, C], U32, name=f"slot_words{e}_{s}", align_bytes=64) for s in range(PASSES)]
             for e in range(E)
         ]
-
-        def gather_words(e, s, a=0, width=C):
-            first = (e * C + a) // 16
-            nc.vector.tensor_copy(
-                gw[e][s][:, a : a + width],
-                xw[:, s, :].bitcast(U32).indirect(offs_sb[:, first : first + width // 16]),
-            )
-
         for a in range(0, SLOTS, 2 * C):
             nc.vector.tensor_copy(
-                gs[:, a : a + 2 * C], xs_win[:].indirect(offs_sb[:, a // 16 : (a + 2 * C) // 16])
+                slot_scales[:, a : a + 2 * C],
+                x_scale_rows[:].indirect(offs_sb[:, a // LIST_ROWS : (a + 2 * C) // LIST_ROWS]),
             )
-        nc.sync.dma_start(planes[0][0:112, :].bitcast(I32), gs[4:116, :].bitcast(I32))
+        nc.sync.dma_start(moved_planes[0][0:112, :].bitcast(I32), slot_scales[4:116, :].bitcast(I32))
         for r in range(4):
-            nc.scalar.dma_start(planes[1][r:P:32, :].bitcast(I32), gs[8 + r : 24 : 4, :].bitcast(I32))
-        load_weights((1,), (0, 1, 2, 3))
-        load_weight_scales(1, (nc.sync,) * 4)
-        for e in range(2, E):
-            load_weights((e,), (0, 1, 2, 3))
+            nc.scalar.dma_start(
+                moved_planes[1][r:P:32, :].bitcast(I32), slot_scales[8 + r : 24 : 4, :].bitcast(I32)
+            )
+        slot_planes = [slot_scales] + moved_planes
+
+        load_weights(1)
+        load_weight_planes(1, (nc.sync,) * 4)
+        load_weights(2)
+        load_weights(3)
         nc.sync.dma_start(pos_sb[0][:], pos1)
         nc.sync.dma_start(pos_sb[1][:], pos2)
-        gate_sb = {}
-        for tok0, ntok in ((0, 2 * P), (2 * P, P)):
-            gate_sb[tok0] = keep.tile([P, 2, ntok], F32, name=f"gate_sb{tok0}", align_bytes=64)
-            nc.sync.dma_start(gate_sb[tok0][:], gate[:, :, tok0 : tok0 + ntok].rearrange("r p t -> p r t"))
-        nc.sync.dma_start(gate_rows[0:8, :], gate[:, 0, :].rearrange("r (j t) -> r j t", t=P))
-        w2w = keep.tile([P, 2 * N], U8, name="w2w", align_bytes=64)
-        nc.sync.dma_start(w2w[:].bitcast(I32), w2_words[0].bitcast(I32))
-        w2s_rows = w2_scales[0].rearrange("(q r) n -> r q n", r=4)
+        gate_wide = {}
+        for js in (LOW, (2,)):
+            gate_wide[js] = keep.tile([P, 2, len(js) * P], F32, name=f"gate_wide{js[0]}", align_bytes=64)
+            nc.sync.dma_start(
+                gate_wide[js][:], gate[:, :, js[0] * P : (js[-1] + 1) * P].rearrange("r p t -> p r t")
+            )
+        nc.sync.dma_start(gate_rows[0:4, :], gate[:, 0, 2 * P : T].rearrange("r (j t) -> r j t", t=P))
+        w2_sb = keep.tile([P, 2 * N], U8, name="w2_sb", align_bytes=64)
+        nc.sync.dma_start(w2_sb[:].bitcast(I32), w2_words[0].bitcast(I32))
+        w2_scale_rows = w2_scales[0].rearrange("(q r) n -> r q n", r=4)
         for r in range(4):
-            nc.sync.dma_start(w2s[r:P:32, :].bitcast(I32), w2s_rows[r].bitcast(I32))
+            nc.sync.dma_start(w2_plane[r:P:32, :].bitcast(I32), w2_scale_rows[r].bitcast(I32))
+
+        def pass_order(e):
+            return (0, 2, 1) if e == 0 else (0, 1, 2)
+
+        def gather_words(e, s, a, width):
+            first = (e * C + a) // LIST_ROWS
+            nc.vector.tensor_copy(
+                slot_words[e][s][:, a : a + width],
+                x_sb[:, s, :].bitcast(U32).indirect(offs_sb[:, first : first + width // LIST_ROWS]),
+            )
 
         for e in range(E):
-            for s in (0, 2, 1) if e == 0 else (0, 1, 2):
+            for s in pass_order(e):
                 if (e, s) == (E - 1, PASSES - 1):
                     gather_words(e, s, 0, P)
                     gather_words(e, s, P, P)
                 else:
-                    gather_words(e, s)
+                    gather_words(e, s, 0, C)
 
-        sums = {}
+        def hidden(e, sums):
+            order = pass_order(e)
+            banks = {}
+            for s in order:
+                for t, a, width in sums:
+                    if s == order[0]:
+                        banks[t, a] = next_bank([P, width])
+                    slots = slice(e * C + a, e * C + a + width)
+                    nc.tensor.matmul_mx(
+                        out=banks[t, a][:],
+                        lhsT=w1_sb[e][:, s, 2 * P * t : 2 * P * (t + 1)].bitcast(FP4X4),
+                        lhsT_scale=w1_planes[e // 2][:, (e % 2) * PASSES + s, P * t : P * (t + 1)],
+                        rhs=slot_words[e][s][:, a : a + width].bitcast(FP8X4),
+                        rhs_scale=slot_planes[s][:, slots],
+                        start=(s == order[0]),
+                        stop=(s == order[-1]),
+                    )
+                    if s == order[-1]:
+                        nc.scalar.activation(h[t][:, slots], banks[t, a][:], SILU)
 
-        def multiply(e, s, groups, first=0, last=PASSES - 1):
-            for t, a, width in groups:
-                if s == first:
-                    sums[e, t, a] = next_bank([P, width])
-                cols = slice(e * C + a, e * C + a + width)
-                nc.tensor.matmul_mx(
-                    out=sums[e, t, a][:],
-                    lhsT=w1w[e, t][:, s, :].bitcast(FP4X4),
-                    lhsT_scale=w1s[e // 2][:, (e % 2) * PASSES + s, P * t : P * (t + 1)],
-                    rhs=gw[e][s][:, a : a + width].bitcast(FP8X4),
-                    rhs_scale=gs[:, cols] if s == 0 else planes[s - 1][:, cols],
-                    start=(s == first),
-                    stop=(s == last),
-                )
-                if s == last:
-                    nc.scalar.activation(h[t][:, cols], sums[e, t, a][:], SILU)
+        def all_slots(*tiles):
+            return [(t, 0, C) for t in tiles]
 
-        def hidden(e, groups):
-            for s in range(PASSES):
-                multiply(e, s, groups)
-
-        c_tok = keep.tile([P, T // P * H], BF16, name="c_tok")
         fetched = {}
 
-        def fetch(t, tok0, ntok, gated):
+        def fetch(t, js, gated):
             for r in range(2):
-                cols = keep.tile([P, ntok], F32, name=f"cols{tok0}_{t}_{r}")
-                window = h[t][:].indirect(pos_sb[r][:, tok0 // 16 : (tok0 + ntok) // 16])
+                picked = keep.tile([P, len(js) * P], F32, name=f"picked{js[0]}_{t}_{r}")
+                window = h[t][:].indirect(pos_sb[r][:, js[0] * P // LIST_ROWS : (js[-1] + 1) * P // LIST_ROWS])
                 if gated:
-                    nc.vector.tensor_tensor(cols[:], window, gate_sb[tok0][:, r, :], MULT)
+                    nc.vector.tensor_tensor(picked[:], window, gate_wide[js][:, r, :], MULT)
                 else:
-                    nc.scalar.activation(cols[:], window, COPY)
-                for a in range(0, ntok, P):
-                    fetched[(tok0 + a) // P, t, r] = cols[:, a : a + P]
+                    nc.scalar.activation(picked[:], window, COPY)
+                for g, j in enumerate(js):
+                    fetched[j, t, r] = picked[:, g * P : (g + 1) * P]
+
+        c_tok = keep.tile([P, T // P * H], BF16, name="c_tok")
+
+        def c_part(js, ts):
+            rows = c_tok[:, js[0] * H : (js[-1] + 1) * H].rearrange("k (g u i) -> k g u i", u=2, i=H // 2)
+            return rows[:, :, :, P // 2 * ts[0] : P // 2 * (ts[-1] + 1)]
+
+        def turned_place(columns, ts, t):
+            return columns.rearrange("k (u t p e) -> k t p u e", u=2, t=len(ts), e=2)[:, ts.index(t)]
 
         def turn_gated(bank, js, ts, t):
+            width = len(ts) * P
             for g, j in enumerate(js):
-                a = (g * len(ts) + ts.index(t)) * P
                 for r in range(2):
                     nc.tensor.matmul(
-                        bank[:, a : a + P],
+                        turned_place(bank[:, g * width : (g + 1) * width], ts, t),
                         fetched[j, t, r],
                         ident[:],
                         start=(r == 0),
@@ -208,156 +203,109 @@ def tile_moe_sdn_lin_silu_kernel(
                         is_transpose=True,
                     )
 
-        def round_gated(bank, js, ts, parted):
-            rows = c_tok[:, js[0] * H : (js[-1] + 1) * H]
-            if parted:
-                nc.scalar.copy(
-                    rows.rearrange("k (g u p e) -> k g u p e", u=2, p=P, e=2)[
-                        :, :, :, 32 * ts[0] : 32 * (ts[-1] + 1), :
-                    ],
-                    bank[:].rearrange("k (g p u e) -> k g u p e", g=len(js), u=2, e=2),
-                )
-            else:
-                nc.scalar.copy(
-                    rows.rearrange("k (g i) -> k g i", i=H)[:, :, P * ts[0] : P * (ts[-1] + 1)],
-                    bank[:].rearrange("k (g i) -> k g i", g=len(js)),
-                )
+        def round_gated(bank, js, ts):
+            nc.scalar.copy(c_part(js, ts), bank[:].rearrange("k (g u i) -> k g u i", g=len(js), u=2))
 
         def turn_plain(bank, j, ts, t):
+            width = len(ts) * P
             for r in range(2):
-                a = (r * len(ts) + ts.index(t)) * P
-                nc.tensor.transpose(bank[:, a : a + P], fetched[j, t, r], ident[:])
+                place = turned_place(bank[:, r * width : (r + 1) * width], ts, t)
+                nc.tensor.transpose(place, fetched[j, t, r], ident[:])
 
         def gate_plain(bank, j, ts):
             width = len(ts) * P
             first = keep.tile([P, width], F32, name=f"first{j}_{ts[0]}")
-            nc.scalar.activation(first[:], bank[:, 0:width], COPY, scale=gate_cols[:, j : j + 1])
+            nc.scalar.activation(first[:], bank[:, 0:width], COPY, scale=gate_cols[:, j - 2 : j - 1])
             nc.vector.scalar_tensor_tensor(
-                c_tok[:, j * H + ts[0] * P : j * H + ts[0] * P + width],
-                bank[:, width : 2 * width],
-                gate_cols[:, 4 + j : 5 + j],
-                first[:],
+                c_part((j,), ts)[:, 0],
+                bank[:, width : 2 * width].rearrange("k (u i) -> k u i", u=2),
+                gate_cols[:, j : j + 1],
+                first[:].rearrange("k (u i) -> k u i", u=2),
                 MULT,
                 ADD,
             )
 
-        def gate_plain_parted(bank, j, t):
-            first = keep.tile([P, 2, 64], F32, name=f"first{j}_{t}")
-            parts = bank[:].rearrange("k (r p u e) -> k r u p e", r=2, u=2, e=2)
-            nc.scalar.activation(
-                first[:].rearrange("k u (p e) -> k u p e", e=2), parts[:, 0], COPY, scale=gate_cols[:, j : j + 1]
-            )
-            for u in range(2):
-                a = j * H + u * 2 * P + 64 * t
-                nc.vector.scalar_tensor_tensor(
-                    c_tok[:, a : a + 64].rearrange("k (p e) -> k p e", e=2),
-                    parts[:, 1, u],
-                    gate_cols[:, 4 + j : 5 + j],
-                    first[:, u, :].rearrange("k (p e) -> k p e", e=2),
-                    MULT,
-                    ADD,
-                )
-
-        def keep_clock_up(back):
-            unread = next_bank([P, 2 * C], back)
-            for repeat in range(2):
-                nc.tensor.matmul_mx(
-                    out=unread[:],
-                    lhsT=w1w[0, 0][:, 0, :].bitcast(FP4X4),
-                    lhsT_scale=w1s[0][:, 0, 0:P],
-                    rhs=gw_pair[:].bitcast(FP8X4),
-                    rhs_scale=gs[:, 0 : 2 * C],
-                    start=True,
-                    stop=True,
-                )
-
-        def turn_back(js, parted, copy):
-            tiles = len(js)
+        def turn_back(js, copy):
             words = c_tok[:, js[0] * H : (js[-1] + 1) * H].bitcast(F32)
-            turned = next_bank([P, tiles, 2, P])
-            for g in range(tiles):
+            turned = next_bank([P, len(js), 2, P])
+            for g in range(len(js)):
                 for u in range(2):
-                    if parted:
-                        half = words[:, (2 * g + u) * P : (2 * g + u + 1) * P]
-                    else:
-                        half = words[:, 2 * g * P + u : 2 * (g + 1) * P : 2]
-                    nc.tensor.transpose(turned[:, g, u, :], half, ident[:])
-            group = keep.tile([P, tiles, P, 2], F32, name=f"group{js[0]}", align_bytes=64)
-            copy(group[:], turned[:].rearrange("p g u k -> p g k u"))
-            return group
+                    a = (2 * g + u) * P
+                    nc.tensor.transpose(turned[:, g, u, :], words[:, a : a + P], ident[:])
+            c_words = keep.tile([P, len(js), P, 2], F32, name=f"c_words{js[0]}", align_bytes=64)
+            copy(c_words[:], turned[:].rearrange("p g u k -> p g k u"))
+            return c_words
 
-        def second_product(js, group, copy, queue):
+        def second_product(js, c_words, copy, queue):
             ntok = len(js) * P
             codes = keep.tile([P, ntok], U32, name=f"codes{js[0]}", align_bytes=64)
-            scales = keep.tile([P, ntok], U8, name=f"scales{js[0]}", align_bytes=64)
+            plane = keep.tile([P, ntok], U8, name=f"c_plane{js[0]}", align_bytes=64)
             nc.vector.quantize_mx(
                 out=codes[:].bitcast(FP8X4),
-                scales=scales[:],
-                in_=group[:].rearrange("p g k u -> p (g k u)").bitcast(BF16),
+                scales=plane[:],
+                in_=c_words[:].rearrange("p g k u -> p (g k u)").bitcast(BF16),
             )
-            res = next_bank([P, ntok])
+            product = next_bank([P, ntok])
             nc.tensor.matmul_mx(
-                out=res[:],
-                lhsT=w2w[:].bitcast(FP4X4),
-                lhsT_scale=w2s[:],
+                out=product[:],
+                lhsT=w2_sb[:].bitcast(FP4X4),
+                lhsT_scale=w2_plane[:],
                 rhs=codes[:].bitcast(FP8X4),
-                rhs_scale=scales[:],
+                rhs_scale=plane[:],
                 start=True,
                 stop=True,
             )
             result = keep.tile([P, ntok], F32, name=f"result{js[0]}")
-            copy(result[:], res[:])
+            copy(result[:], product[:])
             queue.dma_start(out[:, js[0] * P : js[0] * P + ntok], result[:])
 
-        low, high, gated = (0, 1), (2, 3), (0, 1, 2)
-        whole = [(t, 0, C) for t in range(H_TILES)]
-        for s in (0, 2, 1):
-            multiply(0, s, whole, last=1)
-        hidden(1, whole)
-        hidden(2, [(t, 0, C) for t in low])
-        hidden(3, [(0, 0, P), (0, P, P), (1, 0, C)])
-        for e in range(2, E):
-            hidden(e, [(2, 0, C)])
-        fetch(0, 0, 2 * P, True)
-        fetch(0, 2 * P, 2 * P, False)
-        for e in range(2, E):
-            hidden(e, [(3, 0, C)])
+        hidden(0, all_slots(0, 1, 2, 3))
+        hidden(1, all_slots(0, 1, 2, 3))
+        hidden(2, all_slots(0, 1, 2))
+        hidden(3, [(0, 0, P), (0, P, P)] + all_slots(1))
+        hidden(3, all_slots(2))
+        fetch(0, LOW, True)
+        fetch(0, HIGH, False)
+        hidden(2, all_slots(3))
+        hidden(3, all_slots(3))
+
         gate_bank = next_bank([P, P])
         nc.tensor.transpose(gate_bank[:], gate_rows[:], ident[:])
-        gate_cols = keep.tile([P, 8], F32, name="gate_cols")
-        nc.scalar.copy(gate_cols[:], gate_bank[:, 0:8])
-        fetch(1, 0, 2 * P, True)
-        fetch(1, 2 * P, 2 * P, False)
+        gate_cols = keep.tile([P, 4], F32, name="gate_cols")
+        nc.scalar.copy(gate_cols[:], gate_bank[:, 0:4])
+
+        fetch(1, LOW, True)
+        fetch(1, HIGH, False)
         gated_low = next_bank([P, 4 * P])
-        plain_low = [next_bank([P, 4 * P]) for j in high]
-        for t in low:
-            turn_gated(gated_low, low, low, t)
-            for j in high:
-                turn_plain(plain_low[j - 2], j, low, t)
-        round_gated(gated_low, low, low, True)
+        plain_low = {j: next_bank([P, 4 * P]) for j in HIGH}
+        for t in LOW:
+            turn_gated(gated_low, LOW, LOW, t)
+            for j in HIGH:
+                turn_plain(plain_low[j], j, LOW, t)
+        round_gated(gated_low, LOW, LOW)
+
         gated_high = next_bank([P, 4 * P])
         plain_high = next_bank([P, 4 * P])
-        for t in high:
-            fetch(t, 0, 2 * P, True)
-            turn_gated(gated_high, low, high, t)
-            if t == 2:
-                keep_clock_up(6)
-        for j in high:
-            gate_plain(plain_low[j - 2], j, low)
-        for t in high:
-            fetch(t, 3 * P, P, False)
-            turn_plain(plain_high, 3, high, t)
-        round_gated(gated_high, low, high, True)
+        for t in HIGH:
+            fetch(t, LOW, True)
+            turn_gated(gated_high, LOW, HIGH, t)
+        for j in HIGH:
+            gate_plain(plain_low[j], j, LOW)
+        for t in HIGH:
+            fetch(t, (3,), False)
+            turn_plain(plain_high, 3, HIGH, t)
+        round_gated(gated_high, LOW, HIGH)
         gated_last = next_bank([P, 2 * P])
-        for t in high:
-            fetch(t, 2 * P, P, True)
-        gate_plain(plain_high, 3, high)
-        for t in high:
-            turn_gated(gated_last, (2,), high, t)
-        round_gated(gated_last, (2,), high, False)
-        group_low = turn_back(low, True, nc.vector.tensor_copy)
-        group_3 = turn_back((3,), False, nc.scalar.copy)
-        group_2 = turn_back((2,), False, nc.scalar.copy)
-        second_product(low, group_low, nc.scalar.copy, nc.sync)
-        second_product((3,), group_3, nc.vector.tensor_copy, nc.sync)
-        second_product((2,), group_2, nc.scalar.copy, nc.scalar)
+        for t in HIGH:
+            fetch(t, (2,), True)
+        gate_plain(plain_high, 3, HIGH)
+        for t in HIGH:
+            turn_gated(gated_last, (2,), HIGH, t)
+        round_gated(gated_last, (2,), HIGH)
+
+        words_low = turn_back(LOW, nc.vector.tensor_copy)
+        words_3 = turn_back((3,), nc.scalar.copy)
+        words_2 = turn_back((2,), nc.scalar.copy)
+        second_product(LOW, words_low, nc.scalar.copy, nc.sync)
+        second_product((3,), words_3, nc.vector.tensor_copy, nc.sync)
+        second_product((2,), words_2, nc.scalar.copy, nc.scalar)

@@ -25,7 +25,8 @@ SLOTS = E * C
 H_TILES = H // P
 BANKS = 8
 LIST_ROWS = 16
-SCALE_WINDOW = T + T // 2
+SCALE_WINDOW = SLOTS + SLOTS // 2
+WORD_WINDOW = T + T // 2
 LOW, HIGH = (0, 1), (2, 3)
 
 
@@ -48,39 +49,43 @@ def tile_moe_sdn_lin_silu_kernel(
         pos_sb = [lists.tile([P, T // LIST_ROWS], U16, name=f"pos_sb{r}") for r in range(2)]
 
         x_scale_rows = keep.tile([P, SCALE_WINDOW], U8, name="x_scale_rows", align_bytes=64)
+        rows = x_scales.rearrange("s b t -> (s b) t").bitcast(I32)
+        nc.sync.dma_start(offs_sb[:], offs)
+        for q in range(3):
+            queue = nc.scalar if q % 2 == 0 else nc.sync
+            queue.dma_start(x_scale_rows[32 * q : 32 * q + 32, 0:T].bitcast(I32), rows[4 * q : 4 * q + 32, :])
+        nc.sync.dma_start(
+            x_scale_rows[96:P, 0:T].bitcast(I32), rows[8:48, :].rearrange("(a j) t -> a j t", a=2)[:, 4:20, :]
+        )
+
         w1_planes = [keep.tile([P, 2 * PASSES, H], U8, name=f"w1_planes{a}", align_bytes=64) for a in range(2)]
         w2_plane = keep.tile([P, N], U8, name="w2_plane", align_bytes=64)
-        moved_planes = [keep.tile([P, SLOTS], U8, name=f"moved_plane{s}", align_bytes=64) for s in (1, 2)]
+        moved_planes = {s: keep.tile([P, SLOTS], U8, name=f"moved_plane{s}", align_bytes=64) for s in (1, 2)}
         ident = keep.tile([P, P], F32, name="ident")
-        gate_rows = keep.tile([P, P], F32, name="gate_rows")
-        nc.gpsimd.memset(x_scale_rows[:].bitcast(I32), 0)
+        x_sb = keep.tile([P, PASSES * T + T // 2], I32, name="x_sb", align_bytes=64)
+        nc.gpsimd.memset(x_scale_rows[:, T:SCALE_WINDOW].bitcast(I32), 0)
+        nc.gpsimd.memset(x_sb[:, PASSES * T :], 0)
         for planes in w1_planes:
             nc.vector.memset(planes[:].rearrange("p a n -> p (a n)").bitcast(I32), 0)
-        nc.vector.memset(ident[:], 0.0)
-        nc.vector.memset(moved_planes[0][96:P, :].bitcast(I32), 0)
-        nc.vector.memset(moved_planes[1][:].bitcast(I32), 0)
+        nc.vector.memset(moved_planes[2][64:P, :].bitcast(I32), 0)
         nc.vector.memset(w2_plane[:].bitcast(I32), 0)
-        nc.vector.memset(gate_rows[:], 0.0)
-        make_identity(nc, ident[:], nomemset=True)
+        make_identity(nc, ident[:])
 
-        x_sb = keep.tile([P, PASSES, T], I32, name="x_sb", align_bytes=64)
         h = [keep.tile([P, SLOTS], F32, name=f"h{t}") for t in range(H_TILES)]
-
-        nc.sync.dma_start(offs_sb[:], offs)
-        for q in range(4):
-            queue = nc.scalar if q % 2 == 0 else nc.sync
-            queue.dma_start(
-                x_scale_rows[32 * q : 32 * q + 8, 0:T].bitcast(I32),
-                x_scales[0:2, 4 * q : 4 * q + 4, :].bitcast(I32),
-            )
-        nc.sync.dma_start(x_scale_rows[8:24, 0:T].bitcast(I32), x_scales[2].bitcast(I32))
-        nc.sync.dma_start(x_sb[:], x_words.rearrange("s p t d -> p s (t d)").bitcast(I32))
+        nc.scalar.dma_start(
+            x_sb[:, 0 : PASSES * T].rearrange("p (s t) -> p s t", s=PASSES),
+            x_words.rearrange("s p t d -> p s (t d)").bitcast(I32),
+        )
 
         w1_sb = {}
 
-        def load_weights(e):
-            w1_sb[e] = keep.tile([P, PASSES, 2 * H], U8, name=f"w1_sb{e}", align_bytes=64)
-            nc.sync.dma_start(w1_sb[e][:].bitcast(I32), w1_words[e].rearrange("s p b -> p s b").bitcast(I32))
+        def load_weights(queue, experts, passes):
+            pieces = [(e, s) for e in experts for s in passes]
+            tile = keep.tile([P, len(pieces), 2 * H], U8, name=f"w1_sb{experts[0]}_{passes[0]}", align_bytes=64)
+            source = w1_words[experts[0] : experts[-1] + 1, passes[0] : passes[-1] + 1]
+            queue.dma_start(tile[:].bitcast(I32), source.rearrange("e s p b -> p (e s) b").bitcast(I32))
+            for a, piece in enumerate(pieces):
+                w1_sb[piece] = tile[:, a, :]
 
         w1_scale_rows = w1_scales.rearrange("(a e) s (q r) n -> a r q (e s) n", a=2, r=4)
 
@@ -88,30 +93,25 @@ def tile_moe_sdn_lin_silu_kernel(
             for r in range(4):
                 queues[r].dma_start(w1_planes[a][r:P:32, :, :].bitcast(I32), w1_scale_rows[a][r].bitcast(I32))
 
-        load_weights(0)
-        load_weight_planes(0, (nc.scalar, nc.scalar, nc.sync, nc.sync))
+        load_weights(nc.sync, (0, 1), (0,))
+        load_weight_planes(0, (nc.sync, nc.sync, nc.sync, nc.scalar))
+        load_weights(nc.scalar, (0,), (1, 2))
 
         slot_scales = keep.tile([P, SLOTS], U8, name="slot_scales", align_bytes=64)
-        slot_words = [
-            [keep.tile([P, C], U32, name=f"slot_words{e}_{s}", align_bytes=64) for s in range(PASSES)]
-            for e in range(E)
-        ]
-        for a in range(0, SLOTS, 2 * C):
-            nc.vector.tensor_copy(
-                slot_scales[:, a : a + 2 * C],
-                x_scale_rows[:].indirect(offs_sb[:, a // LIST_ROWS : (a + 2 * C) // LIST_ROWS]),
+        slot_words = [keep.tile([P, SLOTS], U32, name=f"slot_words{s}", align_bytes=64) for s in range(PASSES)]
+        nc.vector.tensor_copy(slot_scales[:], x_scale_rows[:].indirect(offs_sb[:]))
+        moves = [(1, 0, 16, 64), (2, 0, 60, 64), (1, 64, 24, 64), (2, 64, 120, 4), (2, 96, 124, 4)]
+        for m, (s, to, start, count) in enumerate(moves):
+            queue = nc.scalar if m % 2 == 0 else nc.sync
+            queue.dma_start(
+                moved_planes[s][to : to + count, :].bitcast(I32), slot_scales[start : start + count, :].bitcast(I32)
             )
-        nc.sync.dma_start(moved_planes[0][0:112, :].bitcast(I32), slot_scales[4:116, :].bitcast(I32))
-        for r in range(4):
-            nc.scalar.dma_start(
-                moved_planes[1][r:P:32, :].bitcast(I32), slot_scales[8 + r : 24 : 4, :].bitcast(I32)
-            )
-        slot_planes = [slot_scales] + moved_planes
+        slot_planes = [slot_scales, moved_planes[1], moved_planes[2]]
 
-        load_weights(1)
+        load_weights(nc.sync, (1,), (1, 2))
         load_weight_planes(1, (nc.sync,) * 4)
-        load_weights(2)
-        load_weights(3)
+        load_weights(nc.sync, (2,), (0, 1, 2))
+        load_weights(nc.sync, (3,), (0, 1, 2))
         nc.sync.dma_start(pos_sb[0][:], pos1)
         nc.sync.dma_start(pos_sb[1][:], pos2)
         gate_wide = {}
@@ -120,50 +120,56 @@ def tile_moe_sdn_lin_silu_kernel(
             nc.sync.dma_start(
                 gate_wide[js][:], gate[:, :, js[0] * P : (js[-1] + 1) * P].rearrange("r p t -> p r t")
             )
-        nc.sync.dma_start(gate_rows[0:4, :], gate[:, 0, 2 * P : T].rearrange("r (j t) -> r j t", t=P))
         w2_sb = keep.tile([P, 2 * N], U8, name="w2_sb", align_bytes=64)
         nc.sync.dma_start(w2_sb[:].bitcast(I32), w2_words[0].bitcast(I32))
         w2_scale_rows = w2_scales[0].rearrange("(q r) n -> r q n", r=4)
         for r in range(4):
             nc.sync.dma_start(w2_plane[r:P:32, :].bitcast(I32), w2_scale_rows[r].bitcast(I32))
+        gate_cols = [keep.tile([P, 2], F32, name=f"gate_cols{r}") for r in range(2)]
+        with nc.allow_non_contiguous_dma(reason="one value of gate a partition"):
+            for r in range(2):
+                nc.sync.dma_start(gate_cols[r][:], gate[r, 0, 2 * P : T].rearrange("(j p) -> p j", p=P))
 
-        def pass_order(e):
-            return (0, 2, 1) if e == 0 else (0, 1, 2)
-
-        def gather_words(e, s, a, width):
-            first = (e * C + a) // LIST_ROWS
+        def gather_words(s, first, last):
             nc.vector.tensor_copy(
-                slot_words[e][s][:, a : a + width],
-                x_sb[:, s, :].bitcast(U32).indirect(offs_sb[:, first : first + width // LIST_ROWS]),
+                slot_words[s][:, first:last],
+                x_sb[:, s * T : s * T + WORD_WINDOW].bitcast(U32).indirect(offs_sb[:, first // LIST_ROWS : last // LIST_ROWS]),
             )
 
-        for e in range(E):
-            for s in pass_order(e):
-                if (e, s) == (E - 1, PASSES - 1):
-                    gather_words(e, s, 0, P)
-                    gather_words(e, s, P, P)
-                else:
-                    gather_words(e, s, 0, C)
+        gather_words(0, 0, 2 * C)
+        gather_words(1, 0, C)
+        gather_words(2, 0, C)
+        gather_words(1, C, 3 * C)
+        gather_words(2, C, 2 * C)
+        gather_words(0, 2 * C, 3 * C)
+        gather_words(2, 2 * C, 3 * C)
+        gather_words(0, 3 * C, 4 * C)
+        gather_words(1, 3 * C, 4 * C)
+        gather_words(2, 3 * C, 3 * C + P)
+        gather_words(2, 3 * C + P, 4 * C)
+
+        banks = {}
+
+        def one_pass(e, s, sums):
+            for t, a, width in sums:
+                if s == 0:
+                    banks[e, t, a] = next_bank([P, width])
+                slots = slice(e * C + a, e * C + a + width)
+                nc.tensor.matmul_mx(
+                    out=banks[e, t, a][:],
+                    lhsT=w1_sb[e, s][:, 2 * P * t : 2 * P * (t + 1)].bitcast(FP4X4),
+                    lhsT_scale=w1_planes[e // 2][:, (e % 2) * PASSES + s, P * t : P * (t + 1)],
+                    rhs=slot_words[s][:, slots].bitcast(FP8X4),
+                    rhs_scale=slot_planes[s][:, slots],
+                    start=(s == 0),
+                    stop=(s == PASSES - 1),
+                )
+                if s == PASSES - 1:
+                    nc.scalar.activation(h[t][:, slots], banks[e, t, a][:], SILU)
 
         def hidden(e, sums):
-            order = pass_order(e)
-            banks = {}
-            for s in order:
-                for t, a, width in sums:
-                    if s == order[0]:
-                        banks[t, a] = next_bank([P, width])
-                    slots = slice(e * C + a, e * C + a + width)
-                    nc.tensor.matmul_mx(
-                        out=banks[t, a][:],
-                        lhsT=w1_sb[e][:, s, 2 * P * t : 2 * P * (t + 1)].bitcast(FP4X4),
-                        lhsT_scale=w1_planes[e // 2][:, (e % 2) * PASSES + s, P * t : P * (t + 1)],
-                        rhs=slot_words[e][s][:, a : a + width].bitcast(FP8X4),
-                        rhs_scale=slot_planes[s][:, slots],
-                        start=(s == order[0]),
-                        stop=(s == order[-1]),
-                    )
-                    if s == order[-1]:
-                        nc.scalar.activation(h[t][:, slots], banks[t, a][:], SILU)
+            for s in range(PASSES):
+                one_pass(e, s, sums)
 
         def all_slots(*tiles):
             return [(t, 0, C) for t in tiles]
@@ -215,11 +221,11 @@ def tile_moe_sdn_lin_silu_kernel(
         def gate_plain(bank, j, ts):
             width = len(ts) * P
             first = keep.tile([P, width], F32, name=f"first{j}_{ts[0]}")
-            nc.scalar.activation(first[:], bank[:, 0:width], COPY, scale=gate_cols[:, j - 2 : j - 1])
+            nc.scalar.activation(first[:], bank[:, 0:width], COPY, scale=gate_cols[0][:, j - 2 : j - 1])
             nc.vector.scalar_tensor_tensor(
                 c_part((j,), ts)[:, 0],
                 bank[:, width : 2 * width].rearrange("k (u i) -> k u i", u=2),
-                gate_cols[:, j : j + 1],
+                gate_cols[1][:, j - 2 : j - 1],
                 first[:].rearrange("k (u i) -> k u i", u=2),
                 MULT,
                 ADD,
@@ -259,8 +265,12 @@ def tile_moe_sdn_lin_silu_kernel(
             copy(result[:], product[:])
             queue.dma_start(out[:, js[0] * P : js[0] * P + ntok], result[:])
 
-        hidden(0, all_slots(0, 1, 2, 3))
-        hidden(1, all_slots(0, 1, 2, 3))
+        for e in (0, 1):
+            one_pass(e, 0, all_slots(0, 1, 2, 3))
+        for e in (0, 1):
+            for t in range(H_TILES):
+                one_pass(e, 1, all_slots(t))
+                one_pass(e, 2, all_slots(t))
         hidden(2, all_slots(0, 1, 2))
         hidden(3, [(0, 0, P), (0, P, P)] + all_slots(1))
         hidden(3, all_slots(2))
@@ -268,11 +278,6 @@ def tile_moe_sdn_lin_silu_kernel(
         fetch(0, HIGH, False)
         hidden(2, all_slots(3))
         hidden(3, all_slots(3))
-
-        gate_bank = next_bank([P, P])
-        nc.tensor.transpose(gate_bank[:], gate_rows[:], ident[:])
-        gate_cols = keep.tile([P, 4], F32, name="gate_cols")
-        nc.scalar.copy(gate_cols[:], gate_bank[:, 0:4])
 
         fetch(1, LOW, True)
         fetch(1, HIGH, False)

@@ -79,13 +79,14 @@ def tile_moe_sdn_lin_silu_kernel(
 
         w1_sb = {}
 
-        def load_weights(queue, experts, passes):
-            pieces = [(e, s) for e in experts for s in passes]
-            tile = keep.tile([P, len(pieces), 2 * H], U8, name=f"w1_sb{experts[0]}_{passes[0]}", align_bytes=64)
-            source = w1_words[experts[0] : experts[-1] + 1, passes[0] : passes[-1] + 1]
-            queue.dma_start(tile[:].bitcast(I32), source.rearrange("e s p b -> p (e s) b").bitcast(I32))
+        def load_weights(queue, source, pieces):
+            tile = keep.tile([P, len(pieces), 2 * H], U8, name=f"w1_sb{pieces[0][0]}_{pieces[0][1]}", align_bytes=64)
+            queue.dma_start(tile[:].bitcast(I32), source.rearrange("a p b -> p a b").bitcast(I32))
             for a, piece in enumerate(pieces):
                 w1_sb[piece] = tile[:, a, :]
+
+        w1_rows = w1_words.rearrange("e s p b -> (e s) p b")
+        pieces = [(e, s) for e in range(E) for s in range(PASSES)]
 
         w1_scale_rows = w1_scales.rearrange("(a e) s (q r) n -> a r q (e s) n", a=2, r=4)
 
@@ -93,9 +94,8 @@ def tile_moe_sdn_lin_silu_kernel(
             for r in range(4):
                 queues[r].dma_start(w1_planes[a][r:P:32, :, :].bitcast(I32), w1_scale_rows[a][r].bitcast(I32))
 
-        load_weights(nc.sync, (0, 1), (0,))
-        load_weight_planes(0, (nc.sync, nc.sync, nc.sync, nc.scalar))
-        load_weights(nc.scalar, (0,), (1, 2))
+        load_weights(nc.scalar, w1_rows[0:4], pieces[0:4])
+        load_weight_planes(0, (nc.sync,) * 4)
 
         slot_scales = keep.tile([P, SLOTS], U8, name="slot_scales", align_bytes=64)
         slot_words = [keep.tile([P, SLOTS], U32, name=f"slot_words{s}", align_bytes=64) for s in range(PASSES)]
@@ -108,10 +108,10 @@ def tile_moe_sdn_lin_silu_kernel(
             )
         slot_planes = [slot_scales, moved_planes[1], moved_planes[2]]
 
-        load_weights(nc.sync, (1,), (1, 2))
+        load_weights(nc.sync, w1_rows[4:6], pieces[4:6])
         load_weight_planes(1, (nc.sync,) * 4)
-        load_weights(nc.sync, (2,), (0, 1, 2))
-        load_weights(nc.sync, (3,), (0, 1, 2))
+        load_weights(nc.sync, w1_rows[6:9], pieces[6:9])
+        load_weights(nc.sync, w1_rows[9:12], pieces[9:12])
         nc.sync.dma_start(pos_sb[0][:], pos1)
         nc.sync.dma_start(pos_sb[1][:], pos2)
         gate_wide = {}

@@ -94,8 +94,9 @@ def tile_moe_sdn_lin_silu_kernel(
             for r in range(4):
                 queues[r].dma_start(w1_planes[a][r:P:32, :, :].bitcast(I32), w1_scale_rows[a][r].bitcast(I32))
 
-        load_weights(nc.scalar, w1_rows[0:4], pieces[0:4])
-        load_weight_planes(0, (nc.sync,) * 4)
+        load_weights(nc.sync, w1_rows[0:1], pieces[0:1])
+        load_weight_planes(0, (nc.sync, nc.sync, nc.sync, nc.scalar))
+        load_weights(nc.sync, w1_rows[1:6], pieces[1:6])
 
         slot_scales = keep.tile([P, SLOTS], U8, name="slot_scales", align_bytes=64)
         slot_words = [keep.tile([P, SLOTS], U32, name=f"slot_words{s}", align_bytes=64) for s in range(PASSES)]
@@ -108,9 +109,8 @@ def tile_moe_sdn_lin_silu_kernel(
             )
         slot_planes = [slot_scales, moved_planes[1], moved_planes[2]]
 
-        load_weights(nc.sync, w1_rows[4:6], pieces[4:6])
-        load_weight_planes(1, (nc.sync,) * 4)
         load_weights(nc.sync, w1_rows[6:9], pieces[6:9])
+        load_weight_planes(1, (nc.sync,) * 4)
         load_weights(nc.sync, w1_rows[9:12], pieces[9:12])
         nc.sync.dma_start(pos_sb[0][:], pos1)
         nc.sync.dma_start(pos_sb[1][:], pos2)

@@ -41,9 +41,11 @@ def tile_moe_sdn_lin_silu_kernel(
 
         bank_tags = [f"bank{b}" for b in range(BANKS)]
 
-        def next_bank(shape):
-            bank_tags.append(bank_tags.pop(0))
-            return psum.tile(shape, F32, name="bank", tag=bank_tags[-1])
+        def next_bank(shape, tag=None):
+            tag = tag or bank_tags[0]
+            bank_tags.remove(tag)
+            bank_tags.append(tag)
+            return psum.tile(shape, F32, name="bank", tag=tag)
 
         offs_sb = lists.tile([P, SLOTS // LIST_ROWS], U16, name="offs_sb")
         pos_sb = [lists.tile([P, T // LIST_ROWS], U16, name=f"pos_sb{r}") for r in range(2)]
@@ -231,9 +233,9 @@ def tile_moe_sdn_lin_silu_kernel(
                 ADD,
             )
 
-        def turn_back(js, copy):
+        def turn_back(js, copy, tag=None):
             words = c_tok[:, js[0] * H : (js[-1] + 1) * H].bitcast(F32)
-            turned = next_bank([P, len(js), 2, P])
+            turned = next_bank([P, len(js), 2, P], tag)
             for g in range(len(js)):
                 for u in range(2):
                     a = (2 * g + u) * P
@@ -291,6 +293,7 @@ def tile_moe_sdn_lin_silu_kernel(
 
         gated_high = next_bank([P, 4 * P])
         plain_high = next_bank([P, 4 * P])
+        plain_high_tag = bank_tags[-1]
         for t in HIGH:
             fetch(t, LOW, True)
             turn_gated(gated_high, LOW, HIGH, t)
@@ -308,9 +311,10 @@ def tile_moe_sdn_lin_silu_kernel(
             turn_gated(gated_last, (2,), HIGH, t)
         round_gated(gated_last, (2,), HIGH)
 
-        words_low = turn_back(LOW, nc.vector.tensor_copy)
-        words_3 = turn_back((3,), nc.scalar.copy)
-        words_2 = turn_back((2,), nc.scalar.copy)
-        second_product(LOW, words_low, nc.scalar.copy, nc.sync)
-        second_product((3,), words_3, nc.vector.tensor_copy, nc.sync)
-        second_product((2,), words_2, nc.scalar.copy, nc.scalar)
+        words = {j: turn_back((j,), nc.vector.tensor_copy) for j in LOW}
+        words[3] = turn_back((3,), nc.scalar.copy)
+        words[2] = turn_back((2,), nc.scalar.copy, plain_high_tag)
+        second_product((0,), words[0], nc.scalar.copy, nc.sync)
+        second_product((1,), words[1], nc.scalar.copy, nc.sync)
+        second_product((3,), words[3], nc.scalar.copy, nc.scalar)
+        second_product((2,), words[2], nc.vector.tensor_copy, nc.sync)

@@ -303,18 +303,18 @@ def tile_moe_sdn_lin_silu_kernel(
             fetch(t, (3,), False)
             turn_plain(plain_high, 3, HIGH, t)
         round_gated(gated_high, LOW, HIGH)
-        gated_last = next_bank([P, 2 * P])
+        gated_last = {t: next_bank([P, P]) for t in HIGH}
         for t in HIGH:
             fetch(t, (2,), True)
         gate_plain(plain_high, 3, HIGH)
         for t in HIGH:
-            turn_gated(gated_last, (2,), HIGH, t)
-        round_gated(gated_last, (2,), HIGH)
+            turn_gated(gated_last[t], (2,), (t,), t)
+            round_gated(gated_last[t], (2,), (t,))
 
-        words = {j: turn_back((j,), nc.vector.tensor_copy) for j in LOW}
+        words = {0: turn_back((0,), nc.vector.tensor_copy), 1: turn_back((1,), nc.scalar.copy)}
         words[3] = turn_back((3,), nc.scalar.copy)
-        words[2] = turn_back((2,), nc.scalar.copy, plain_high_tag)
+        words[2] = turn_back((2,), nc.vector.tensor_copy, plain_high_tag)
         second_product((0,), words[0], nc.scalar.copy, nc.sync)
         second_product((1,), words[1], nc.scalar.copy, nc.sync)
-        second_product((3,), words[3], nc.scalar.copy, nc.scalar)
-        second_product((2,), words[2], nc.vector.tensor_copy, nc.sync)
+        second_product((3,), words[3], nc.vector.tensor_copy, nc.sync)
+        second_product((2,), words[2], nc.scalar.copy, nc.scalar)

from contextlib import ExitStack

import concourse.mybir as mybir
from concourse.masks import make_identity

K, T, E, C, H, N = 1536, 512, 4, 256, 512, 128
FLOPS = 2 * K * H * E * C + 2 * H * N * T

F32 = mybir.dt.float32
BF16 = mybir.dt.bfloat16
I32 = mybir.dt.int32
U32 = mybir.dt.uint32
U16 = mybir.dt.uint16
U8 = mybir.dt.uint8
FP8X4 = mybir.dt.float8_e4m3fn_x4
FP4X4 = mybir.dt.float4_e2m1fn_x4
MULT = mybir.AluOpType.mult
ADD = mybir.AluOpType.add
COPY = mybir.ActivationFunctionType.Copy
SILU = mybir.ActivationFunctionType.Silu

P = 128
PASSES = K // 512
SLOTS = E * C
H_TILES = H // P
BANKS = 8
LIST_ROWS = 16
SCALE_WINDOW = SLOTS + SLOTS // 2
WORD_WINDOW = T + T // 2
LOW, HIGH = (0, 1), (2, 3)


def tile_moe_sdn_lin_silu_kernel(
    tc, x_words, x_scales, w1_words, w1_scales, w2_words, w2_scales, gate, offs, pos1, pos2, out
):
    nc = tc.nc
    with ExitStack() as ctx:
        lists = ctx.enter_context(tc.tile_pool(name="lists", bufs=1))
        keep = ctx.enter_context(tc.tile_pool(name="keep", bufs=1))
        psum = ctx.enter_context(tc.psum_pool(name="psum", bufs=1))

        bank_tags = [f"bank{b}" for b in range(BANKS)]

        def next_bank(shape, tag=None):
            tag = tag or bank_tags[0]
            bank_tags.remove(tag)
            bank_tags.append(tag)
            return psum.tile(shape, F32, name="bank", tag=tag)

        offs_sb = lists.tile([P, SLOTS // LIST_ROWS], U16, name="offs_sb")
        pos_sb = [lists.tile([P, T // LIST_ROWS], U16, name=f"pos_sb{r}") for r in range(2)]

        x_scale_rows = keep.tile([P, SCALE_WINDOW], U8, name="x_scale_rows", align_bytes=64)
        rows = x_scales.rearrange("s b t -> (s b) t").bitcast(I32)
        nc.sync.dma_start(offs_sb[:], offs)
        for q in range(3):
            queue = nc.scalar if q % 2 == 0 else nc.sync
            queue.dma_start(x_scale_rows[32 * q : 32 * q + 32, 0:T].bitcast(I32), rows[4 * q : 4 * q + 32, :])
        nc.sync.dma_start(
            x_scale_rows[96:P, 0:T].bitcast(I32), rows[8:48, :].rearrange("(a j) t -> a j t", a=2)[:, 4:20, :]
        )

        w1_planes = [keep.tile([P, 2 * PASSES, H], U8, name=f"w1_planes{a}", align_bytes=64) for a in range(2)]
        w2_plane = keep.tile([P, N], U8, name="w2_plane", align_bytes=64)
        moved_planes = {s: keep.tile([P, SLOTS], U8, name=f"moved_plane{s}", align_bytes=64) for s in (1, 2)}
        ident = keep.tile([P, P], F32, name="ident")
        x_sb = keep.tile([P, PASSES * T + T // 2], I32, name="x_sb", align_bytes=64)
        nc.gpsimd.memset(x_scale_rows[:, T:SCALE_WINDOW].bitcast(I32), 0)
        nc.gpsimd.memset(x_sb[:, PASSES * T :], 0)
        for planes in w1_planes:
            nc.vector.memset(planes[:].rearrange("p a n -> p (a n)").bitcast(I32), 0)
        nc.vector.memset(moved_planes[2][64:P, :].bitcast(I32), 0)
        nc.vector.memset(w2_plane[:].bitcast(I32), 0)
        make_identity(nc, ident[:])

        h = [keep.tile([P, SLOTS], F32, name=f"h{t}") for t in range(H_TILES)]
        nc.scalar.dma_start(
            x_sb[:, 0 : PASSES * T].rearrange("p (s t) -> p s t", s=PASSES),
            x_words.rearrange("s p t d -> p s (t d)").bitcast(I32),
        )

        w1_sb = {}

        def load_weights(queue, source, pieces):
            tile = keep.tile([P, len(pieces), 2 * H], U8, name=f"w1_sb{pieces[0][0]}_{pieces[0][1]}", align_bytes=64)
            queue.dma_start(tile[:].bitcast(I32), source.rearrange("a p b -> p a b").bitcast(I32))
            for a, piece in enumerate(pieces):
                w1_sb[piece] = tile[:, a, :]

        w1_rows = w1_words.rearrange("e s p b -> (e s) p b")
        pieces = [(e, s) for e in range(E) for s in range(PASSES)]

        w1_scale_rows = w1_scales.rearrange("(a e) s (q r) n -> a r q (e s) n", a=2, r=4)

        def load_weight_planes(a, queues):
            for r in range(4):
                queues[r].dma_start(w1_planes[a][r:P:32, :, :].bitcast(I32), w1_scale_rows[a][r].bitcast(I32))

        load_weights(nc.sync, w1_rows[0:1], pieces[0:1])
        load_weight_planes(0, (nc.sync, nc.sync, nc.sync, nc.scalar))
        load_weights(nc.sync, w1_rows[1:6], pieces[1:6])

        slot_scales = keep.tile([P, SLOTS], U8, name="slot_scales", align_bytes=64)
        slot_words = [keep.tile([P, SLOTS], U32, name=f"slot_words{s}", align_bytes=64) for s in range(PASSES)]
        nc.vector.tensor_copy(slot_scales[:], x_scale_rows[:].indirect(offs_sb[:]))
        moves = [(1, 0, 16, 64), (2, 0, 60, 64), (1, 64, 24, 64), (2, 64, 120, 4), (2, 96, 124, 4)]
        for m, (s, to, start, count) in enumerate(moves):
            queue = nc.scalar if m % 2 == 0 else nc.sync
            queue.dma_start(
                moved_planes[s][to : to + count, :].bitcast(I32), slot_scales[start : start + count, :].bitcast(I32)
            )
        slot_planes = [slot_scales, moved_planes[1], moved_planes[2]]

        load_weights(nc.sync, w1_rows[6:9], pieces[6:9])
        load_weight_planes(1, (nc.sync,) * 4)
        load_weights(nc.sync, w1_rows[9:12], pieces[9:12])
        nc.sync.dma_start(pos_sb[0][:], pos1)
        nc.sync.dma_start(pos_sb[1][:], pos2)
        gate_wide = {}
        for js in (LOW, (2,)):
            gate_wide[js] = keep.tile([P, 2, len(js) * P], F32, name=f"gate_wide{js[0]}", align_bytes=64)
            nc.sync.dma_start(
                gate_wide[js][:], gate[:, :, js[0] * P : (js[-1] + 1) * P].rearrange("r p t -> p r t")
            )
        w2_sb = keep.tile([P, 2 * N], U8, name="w2_sb", align_bytes=64)
        nc.sync.dma_start(w2_sb[:].bitcast(I32), w2_words[0].bitcast(I32))
        w2_scale_rows = w2_scales[0].rearrange("(q r) n -> r q n", r=4)
        for r in range(4):
            nc.sync.dma_start(w2_plane[r:P:32, :].bitcast(I32), w2_scale_rows[r].bitcast(I32))
        gate_cols = [keep.tile([P, 2], F32, name=f"gate_cols{r}") for r in range(2)]
        with nc.allow_non_contiguous_dma(reason="one value of gate a partition"):
            for r in range(2):
                nc.sync.dma_start(gate_cols[r][:], gate[r, 0, 2 * P : T].rearrange("(j p) -> p j", p=P))

        def gather_words(s, first, last):
            nc.vector.tensor_copy(
                slot_words[s][:, first:last],
                x_sb[:, s * T : s * T + WORD_WINDOW].bitcast(U32).indirect(offs_sb[:, first // LIST_ROWS : last // LIST_ROWS]),
            )

        gather_words(0, 0, 2 * C)
        gather_words(1, 0, C)
        gather_words(2, 0, C)
        gather_words(1, C, 3 * C)
        gather_words(2, C, 2 * C)
        gather_words(0, 2 * C, 3 * C)
        gather_words(2, 2 * C, 3 * C)
        gather_words(0, 3 * C, 4 * C)
        gather_words(1, 3 * C, 4 * C)
        gather_words(2, 3 * C, 3 * C + P)
        gather_words(2, 3 * C + P, 4 * C)

        banks = {}

        def one_pass(e, s, sums):
            for t, a, width in sums:
                if s == 0:
                    banks[e, t, a] = next_bank([P, width])
                slots = slice(e * C + a, e * C + a + width)
                nc.tensor.matmul_mx(
                    out=banks[e, t, a][:],
                    lhsT=w1_sb[e, s][:, 2 * P * t : 2 * P * (t + 1)].bitcast(FP4X4),
                    lhsT_scale=w1_planes[e // 2][:, (e % 2) * PASSES + s, P * t : P * (t + 1)],
                    rhs=slot_words[s][:, slots].bitcast(FP8X4),
                    rhs_scale=slot_planes[s][:, slots],
                    start=(s == 0),
                    stop=(s == PASSES - 1),
                )
                if s == PASSES - 1:
                    nc.scalar.activation(h[t][:, slots], banks[e, t, a][:], SILU)

        def hidden(e, sums):
            for s in range(PASSES):
                one_pass(e, s, sums)

        def all_slots(*tiles):
            return [(t, 0, C) for t in tiles]

        fetched = {}

        def fetch(t, js, gated):
            for r in range(2):
                picked = keep.tile([P, len(js) * P], F32, name=f"picked{js[0]}_{t}_{r}")
                window = h[t][:].indirect(pos_sb[r][:, js[0] * P // LIST_ROWS : (js[-1] + 1) * P // LIST_ROWS])
                if gated:
                    nc.vector.tensor_tensor(picked[:], window, gate_wide[js][:, r, :], MULT)
                else:
                    nc.scalar.activation(picked[:], window, COPY)
                for g, j in enumerate(js):
                    fetched[j, t, r] = picked[:, g * P : (g + 1) * P]

        c_tok = keep.tile([P, T // P * H], BF16, name="c_tok")

        def c_part(js, ts):
            rows = c_tok[:, js[0] * H : (js[-1] + 1) * H].rearrange("k (g u i) -> k g u i", u=2, i=H // 2)
            return rows[:, :, :, P // 2 * ts[0] : P // 2 * (ts[-1] + 1)]

        def turned_place(columns, ts, t):
            return columns.rearrange("k (u t p e) -> k t p u e", u=2, t=len(ts), e=2)[:, ts.index(t)]

        def turn_gated(bank, js, ts, t):
            width = len(ts) * P
            for g, j in enumerate(js):
                for r in range(2):
                    nc.tensor.matmul(
                        turned_place(bank[:, g * width : (g + 1) * width], ts, t),
                        fetched[j, t, r],
                        ident[:],
                        start=(r == 0),
                        stop=(r == 1),
                        is_transpose=True,
                    )

        def round_gated(bank, js, ts):
            nc.scalar.copy(c_part(js, ts), bank[:].rearrange("k (g u i) -> k g u i", g=len(js), u=2))

        def turn_plain(bank, j, ts, t):
            width = len(ts) * P
            for r in range(2):
                place = turned_place(bank[:, r * width : (r + 1) * width], ts, t)
                nc.tensor.transpose(place, fetched[j, t, r], ident[:])

        def gate_plain(bank, j, ts):
            width = len(ts) * P
            first = keep.tile([P, width], F32, name=f"first{j}_{ts[0]}")
            nc.scalar.activation(first[:], bank[:, 0:width], COPY, scale=gate_cols[0][:, j - 2 : j - 1])
            nc.vector.scalar_tensor_tensor(
                c_part((j,), ts)[:, 0],
                bank[:, width : 2 * width].rearrange("k (u i) -> k u i", u=2),
                gate_cols[1][:, j - 2 : j - 1],
                first[:].rearrange("k (u i) -> k u i", u=2),
                MULT,
                ADD,
            )

        def turn_back(js, copy, tag=None):
            words = c_tok[:, js[0] * H : (js[-1] + 1) * H].bitcast(F32)
            turned = next_bank([P, len(js), 2, P], tag)
            for g in range(len(js)):
                for u in range(2):
                    a = (2 * g + u) * P
                    nc.tensor.transpose(turned[:, g, u, :], words[:, a : a + P], ident[:])
            c_words = keep.tile([P, len(js), P, 2], F32, name=f"c_words{js[0]}", align_bytes=64)
            copy(c_words[:], turned[:].rearrange("p g u k -> p g k u"))
            return c_words

        def second_product(js, c_words, copy, queue):
            ntok = len(js) * P
            codes = keep.tile([P, ntok], U32, name=f"codes{js[0]}", align_bytes=64)
            plane = keep.tile([P, ntok], U8, name=f"c_plane{js[0]}", align_bytes=64)
            nc.vector.quantize_mx(
                out=codes[:].bitcast(FP8X4),
                scales=plane[:],
                in_=c_words[:].rearrange("p g k u -> p (g k u)").bitcast(BF16),
            )
            product = next_bank([P, ntok])
            nc.tensor.matmul_mx(
                out=product[:],
                lhsT=w2_sb[:].bitcast(FP4X4),
                lhsT_scale=w2_plane[:],
                rhs=codes[:].bitcast(FP8X4),
                rhs_scale=plane[:],
                start=True,
                stop=True,
            )
            result = keep.tile([P, ntok], F32, name=f"result{js[0]}")
            copy(result[:], product[:])
            queue.dma_start(out[:, js[0] * P : js[0] * P + ntok], result[:])

        for e in (0, 1):
            one_pass(e, 0, all_slots(0, 1, 2, 3))
        for e in (0, 1):
            for t in range(H_TILES):
                one_pass(e, 1, all_slots(t))
                one_pass(e, 2, all_slots(t))
        hidden(2, all_slots(0, 1, 2))
        hidden(3, [(0, 0, P), (0, P, P)] + all_slots(1))
        hidden(3, all_slots(2))
        fetch(0, LOW, True)
        fetch(0, HIGH, False)
        hidden(2, all_slots(3))
        hidden(3, all_slots(3))

        fetch(1, LOW, True)
        fetch(1, HIGH, False)
        gated_low = next_bank([P, 4 * P])
        plain_low = {j: next_bank([P, 4 * P]) for j in HIGH}
        for t in LOW:
            turn_gated(gated_low, LOW, LOW, t)
            for j in HIGH:
                turn_plain(plain_low[j], j, LOW, t)
        round_gated(gated_low, LOW, LOW)

        gated_high = next_bank([P, 4 * P])
        plain_high = next_bank([P, 4 * P])
        plain_high_tag = bank_tags[-1]
        for t in HIGH:
            fetch(t, LOW, True)
            turn_gated(gated_high, LOW, HIGH, t)
        for j in HIGH:
            gate_plain(plain_low[j], j, LOW)
        for t in HIGH:
            fetch(t, (3,), False)
            turn_plain(plain_high, 3, HIGH, t)
        round_gated(gated_high, LOW, HIGH)
        gated_last = {t: next_bank([P, P]) for t in HIGH}
        for t in HIGH:
            fetch(t, (2,), True)
        gate_plain(plain_high, 3, HIGH)
        for t in HIGH:
            turn_gated(gated_last[t], (2,), (t,), t)
            round_gated(gated_last[t], (2,), (t,))

        words = {0: turn_back((0,), nc.vector.tensor_copy), 1: turn_back((1,), nc.scalar.copy)}
        words[3] = turn_back((3,), nc.scalar.copy)
        words[2] = turn_back((2,), nc.vector.tensor_copy, plain_high_tag)
        second_product((0,), words[0], nc.scalar.copy, nc.sync)
        second_product((1,), words[1], nc.scalar.copy, nc.sync)
        second_product((3,), words[3], nc.vector.tensor_copy, nc.sync)
        second_product((2,), words[2], nc.scalar.copy, nc.scalar)
